import numpy as np
import ml_dtypes


def mxq(x, axis, fmt="e4m3"):
    dtype, down = {"e4m3": (ml_dtypes.float8_e4m3fn, 7), "e5m2": (ml_dtypes.float8_e5m2, 14)}[fmt]
    v = np.moveaxis(np.asarray(x, np.float32).astype(ml_dtypes.bfloat16).astype(np.float64), axis, -1)
    blocks = v.reshape(v.shape[:-1] + (-1, 32))
    amax = np.abs(blocks).max(-1, keepdims=True)
    byte = np.maximum(np.where(amax > 0, np.frexp(amax)[1] - 1 + 127, 0) - down, 1)
    scale = np.exp2(byte - 127.0)
    codes = (blocks / scale).astype(np.float32).astype(dtype).astype(np.float64)
    return np.moveaxis((codes * scale).reshape(v.shape), -1, axis)


WIDE = False


def mx_kscale(k):
    if not WIDE:
        return np.ones(k)
    levels = np.array([10, -10, 5, -5, 0])
    if k % 512:
        return np.exp2(np.random.permutation(np.resize(levels, k // 32))).repeat(32)
    a = np.empty((k // 512, 16))
    for p in range(k // 512):
        a[p, :8] = np.random.permutation(np.resize(levels, 8))
        for g in range(8):
            far = levels[np.abs(levels - a[p, g]) >= 10]
            a[p, g + 8] = far[np.random.randint(len(far))]
    return np.exp2(a.ravel()).repeat(32)


BF16 = ml_dtypes.bfloat16


def bf(x):
    return np.asarray(x, np.float32).astype(BF16)


def f64(x):
    return np.asarray(x).astype(np.float64)

def planes(Y):
    n, m = Y.shape
    b = f64(bf(Y)).reshape(n // 32, 32, m)
    amax = np.abs(b).max(1)
    byte = np.clip(np.where(amax > 0, np.frexp(amax)[1] - 1 + 127 - 7, 1), 1, 254)
    codes = (b * np.exp2(127.0 - byte)[:, None, :]).reshape(n, m).astype(np.float32).astype(ml_dtypes.float8_e4m3fn).view(np.uint8)
    words = codes.reshape(n // 512, 128, 4, m).transpose(0, 1, 3, 2)
    return np.ascontiguousarray(words), np.ascontiguousarray(byte.astype(np.uint8).reshape(n // 512, 16, m))


N, D, C = 1024, 1024, 1024


def sigmoid(v):
    return 1.0 / (1.0 + np.exp(-v))


def pull_back(r, gamma, wt, beta):
    return (mxq(r * beta[None, :], 1, "e4m3") @ wt) * gamma[None, :]


def setup_inputs():
    s, t = mx_kscale(D), mx_kscale(C)
    x = np.random.standard_normal((N, D))
    gamma = 1.0 + 0.1 * np.random.standard_normal(D)
    w = np.random.standard_normal((D, C)) / np.sqrt(D)
    beta = 1.0 + 0.1 * np.random.standard_normal(C)
    y = np.random.uniform(0.0, 1.0, (N, C))
    z = np.random.standard_normal(N)
    a = np.random.standard_normal(C)
    return {"x": bf(x), "gamma": bf(gamma * s), "w": bf(w / s[:, None] * t[None, :]), "beta": bf(beta / t),
            "y": bf(y), "z": bf(z), "a": bf(a)}


def core(x, gamma, w, beta, y, z, a):
    x, gamma, w, beta, y, z, a = f64(x), f64(gamma), f64(w), f64(beta), f64(y), f64(z), f64(a)

    s = (mxq(x * gamma[None, :], 1, "e4m3") @ mxq(w, 0, "e4m3")) * beta[None, :]

    r1 = sigmoid(s) - y

    q = np.tanh(s)
    r2 = (a[None, :] * q - z[:, None]) * a[None, :] * (1.0 - q * q)

    wt = mxq(w.T, 0, "e4m3")
    g = pull_back(r1, gamma, wt, beta)
    h = pull_back(r2, gamma, wt, beta)

    k = np.sum(g * h, axis=1) / (np.sum(h * h, axis=1) + 1e-6)

    return g - k[:, None] * h - 0.5 * h


def reference(x, gamma, w, beta, y, z, a):
    R_out = core(x, gamma, w, beta, y, z, a)
    words, scales = planes(R_out)
    return R_out, words, scales

@@ -1,0 +1,437 @@
+from contextlib import ExitStack
+
+import concourse.mybir as mybir
+from concourse.masks import make_identity
+
+F32 = mybir.dt.float32
+BF16 = mybir.dt.bfloat16
+U32 = mybir.dt.uint32
+I32 = mybir.dt.int32
+U8 = mybir.dt.uint8
+FP8X4 = mybir.dt.float8_e4m3fn_x4
+ALU = mybir.AluOpType
+ACT = mybir.ActivationFunctionType
+
+P = 128
+W = 1024
+H = 512
+FLOPS = 3 * 2 * W * W * W
+
+
+def tile_adversarialdebiasingprojectedrepresentat_x1_kernel(tc, x, gamma, w, beta, y, z, a, out_0, out_1, out_2):
+    nc = tc.nc
+    with ExitStack() as ctx:
+        sb = ctx.enter_context(tc.tile_pool(name="sb", bufs=1))
+        ps = ctx.enter_context(tc.psum_pool(name="ps", bufs=1))
+        ctx.enter_context(tc.manual_schedule())
+
+        def bank(i, dtype=F32):
+            return ps.tile([P, H if dtype is F32 else W], dtype, name="bank%d" % i, tag="bank%d" % i)
+
+        def stage():
+            return sb.tile([P, 4 * H], BF16, name="stage", tag="stage", bufs=6, align_bytes=64)
+
+        def slot():
+            return sb.tile([P, 4, H], F32, name="slot", tag="slot", bufs=6)
+
+        def operand(name):
+            codes = sb.tile([P, 2, W], U32, name=name + "_codes", align_bytes=64)
+            scales = sb.tile([P, 2, W], U8, name=name + "_scales", align_bytes=64)
+            return codes, scales
+
+        def quantize(op, g, c0, src):
+            n = src.shape[1] // 4
+            nc.vector.quantize_mx(out=op[0][:, g, c0:c0 + n].bitcast(FP8X4), scales=op[1][:, g, c0:c0 + n], in_=src)
+
+        def mx(out, lhs, l0, rhs, r0):
+            for g in range(2):
+                nc.tensor.matmul_mx(
+                    out=out,
+                    lhsT=lhs[0][:, g, l0:l0 + P].bitcast(FP8X4), lhsT_scale=lhs[1][:, g, l0:l0 + P],
+                    rhs=rhs[0][:, g, r0:r0 + H].bitcast(FP8X4), rhs_scale=rhs[1][:, g, r0:r0 + H],
+                    start=(g == 0), stop=(g == 1))
+
+        vec = {}
+        for name, src in (("gamma", gamma), ("z", z), ("beta", beta), ("a", a)):
+            vec[name] = sb.tile([P, 2, 4], BF16, name="vec_" + name)
+            nc.scalar.dma_start(out=vec[name][:], in_=src.rearrange("(g p t) -> p g t", g=2, t=4))
+        x_raw = sb.tile([P, 8, W], BF16, name="x_raw", tag="big0")
+        w_raw = sb.tile([P, 4, 4, H], BF16, name="w_raw", tag="big1")
+        y_raw = sb.tile([P, 8, W], BF16, name="y_raw")
+        beta_b = sb.tile([P, W], BF16, name="beta_b")
+        gamma_b = sb.tile([P, W], BF16, name="gamma_b")
+
+        def rows(src, h):
+            return src[h * H:(h + 1) * H, :].rearrange("(p t) d -> p t d", t=4)
+
+        def load_x(h, tp):
+            nc.sync.dma_start(out=x_raw[:, 4 * h + 2 * tp:4 * h + 2 * tp + 2, :], in_=rows(x, h)[:, 2 * tp:2 * tp + 2, :])
+
+        def load_w(g, gd):
+            nc.sync.dma_start(out=w_raw[:, 2 * g + gd, :, :], in_=rows(w, gd)[:, :, g * H:(g + 1) * H])
+
+        def load_y(h):
+            nc.sync.dma_start(out=y_raw[:, 4 * h:4 * h + 4, :], in_=rows(y, h))
+
+        load_x(0, 0)
+        load_w(0, 0)
+        load_x(0, 1)
+        load_w(0, 1)
+        load_w(1, 0)
+        load_w(1, 1)
+        load_y(0)
+        nc.sync.dma_start(out=beta_b[:], in_=beta.partition_broadcast(P))
+        load_x(1, 0)
+        load_x(1, 1)
+        load_y(1)
+        nc.sync.dma_start(out=gamma_b[:], in_=gamma.partition_broadcast(P))
+
+        ident_f = sb.tile([P, P], F32, name="ident_f")
+        ident_b = sb.tile([P, P], BF16, name="ident_b")
+        neg_ident = sb.tile([P, P], BF16, name="neg_ident")
+        ab_cols = sb.tile([P, 8, P], BF16, name="ab_cols")
+        make_identity(nc, ident_f[:])
+        make_identity(nc, ident_b[:])
+        nc.gpsimd.memset(ab_cols[:], 0.0)
+        nc.gpsimd.tensor_scalar(out=neg_ident[:], in0=ident_b[:], scalar1=-1.0, scalar2=0.0, op0=ALU.mult, op1=ALU.add)
+        warm = sb.tile([P, 1], F32, name="warm")
+        nc.scalar.activation(out=warm[:], in_=ident_f[:, 0:1], func=ACT.Sigmoid)
+
+        def col8(name):
+            return vec[name][:].rearrange("p g t -> p (g t)")
+
+        gamma_f = sb.tile([P, 8], F32, name="gamma_f")
+        beta_f = sb.tile([P, 8], F32, name="beta_f")
+        ab = sb.tile([P, 8], F32, name="ab")
+        neg_a = sb.tile([P, 8], F32, name="neg_a")
+        neg_aab = sb.tile([P, 8], F32, name="neg_aab")
+        nc.gpsimd.tensor_tensor(out=ab[:], in0=col8("a"), in1=col8("beta"), op=ALU.mult)
+        nc.gpsimd.tensor_copy(out=ab_cols[:, :, 0], in_=ab[:])
+        nc.gpsimd.tensor_tensor(out=ab_cols[:, :, 1], in0=ab[:], in1=ab_cols[:, :, 0], op=ALU.subtract)
+        nc.gpsimd.tensor_copy(out=beta_f[:], in_=col8("beta"))
+        nc.gpsimd.tensor_scalar(out=neg_a[:], in0=col8("a"), scalar1=-1.0, scalar2=0.0, op0=ALU.mult, op1=ALU.add)
+        nc.gpsimd.tensor_tensor(out=neg_aab[:], in0=neg_a[:], in1=ab[:], op=ALU.mult)
+        nc.gpsimd.tensor_copy(out=gamma_f[:], in_=col8("gamma"))
+
+        z_rows = sb.tile([P, W], BF16, name="z_rows")
+        ab_rows = sb.tile([P, W], BF16, name="ab_rows")
+
+        def spread_z():
+            b = bank(4, BF16)
+            for i in range(8):
+                nc.tensor.transpose(b[:, i * P:(i + 1) * P], col8("z")[:, i:i + 1].to_broadcast([P, P]), ident_b[:])
+            nc.scalar.copy(out=z_rows[:], in_=b[:])
+
+        def turn_ab():
+            b = bank(5, BF16)
+            for i in range(8):
+                nc.tensor.transpose(b[:, i * P:(i + 1) * P], ab_cols[:, i, :], ident_b[:])
+            nc.scalar.copy(out=ab_rows[:], in_=b[:])
+
+        xq, wq, wtq, r1q, r2q, oq = [operand(n) for n in ("xq", "wq", "wtq", "r1q", "r2q", "oq")]
+        st = {}
+
+        def turn_words(bk, srcs):
+            b = bank(bk)
+            for u in range(2):
+                for i in range(2):
+                    nc.tensor.transpose(b[:, (2 * u + i) * P:(2 * u + i + 1) * P], srcs(u, i), ident_f[:])
+            return b
+
+        def copy_words(dst, half, b):
+            nc.scalar.copy(out=dst[:].bitcast(F32)[:, half * H:(half + 1) * H].rearrange("p (n u) -> p n u", u=2),
+                           in_=b[:].rearrange("p (u n) -> p n u", u=2))
+
+        def x_turn(h, gd, tp, bk):
+            st["xb", h, gd, tp] = turn_words(
+                bk, lambda u, i: x_raw[:, 4 * h + 2 * tp + i, :].bitcast(F32)[:, 256 * gd + u:256 * gd + 256:2])
+
+        def x_scale(h, gd, tp):
+            if tp == 0:
+                st["xs", h, gd] = stage()
+            nc.vector.tensor_tensor(
+                out=st["xs", h, gd][:, tp * W:(tp + 1) * W].rearrange("p (n u e) -> p n u e", u=2, e=2),
+                in0=st["xb", h, gd, tp][:].bitcast(BF16).rearrange("p (u n e) -> p n u e", u=2, e=2),
+                in1=vec["gamma"][:, gd, :].rearrange("p (u e) -> p u e", u=2).unsqueeze(1).to_broadcast([P, 256, 2, 2]),
+                op=ALU.mult)
+
+        def x_quant(h, gd):
+            quantize(xq, gd, h * H, st["xs", h, gd][:])
+
+        def w_weave(g, gd, t0, t1, on_vector):
+            if t0 == 0:
+                st["ws", g, gd] = stage()
+            dst = st["ws", g, gd][:].rearrange("p (t m j) -> p t m j", t=4, j=4)[:, t0:t1]
+            src = w_raw[:, 2 * g + gd, :, :].rearrange("p j (m t) -> p t m j", t=4)[:, t0:t1]
+            if on_vector:
+                nc.vector.tensor_copy(out=dst, in_=src)
+            else:
+                nc.scalar.copy(out=dst, in_=src)
+
+        def w_quant(g, gd):
+            quantize(wq, gd, g * H, st["ws", g, gd][:])
+
+        def wt_turn(g, gd, jp, bk):
+            if jp == 0:
+                st["wts", g, gd] = stage()
+            b = turn_words(bk, lambda u, i: w_raw[:, 2 * g + gd, 2 * jp + i, :].bitcast(F32)[:, u:256:2])
+            copy_words(st["wts", g, gd], jp, b)
+
+        def wt_quant(g, gd):
+            quantize(wtq, g, gd * H, st["wts", g, gd][:])
+
+        def unit(s):
+            return s // 8, (s // 4) % 2, s % 4
+
+        def s_mm(s):
+            h, g, t = unit(s)
+            st["s", s] = bank(s % 2)
+            mx(st["s", s][:], wq, g * H + t * P, xq, h * H)
+
+        def acts(s):
+            h, g, t = unit(s)
+            b = s // 4
+            if t == 0:
+                st["q", b], st["sig", b], st["q2", b] = slot(), slot(), slot()
+            scale = beta_f[:, 4 * g + t:4 * g + t + 1]
+            nc.scalar.activation(out=st["q", b][:, t, :], in_=st["s", s][:], func=ACT.Tanh, scale=scale)
+            nc.scalar.activation(out=st["sig", b][:, t, :], in_=st["s", s][:], func=ACT.Sigmoid, scale=scale)
+            nc.scalar.activation(out=st["q2", b][:, t, :], in_=st["q", b][:, t, :], func=ACT.Square)
+
+        def p_mm(s):
+            h, g, t = unit(s)
+            st["p", s] = bank(2 + s % 2)
+            i = 4 * g + t
+            nc.tensor.matmul(st["p", s][:], lhsT=ab_rows[:, i * P:(i + 1) * P], rhs=z_rows[:, h * H:(h + 1) * H], start=True, stop=True)
+
+        def u_step(s):
+            h, g, t = unit(s)
+            q = st["q", s // 4][:, t, :]
+            nc.vector.scalar_tensor_tensor(out=q, in0=q, scalar=neg_aab[:, 4 * g + t:4 * g + t + 1], in1=st["p", s][:],
+                                           op0=ALU.mult, op1=ALU.add)
+
+        def r2_weave(b, half):
+            if half == 0:
+                st["r2s", b] = stage()
+            n = slice(half * 256, (half + 1) * 256)
+            nc.vector.scalar_tensor_tensor(
+                out=st["r2s", b][:, half * W:(half + 1) * W].rearrange("p (n t) -> p n t", t=4),
+                in0=st["q2", b][:, :, n].rearrange("p t n -> p n t"), scalar=1.0,
+                in1=st["q", b][:, :, n].rearrange("p t n -> p n t"), op0=ALU.subtract, op1=ALU.mult)
+
+        def r2_quant(b):
+            quantize(r2q, b % 2, (b // 2) * H, st["r2s", b][:])
+
+        def n_mm(s):
+            h, g, tn = unit(s)
+            b = bank(4 + s % 2)
+            st["n", s] = b
+            nc.tensor.matmul(b[:].rearrange("p (t m) -> p t m", t=4), lhsT=neg_ident[:],
+                             rhs=y_raw[:, 4 * h + tn, g * H:(g + 1) * H].rearrange("p (m t) -> p t m", t=4), start=True, stop=False)
+            for t in range(4):
+                nc.tensor.matmul(b[:, t * P:(t + 1) * P], lhsT=st["sig", s // 4][:, t, tn * P:(tn + 1) * P], rhs=ident_f[:],
+                                 start=False, stop=(t == 3), is_transpose=True)
+
+        def n_scale(s):
+            h, g, tn = unit(s)
+            st["r1n", s] = sb.tile([P, H], BF16, name="r1n", tag="r1n", bufs=4)
+            nc.vector.tensor_tensor(
+                out=st["r1n", s][:].rearrange("p (u m e) -> p u m e", u=2, e=2),
+                in0=st["n", s][:].rearrange("p (u e m) -> p u m e", u=2, e=2),
+                in1=beta_b[:, g * H:(g + 1) * H].rearrange("p (m u e) -> p u m e", u=2, e=2), op=ALU.mult)
+
+        def r1_turn(b, tp, bk):
+            if tp == 0:
+                st["r1s", b] = stage()
+            t = turn_words(bk, lambda u, i: st["r1n", 4 * b + 2 * tp + i][:].bitcast(F32)[:, u * P:(u + 1) * P])
+            copy_words(st["r1s", b], tp, t)
+
+        def r1_quant(b):
+            quantize(r1q, b % 2, (b // 2) * H, st["r1s", b][:])
+
+        def gt_unit(h, jd):
+            gd, j = divmod(jd, 4)
+            if j == 0:
+                st["gt", h, gd] = slot()
+            b = bank(jd % 2)
+            mx(b[:], wtq, jd * P, r1q, h * H)
+            nc.scalar.activation(out=st["gt", h, gd][:, j, :], in_=b[:], func=ACT.Copy, scale=gamma_f[:, jd:jd + 1])
+
+        def g_turn(i):
+            h, tn = divmod(i, 4)
+            for gd in range(2):
+                b = bank(2 + 2 * (i % 2) + gd)
+                st["g", i, gd] = b
+                for j in range(4):
+                    nc.tensor.transpose(b[:, j * P:(j + 1) * P], st["gt", h, gd][:, j, tn * P:(tn + 1) * P], ident_f[:])
+
+        def h_mm(i):
+            for gd in range(2):
+                st["hp", i, gd] = bank(6 + gd)
+                mx(st["hp", i, gd][:], r2q, i * P, wtq, gd * H)
+
+        def natural(b):
+            return b[:].rearrange("p (j m) -> p m j", j=4)
+
+        def by4(ap):
+            return ap.rearrange("p (m j) -> p m j", j=4)
+
+        def h_scale(i):
+            st["h", i] = sb.tile([P, W], F32, name="h", tag="h", bufs=2)
+            for gd in range(2):
+                c = slice(gd * H, (gd + 1) * H)
+                nc.vector.tensor_tensor(out=by4(st["h", i][:, c]), in0=natural(st["hp", i, gd]), in1=by4(gamma_b[:, c]), op=ALU.mult)
+
+        junk_s = sb.tile([P, W], BF16, name="junk_s")
+        junk_v = sb.tile([P, 2, H], BF16, name="junk_v")
+
+        def small(name):
+            return sb.tile([P, 1], F32, name=name, tag=name, bufs=2)
+
+        def hh_sum(i):
+            hh = small("hh")
+            nc.scalar.activation(out=junk_s[:], in_=st["h", i][:], func=ACT.Square, accum_out=hh[:])
+            st["den", i] = small("den")
+            nc.gpsimd.tensor_scalar(out=st["den", i][:], in0=hh[:], scalar1=1e-6, scalar2=1.0, op0=ALU.add, op1=ALU.mult)
+
+        def gh_sum(i):
+            part = [small("gh0"), small("gh1")]
+            rec = small("rec")
+            for gd in range(2):
+                nc.vector.scalar_tensor_tensor(
+                    out=by4(junk_v[:, gd, :]), in0=natural(st["g", i, gd]), scalar=-1.0, in1=by4(st["h", i][:, gd * H:(gd + 1) * H]),
+                    op0=ALU.mult, op1=ALU.mult, accum_out=part[gd][:])
+                if gd == 0:
+                    nc.vector.reciprocal(out=rec[:], in_=st["den", i][:])
+            neg_k = small("neg_k")
+            nc.gpsimd.tensor_scalar(out=neg_k[:], in0=part[0][:], scalar1=part[1][:], scalar2=rec[:], op0=ALU.add, op1=ALU.mult)
+            st["coef", i] = small("coef")
+            nc.gpsimd.tensor_scalar(out=st["coef", i][:], in0=neg_k[:], scalar1=1.0, scalar2=-0.5, op0=ALU.mult, op1=ALU.add)
+
+        def combine(i):
+            h, tn = divmod(i, 4)
+            if tn == 0:
+                st["o", h] = sb.tile([P, 4, W], F32, name="o", tag="big%d" % h)
+            for gd in range(2):
+                c = slice(gd * H, (gd + 1) * H)
+                nc.vector.scalar_tensor_tensor(
+                    out=by4(st["o", h][:, tn, c]), in0=by4(st["h", i][:, c]), scalar=st["coef", i][:], in1=natural(st["g", i, gd]),
+                    op0=ALU.mult, op1=ALU.add)
+            nc.sync.dma_start(out=rows(out_0, h)[:, tn, :], in_=st["o", h][:, tn, :])
+
+        def o_weave(h, c, on_vector):
+            if c % 2 == 0:
+                st["os", h, c // 2] = stage()
+            dst = st["os", h, c // 2][:, (c % 2) * W:(c % 2 + 1) * W].rearrange("p (d t) -> p d t", t=4)
+            src = st["o", h][:, :, c * 256:(c + 1) * 256].rearrange("p t d -> p d t")
+            if on_vector:
+                nc.vector.tensor_copy(out=dst, in_=src)
+            else:
+                nc.scalar.copy(out=dst, in_=src)
+
+        def o_quant(h, gd):
+            quantize(oq, h, gd * H, st["os", h, gd][:])
+            c = slice(gd * H, (gd + 1) * H)
+            nc.sync.dma_start(out=out_1[h].rearrange("p m t -> p (m t)").bitcast(I32)[:, c], in_=oq[0][:, h, c].bitcast(I32))
+
+        def o_scales(h):
+            for quad in range(4):
+                eng = nc.sync if quad % 2 == 0 else nc.scalar
+                eng.dma_start(out=out_2[h, 4 * quad:4 * quad + 4, :].bitcast(I32), in_=oq[1][32 * quad:32 * quad + 4, h, :].bitcast(I32))
+
+        x_turn(0, 0, 0, 6)
+        x_turn(0, 1, 0, 7)
+        spread_z()
+        x_scale(0, 0, 0)
+        x_scale(0, 1, 0)
+        w_weave(0, 0, 0, 2, False)
+        w_weave(0, 0, 2, 4, True)
+        x_turn(0, 0, 1, 2)
+        x_turn(0, 1, 1, 3)
+        turn_ab()
+        x_scale(0, 0, 1)
+        w_quant(0, 0)
+        x_scale(0, 1, 1)
+        x_quant(0, 0)
+        w_weave(0, 1, 0, 2, False)
+        w_weave(0, 1, 2, 4, True)
+        x_quant(0, 1)
+        w_quant(0, 1)
+        s_mm(0)
+
+        extra = {
+            0: [lambda: w_weave(1, 0, 0, 4, True)],
+            1: [lambda: w_weave(1, 1, 0, 4, True), lambda: w_quant(1, 0), lambda: wt_turn(0, 0, 0, 6)],
+            2: [lambda: w_quant(1, 1), lambda: wt_turn(0, 0, 1, 7)],
+            3: [lambda: x_turn(1, 0, 0, 6), lambda: x_turn(1, 0, 1, 7), lambda: wt_quant(0, 0), lambda: x_scale(1, 0, 0), lambda: x_scale(1, 0, 1)],
+            4: [lambda: x_turn(1, 1, 0, 6), lambda: x_turn(1, 1, 1, 7), lambda: x_scale(1, 1, 0), lambda: x_quant(1, 0), lambda: x_scale(1, 1, 1)],
+            5: [lambda: wt_turn(0, 1, 0, 7), lambda: x_quant(1, 1)],
+            7: [lambda: wt_turn(0, 1, 1, 7)],
+            8: [lambda: wt_quant(0, 1)],
+            9: [lambda: wt_turn(1, 0, 0, 7)],
+            11: [lambda: wt_turn(1, 0, 1, 7)],
+            12: [lambda: wt_quant(1, 0)],
+            13: [lambda: wt_turn(1, 1, 0, 7)],
+            15: [lambda: wt_turn(1, 1, 1, 7), lambda: wt_quant(1, 1)],
+        }
+        for s in range(20):
+            b, t = divmod(s, 4)
+            if s + 1 < 16:
+                s_mm(s + 1)
+            if s < 16:
+                acts(s)
+                p_mm(s)
+            if s >= 4:
+                n_mm(s - 4)
+            if 1 <= s <= 16:
+                u_step(s - 1)
+            if s >= 4:
+                n_scale(s - 4)
+            if b >= 2 and t == 0:
+                r1_turn(b - 2, 1, 6)
+            if b >= 1 and t == 2:
+                r1_turn(b - 1, 0, 6)
+            if b >= 1 and t in (1, 2):
+                r2_weave(b - 1, t - 1)
+            if b >= 2 and t == 1:
+                r1_quant(b - 2)
+            if b >= 1 and t == 3:
+                r2_quant(b - 1)
+            for f in extra.get(s, []):
+                f()
+            if s >= 16:
+                gt_unit(0, 2 * t)
+                gt_unit(0, 2 * t + 1)
+        h_mm(0)
+        r1_turn(3, 1, 0)
+        g_turn(0)
+        gt_next = [[0, 1], [2, 3, 4], [5, 6, 7]]
+        for i in range(8):
+            h_scale(i)
+            hh_sum(i)
+            if i == 0:
+                r1_quant(3)
+            if i + 1 < 8:
+                h_mm(i + 1)
+            if i < 3:
+                for jd in gt_next[i]:
+                    gt_unit(1, jd)
+            if i >= 1:
+                combine(i - 1)
+            if i + 1 < 8:
+                g_turn(i + 1)
+            if i >= 4:
+                o_weave(0, i - 4, False)
+            gh_sum(i)
+            if i == 6:
+                o_quant(0, 0)
+        o_quant(0, 1)
+        o_scales(0)
+        combine(7)
+        o_weave(1, 0, False)
+        o_weave(1, 1, True)
+        o_weave(1, 2, True)
+        o_weave(1, 3, False)
+        o_quant(1, 0)
+        o_quant(1, 1)
+        o_scales(1)

@@ -17,6 +17,10 @@ W = 1024
 H = 512
 FLOPS = 3 * 2 * W * W * W
 
+G_BANKS = [2, 4, 2, 4, 2, 4, 0, 2]
+GT_SLOTS = [0, 2, 1, 3]
+H_TILES = 4
+
 
 def tile_adversarialdebiasingprojectedrepresentat_x1_kernel(tc, x, gamma, w, beta, y, z, a, out_0, out_1, out_2):
     nc = tc.nc
@@ -25,23 +29,23 @@ def tile_adversarialdebiasingprojectedrepresentat_x1_kernel(tc, x, gamma, w, bet
         ps = ctx.enter_context(tc.psum_pool(name="ps", bufs=1))
         ctx.enter_context(tc.manual_schedule())
 
-        def bank(i, dtype=F32):
-            return ps.tile([P, H if dtype is F32 else W], dtype, name="bank%d" % i, tag="bank%d" % i)
+        def bank(n, dtype=F32):
+            return ps.tile([P, H if dtype is F32 else W], dtype, name="bank%d" % n, tag="bank%d" % n)
 
-        def stage():
-            return sb.tile([P, 4 * H], BF16, name="stage", tag="stage", bufs=6, align_bytes=64)
+        def stage(n):
+            return sb.tile([P, 4 * H], BF16, name="stage%d" % n, tag="stage%d" % n, align_bytes=64)
 
-        def slot():
-            return sb.tile([P, 4, H], F32, name="slot", tag="slot", bufs=6)
+        def slot(n):
+            return sb.tile([P, 4, H], F32, name="slot%d" % n, tag="slot%d" % n)
 
         def operand(name):
             codes = sb.tile([P, 2, W], U32, name=name + "_codes", align_bytes=64)
             scales = sb.tile([P, 2, W], U8, name=name + "_scales", align_bytes=64)
             return codes, scales
 
-        def quantize(op, g, c0, src):
+        def quantize(op, g, first, src):
             n = src.shape[1] // 4
-            nc.vector.quantize_mx(out=op[0][:, g, c0:c0 + n].bitcast(FP8X4), scales=op[1][:, g, c0:c0 + n], in_=src)
+            nc.vector.quantize_mx(out=op[0][:, g, first:first + n].bitcast(FP8X4), scales=op[1][:, g, first:first + n], in_=src)
 
         def mx(out, lhs, l0, rhs, r0):
             for g in range(2):
@@ -51,9 +55,18 @@ def tile_adversarialdebiasingprojectedrepresentat_x1_kernel(tc, x, gamma, w, bet
                     rhs=rhs[0][:, g, r0:r0 + H].bitcast(FP8X4), rhs_scale=rhs[1][:, g, r0:r0 + H],
                     start=(g == 0), stop=(g == 1))
 
+        def move(engine, dst, src):
+            if engine == "vector":
+                nc.vector.tensor_copy(out=dst, in_=src)
+            elif engine == "scalar":
+                nc.scalar.copy(out=dst, in_=src)
+            else:
+                nc.gpsimd.tensor_scalar(out=dst, in0=src, scalar1=1.0, scalar2=0.0, op0=ALU.mult, op1=ALU.add)
+
         vec = {}
-        for name, src in (("gamma", gamma), ("z", z), ("beta", beta), ("a", a)):
+        for name in ("gamma", "z", "beta", "a"):
             vec[name] = sb.tile([P, 2, 4], BF16, name="vec_" + name)
+        for name, src in (("gamma", gamma), ("z", z), ("beta", beta), ("a", a)):
             nc.scalar.dma_start(out=vec[name][:], in_=src.rearrange("(g p t) -> p g t", g=2, t=4))
         x_raw = sb.tile([P, 8, W], BF16, name="x_raw", tag="big0")
         w_raw = sb.tile([P, 4, 4, H], BF16, name="w_raw", tag="big1")
@@ -64,8 +77,8 @@ def tile_adversarialdebiasingprojectedrepresentat_x1_kernel(tc, x, gamma, w, bet
         def rows(src, h):
             return src[h * H:(h + 1) * H, :].rearrange("(p t) d -> p t d", t=4)
 
-        def load_x(h, tp):
-            nc.sync.dma_start(out=x_raw[:, 4 * h + 2 * tp:4 * h + 2 * tp + 2, :], in_=rows(x, h)[:, 2 * tp:2 * tp + 2, :])
+        def load_x(h, tp, c0, c1):
+            nc.sync.dma_start(out=x_raw[:, 4 * h + 2 * tp:4 * h + 2 * tp + 2, c0:c1], in_=rows(x, h)[:, 2 * tp:2 * tp + 2, c0:c1])
 
         def load_w(g, gd):
             nc.sync.dma_start(out=w_raw[:, 2 * g + gd, :, :], in_=rows(w, gd)[:, :, g * H:(g + 1) * H])
@@ -73,23 +86,16 @@ def tile_adversarialdebiasingprojectedrepresentat_x1_kernel(tc, x, gamma, w, bet
         def load_y(h):
             nc.sync.dma_start(out=y_raw[:, 4 * h:4 * h + 4, :], in_=rows(y, h))
 
-        load_x(0, 0)
-        load_w(0, 0)
-        load_x(0, 1)
-        load_w(0, 1)
-        load_w(1, 0)
-        load_w(1, 1)
-        load_y(0)
-        nc.sync.dma_start(out=beta_b[:], in_=beta.partition_broadcast(P))
-        load_x(1, 0)
-        load_x(1, 1)
-        load_y(1)
-        nc.sync.dma_start(out=gamma_b[:], in_=gamma.partition_broadcast(P))
+        def load_spread(name):
+            dst, src = {"beta": (beta_b, beta), "gamma": (gamma_b, gamma)}[name]
+            nc.sync.dma_start(out=dst[:], in_=src.partition_broadcast(P))
 
         ident_f = sb.tile([P, P], F32, name="ident_f")
         ident_b = sb.tile([P, P], BF16, name="ident_b")
         neg_ident = sb.tile([P, P], BF16, name="neg_ident")
         ab_cols = sb.tile([P, 8, P], BF16, name="ab_cols")
+        zeros = sb.tile([P, H], BF16, name="zeros")
+        nc.vector.memset(zeros[:], 0.0)
         make_identity(nc, ident_f[:])
         make_identity(nc, ident_b[:])
         nc.gpsimd.memset(ab_cols[:], 0.0)
@@ -111,327 +117,342 @@ def tile_adversarialdebiasingprojectedrepresentat_x1_kernel(tc, x, gamma, w, bet
         nc.gpsimd.tensor_copy(out=beta_f[:], in_=col8("beta"))
         nc.gpsimd.tensor_scalar(out=neg_a[:], in0=col8("a"), scalar1=-1.0, scalar2=0.0, op0=ALU.mult, op1=ALU.add)
         nc.gpsimd.tensor_tensor(out=neg_aab[:], in0=neg_a[:], in1=ab[:], op=ALU.mult)
-        nc.gpsimd.tensor_copy(out=gamma_f[:], in_=col8("gamma"))
+        gamma_rows = sb.tile([P, P], BF16, name="gamma_rows")
+        nc.gpsimd.memset(gamma_rows[:], 0.0)
 
+        def load_gamma_rows():
+            nc.sync.dma_start(out=gamma_rows[0:8, :], in_=gamma.rearrange("(j p) -> j p", j=8))
+
+        live = {}
         z_rows = sb.tile([P, W], BF16, name="z_rows")
         ab_rows = sb.tile([P, W], BF16, name="ab_rows")
 
-        def spread_z():
-            b = bank(4, BF16)
+        def warm_pe():
+            for n in range(2):
+                b = bank(n)
+                nc.tensor.matmul(b[:], lhsT=zeros[:, 0:P], rhs=zeros[:], start=True, stop=True)
+
+        def turn_gamma(n):
+            live["gamma_bank"] = bank(n, BF16)
+            nc.tensor.transpose(live["gamma_bank"][:, 0:P], gamma_rows[:], ident_b[:])
+
+        def gamma_copy():
+            nc.scalar.copy(out=gamma_f[:], in_=live["gamma_bank"][:, 0:8])
+
+        def spread_z(n):
+            live["z_bank"] = bank(n, BF16)
             for i in range(8):
-                nc.tensor.transpose(b[:, i * P:(i + 1) * P], col8("z")[:, i:i + 1].to_broadcast([P, P]), ident_b[:])
-            nc.scalar.copy(out=z_rows[:], in_=b[:])
+                nc.tensor.transpose(live["z_bank"][:, i * P:(i + 1) * P], col8("z")[:, i:i + 1].to_broadcast([P, P]), ident_b[:])
 
-        def turn_ab():
-            b = bank(5, BF16)
-            for i in range(8):
-                nc.tensor.transpose(b[:, i * P:(i + 1) * P], ab_cols[:, i, :], ident_b[:])
-            nc.scalar.copy(out=ab_rows[:], in_=b[:])
+        def z_copy():
+            nc.scalar.copy(out=z_rows[:], in_=live["z_bank"][:])
 
-        xq, wq, wtq, r1q, r2q, oq = [operand(n) for n in ("xq", "wq", "wtq", "r1q", "r2q", "oq")]
-        st = {}
+        def turn_ab(n):
+            live["ab_bank"] = bank(n, BF16)
+            for col in range(8):
+                nc.tensor.transpose(live["ab_bank"][:, col * P:(col + 1) * P], ab_cols[:, col, :], ident_b[:])
 
-        def turn_words(bk, srcs):
-            b = bank(bk)
+        def ab_copy():
+            nc.scalar.copy(out=ab_rows[:], in_=live["ab_bank"][:])
+
+        xq, wq, wtq, r1q, r2q, oq = [operand(name) for name in ("xq", "wq", "wtq", "r1q", "r2q", "oq")]
+
+        def turn_words(n, words):
+            b = bank(n)
             for u in range(2):
-                for i in range(2):
-                    nc.tensor.transpose(b[:, (2 * u + i) * P:(2 * u + i + 1) * P], srcs(u, i), ident_f[:])
+                for v in range(2):
+                    nc.tensor.transpose(b[:, (2 * u + v) * P:(2 * u + v + 1) * P], words(u, v), ident_f[:])
             return b
 
-        def copy_words(dst, half, b):
-            nc.scalar.copy(out=dst[:].bitcast(F32)[:, half * H:(half + 1) * H].rearrange("p (n u) -> p n u", u=2),
-                           in_=b[:].rearrange("p (u n) -> p n u", u=2))
-
-        def x_turn(h, gd, tp, bk):
-            st["xb", h, gd, tp] = turn_words(
-                bk, lambda u, i: x_raw[:, 4 * h + 2 * tp + i, :].bitcast(F32)[:, 256 * gd + u:256 * gd + 256:2])
+        def x_turn(h, gd, tp, n):
+            live["x_bank", h, gd, tp] = turn_words(
+                n, lambda u, v: x_raw[:, 4 * h + 2 * tp + v, :].bitcast(F32)[:, 256 * gd + u:256 * gd + 256:2])
 
         def x_scale(h, gd, tp):
-            if tp == 0:
-                st["xs", h, gd] = stage()
+            if ("x_woven", h, gd) not in live:
+                live["x_woven", h, gd] = stage(1 + gd - h)
             nc.vector.tensor_tensor(
-                out=st["xs", h, gd][:, tp * W:(tp + 1) * W].rearrange("p (n u e) -> p n u e", u=2, e=2),
-                in0=st["xb", h, gd, tp][:].bitcast(BF16).rearrange("p (u n e) -> p n u e", u=2, e=2),
+                out=live["x_woven", h, gd][:, tp * W:(tp + 1) * W].rearrange("p (n u e) -> p n u e", u=2, e=2),
+                in0=live["x_bank", h, gd, tp][:].bitcast(BF16).rearrange("p (u n e) -> p n u e", u=2, e=2),
                 in1=vec["gamma"][:, gd, :].rearrange("p (u e) -> p u e", u=2).unsqueeze(1).to_broadcast([P, 256, 2, 2]),
                 op=ALU.mult)
 
         def x_quant(h, gd):
-            quantize(xq, gd, h * H, st["xs", h, gd][:])
+            quantize(xq, gd, h * H, live["x_woven", h, gd][:])
 
-        def w_weave(g, gd, t0, t1, on_vector):
-            if t0 == 0:
-                st["ws", g, gd] = stage()
-            dst = st["ws", g, gd][:].rearrange("p (t m j) -> p t m j", t=4, j=4)[:, t0:t1]
+        def w_weave(g, gd, t0, t1, engine):
+            if ("w_woven", g, gd) not in live:
+                live["w_woven", g, gd] = stage(6 + gd if g else 3 * gd)
+            dst = live["w_woven", g, gd][:].rearrange("p (t m j) -> p t m j", t=4, j=4)[:, t0:t1]
             src = w_raw[:, 2 * g + gd, :, :].rearrange("p j (m t) -> p t m j", t=4)[:, t0:t1]
-            if on_vector:
-                nc.vector.tensor_copy(out=dst, in_=src)
-            else:
-                nc.scalar.copy(out=dst, in_=src)
+            move(engine, dst, src)
 
-        def w_quant(g, gd):
-            quantize(wq, gd, g * H, st["ws", g, gd][:])
+        def w_quant(g, gd, t0, t1):
+            quantize(wq, gd, g * H + t0 * P, live["w_woven", g, gd][:, t0 * H:t1 * H])
 
-        def wt_turn(g, gd, jp, bk):
-            if jp == 0:
-                st["wts", g, gd] = stage()
-            b = turn_words(bk, lambda u, i: w_raw[:, 2 * g + gd, 2 * jp + i, :].bitcast(F32)[:, u:256:2])
-            copy_words(st["wts", g, gd], jp, b)
+        def wt_turn(g, gd, jp, n):
+            live["wt_bank", g, gd, jp] = turn_words(n, lambda u, v: w_raw[:, 2 * g + gd, 2 * jp + v, :].bitcast(F32)[:, u:256:2])
+
+        def wt_copy(g, gd, jp):
+            if ("wt_woven", g, gd) not in live:
+                live["wt_woven", g, gd] = stage(4 - 2 * g + gd)
+            words = live["wt_woven", g, gd][:].bitcast(F32).rearrange("p (m j u) -> p m j u", j=4, u=2)
+            nc.scalar.copy(out=words[:, :, 2 * jp:2 * jp + 2, :],
+                           in_=live["wt_bank", g, gd, jp][:].rearrange("p (u j m) -> p m j u", u=2, j=2))
 
         def wt_quant(g, gd):
-            quantize(wtq, g, gd * H, st["wts", g, gd][:])
+            quantize(wtq, g, gd * H, live["wt_woven", g, gd][:])
 
         def unit(s):
             return s // 8, (s // 4) % 2, s % 4
 
         def s_mm(s):
             h, g, t = unit(s)
-            st["s", s] = bank(s % 2)
-            mx(st["s", s][:], wq, g * H + t * P, xq, h * H)
+            live["s_bank", s] = bank(s % 2)
+            mx(live["s_bank", s][:], wq, g * H + t * P, xq, h * H)
 
-        def acts(s):
+        def act(s, name):
             h, g, t = unit(s)
             b = s // 4
-            if t == 0:
-                st["q", b], st["sig", b], st["q2", b] = slot(), slot(), slot()
-            scale = beta_f[:, 4 * g + t:4 * g + t + 1]
-            nc.scalar.activation(out=st["q", b][:, t, :], in_=st["s", s][:], func=ACT.Tanh, scale=scale)
-            nc.scalar.activation(out=st["sig", b][:, t, :], in_=st["s", s][:], func=ACT.Sigmoid, scale=scale)
-            nc.scalar.activation(out=st["q2", b][:, t, :], in_=st["q", b][:, t, :], func=ACT.Square)
+            if (name, b) not in live:
+                live[name, b] = slot(3 * (b % 2) + (0 if name == "q" else 1))
+            nc.scalar.activation(out=live[name, b][:, t, :], in_=live["s_bank", s][:],
+                                 func=ACT.Tanh if name == "q" else ACT.Sigmoid, scale=beta_f[:, 4 * g + t:4 * g + t + 1])
+
+        def square(s, engine):
+            b, t = divmod(s, 4)
+            if ("qq", b) not in live:
+                live["qq", b] = slot(3 * (b % 2) + 2)
+            q = live["q", b][:, t, :]
+            if engine == "scalar":
+                nc.scalar.activation(out=live["qq", b][:, t, :], in_=q, func=ACT.Square)
+            else:
+                nc.gpsimd.tensor_tensor(out=live["qq", b][:, t, :], in0=q, in1=q, op=ALU.mult)
 
         def p_mm(s):
             h, g, t = unit(s)
-            st["p", s] = bank(2 + s % 2)
-            i = 4 * g + t
-            nc.tensor.matmul(st["p", s][:], lhsT=ab_rows[:, i * P:(i + 1) * P], rhs=z_rows[:, h * H:(h + 1) * H], start=True, stop=True)
+            live["p_bank", s] = bank(2 + s % 2)
+            col = 4 * g + t
+            nc.tensor.matmul(live["p_bank", s][:], lhsT=ab_rows[:, col * P:(col + 1) * P], rhs=z_rows[:, h * H:(h + 1) * H],
+                             start=True, stop=True)
 
         def u_step(s):
             h, g, t = unit(s)
-            q = st["q", s // 4][:, t, :]
-            nc.vector.scalar_tensor_tensor(out=q, in0=q, scalar=neg_aab[:, 4 * g + t:4 * g + t + 1], in1=st["p", s][:],
+            q = live["q", s // 4][:, t, :]
+            nc.vector.scalar_tensor_tensor(out=q, in0=q, scalar=neg_aab[:, 4 * g + t:4 * g + t + 1], in1=live["p_bank", s][:],
                                            op0=ALU.mult, op1=ALU.add)
 
-        def r2_weave(b, half):
-            if half == 0:
-                st["r2s", b] = stage()
-            n = slice(half * 256, (half + 1) * 256)
+        def r2_pairs(b, u):
+            if ("r2_pairs", b) not in live:
+                live["r2_pairs", b] = stage(8)
             nc.vector.scalar_tensor_tensor(
-                out=st["r2s", b][:, half * W:(half + 1) * W].rearrange("p (n t) -> p n t", t=4),
-                in0=st["q2", b][:, :, n].rearrange("p t n -> p n t"), scalar=1.0,
-                in1=st["q", b][:, :, n].rearrange("p t n -> p n t"), op0=ALU.subtract, op1=ALU.mult)
+                out=live["r2_pairs", b][:, u * W:(u + 1) * W].rearrange("p (n e) -> p n e", e=2),
+                in0=live["qq", b][:, 2 * u:2 * u + 2, :].rearrange("p e n -> p n e"), scalar=1.0,
+                in1=live["q", b][:, 2 * u:2 * u + 2, :].rearrange("p e n -> p n e"), op0=ALU.subtract, op1=ALU.mult)
+
+        def r2_weave(b, engine):
+            live["r2_woven", b] = stage(4 + b % 2)
+            move(engine, live["r2_woven", b][:].rearrange("p (n u e) -> p n u e", u=2, e=2),
+                 live["r2_pairs", b][:].rearrange("p (u n e) -> p n u e", u=2, e=2))
 
         def r2_quant(b):
-            quantize(r2q, b % 2, (b // 2) * H, st["r2s", b][:])
+            quantize(r2q, b % 2, (b // 2) * H, live["r2_woven", b][:])
 
-        def n_mm(s):
-            h, g, tn = unit(s)
-            b = bank(4 + s % 2)
-            st["n", s] = b
+        def n_mm(r):
+            h, g, tn = unit(r)
+            b = bank(4 + r % 2)
+            live["n_bank", r] = b
             nc.tensor.matmul(b[:].rearrange("p (t m) -> p t m", t=4), lhsT=neg_ident[:],
                              rhs=y_raw[:, 4 * h + tn, g * H:(g + 1) * H].rearrange("p (m t) -> p t m", t=4), start=True, stop=False)
             for t in range(4):
-                nc.tensor.matmul(b[:, t * P:(t + 1) * P], lhsT=st["sig", s // 4][:, t, tn * P:(tn + 1) * P], rhs=ident_f[:],
+                nc.tensor.matmul(b[:, t * P:(t + 1) * P], lhsT=live["sig", r // 4][:, t, tn * P:(tn + 1) * P], rhs=ident_f[:],
                                  start=False, stop=(t == 3), is_transpose=True)
 
-        def n_scale(s):
-            h, g, tn = unit(s)
-            st["r1n", s] = sb.tile([P, H], BF16, name="r1n", tag="r1n", bufs=4)
+        def n_scale(r):
+            h, g, tn = unit(r)
+            live["r1_rows", r] = sb.tile([P, H], BF16, name="r1n%d" % tn, tag="r1n%d" % tn)
             nc.vector.tensor_tensor(
-                out=st["r1n", s][:].rearrange("p (u m e) -> p u m e", u=2, e=2),
-                in0=st["n", s][:].rearrange("p (u e m) -> p u m e", u=2, e=2),
+                out=live["r1_rows", r][:].rearrange("p (u m e) -> p u m e", u=2, e=2),
+                in0=live["n_bank", r][:].rearrange("p (u e m) -> p u m e", u=2, e=2),
                 in1=beta_b[:, g * H:(g + 1) * H].rearrange("p (m u e) -> p u m e", u=2, e=2), op=ALU.mult)
 
-        def r1_turn(b, tp, bk):
-            if tp == 0:
-                st["r1s", b] = stage()
-            t = turn_words(bk, lambda u, i: st["r1n", 4 * b + 2 * tp + i][:].bitcast(F32)[:, u * P:(u + 1) * P])
-            copy_words(st["r1s", b], tp, t)
+        def r1_turn(b, tp, n):
+            live["r1_bank", b, tp] = turn_words(
+                n, lambda u, v: live["r1_rows", 4 * b + 2 * tp + v][:].bitcast(F32)[:, u * P:(u + 1) * P])
+
+        def r1_copy(b, tp):
+            if ("r1_woven", b) not in live:
+                live["r1_woven", b] = stage(6 + b % 2)
+            words = live["r1_woven", b][:].bitcast(F32)[:, tp * H:(tp + 1) * H]
+            nc.scalar.copy(out=words.rearrange("p (n u) -> p n u", u=2),
+                           in_=live["r1_bank", b, tp][:].rearrange("p (u n) -> p n u", u=2))
 
         def r1_quant(b):
-            quantize(r1q, b % 2, (b // 2) * H, st["r1s", b][:])
+            quantize(r1q, b % 2, (b // 2) * H, live["r1_woven", b][:])
 
-        def gt_unit(h, jd):
+        def gt_mm(h, jd):
+            live["gt_bank", h, jd] = bank(jd % 2)
+            mx(live["gt_bank", h, jd][:], wtq, jd * P, r1q, h * H)
+
+        def gt_scale(h, jd):
             gd, j = divmod(jd, 4)
-            if j == 0:
-                st["gt", h, gd] = slot()
-            b = bank(jd % 2)
-            mx(b[:], wtq, jd * P, r1q, h * H)
-            nc.scalar.activation(out=st["gt", h, gd][:, j, :], in_=b[:], func=ACT.Copy, scale=gamma_f[:, jd:jd + 1])
+            if ("gt", h, gd) not in live:
+                live["gt", h, gd] = slot(GT_SLOTS[2 * h + gd])
+            nc.scalar.activation(out=live["gt", h, gd][:, j, :], in_=live["gt_bank", h, jd][:], func=ACT.Copy,
+                                 scale=gamma_f[:, jd:jd + 1])
 
-        def g_turn(i):
+        def g_turn(i, gd):
             h, tn = divmod(i, 4)
-            for gd in range(2):
-                b = bank(2 + 2 * (i % 2) + gd)
-                st["g", i, gd] = b
-                for j in range(4):
-                    nc.tensor.transpose(b[:, j * P:(j + 1) * P], st["gt", h, gd][:, j, tn * P:(tn + 1) * P], ident_f[:])
+            b = bank(G_BANKS[i] + gd)
+            live["g_bank", i, gd] = b
+            for j in range(4):
+                nc.tensor.transpose(b[:, j * P:(j + 1) * P], live["gt", h, gd][:, j, tn * P:(tn + 1) * P], ident_f[:])
 
-        def h_mm(i):
-            for gd in range(2):
-                st["hp", i, gd] = bank(6 + gd)
-                mx(st["hp", i, gd][:], r2q, i * P, wtq, gd * H)
+        def h_mm(i, n, gd):
+            live["h_bank", i, gd] = bank(n)
+            mx(live["h_bank", i, gd][:], r2q, i * P, wtq, gd * H)
 
-        def natural(b):
-            return b[:].rearrange("p (j m) -> p m j", j=4)
+        h_rows = [sb.tile([P, W + 8], F32, name="h_rows%d" % n) for n in range(H_TILES)]
+        for tile in h_rows:
+            nc.gpsimd.tensor_scalar(out=tile[:, W:W + 1], in0=ident_f[:, 0:1], scalar1=0.0, scalar2=1e-3, op0=ALU.mult, op1=ALU.add)
 
-        def by4(ap):
-            return ap.rearrange("p (m j) -> p m j", j=4)
+        def h_cols(i, gd):
+            return h_rows[i % H_TILES][:, gd * H:(gd + 1) * H]
 
-        def h_scale(i):
-            st["h", i] = sb.tile([P, W], F32, name="h", tag="h", bufs=2)
-            for gd in range(2):
-                c = slice(gd * H, (gd + 1) * H)
-                nc.vector.tensor_tensor(out=by4(st["h", i][:, c]), in0=natural(st["hp", i, gd]), in1=by4(gamma_b[:, c]), op=ALU.mult)
+        def h_scale(i, gd):
+            nc.vector.tensor_tensor(out=h_cols(i, gd), in0=live["h_bank", i, gd][:], in1=gamma_b[:, gd * H:(gd + 1) * H], op=ALU.mult)
 
-        junk_s = sb.tile([P, W], BF16, name="junk_s")
-        junk_v = sb.tile([P, 2, H], BF16, name="junk_v")
+        def h_copy(i, gd):
+            nc.scalar.copy(out=h_cols(i, gd), in_=live["h_bank", i, gd][:])
 
-        def small(name):
-            return sb.tile([P, 1], F32, name=name, tag=name, bufs=2)
+        def h_finish(i, gd):
+            nc.gpsimd.tensor_tensor(out=h_cols(i, gd), in0=h_cols(i, gd), in1=gamma_b[:, gd * H:(gd + 1) * H], op=ALU.mult)
+
+        squares_out = sb.tile([P, W + 8], BF16, name="junk_s")
+        products_out = sb.tile([P, 2, H], BF16, name="junk_v")
+
+        def small(name, i, n=1):
+            return sb.tile([P, n], F32, name="%s%d" % (name, i))
 
         def hh_sum(i):
-            hh = small("hh")
-            nc.scalar.activation(out=junk_s[:], in_=st["h", i][:], func=ACT.Square, accum_out=hh[:])
-            st["den", i] = small("den")
-            nc.gpsimd.tensor_scalar(out=st["den", i][:], in0=hh[:], scalar1=1e-6, scalar2=1.0, op0=ALU.add, op1=ALU.mult)
+            live["den", i] = small("den", i)
+            nc.scalar.activation(out=squares_out[:, 0:W + 1], in_=h_rows[i % H_TILES][:, 0:W + 1], func=ACT.Square,
+                                 accum_out=live["den", i][:])
 
-        def gh_sum(i):
-            part = [small("gh0"), small("gh1")]
-            rec = small("rec")
-            for gd in range(2):
-                nc.vector.scalar_tensor_tensor(
-                    out=by4(junk_v[:, gd, :]), in0=natural(st["g", i, gd]), scalar=-1.0, in1=by4(st["h", i][:, gd * H:(gd + 1) * H]),
-                    op0=ALU.mult, op1=ALU.mult, accum_out=part[gd][:])
-                if gd == 0:
-                    nc.vector.reciprocal(out=rec[:], in_=st["den", i][:])
-            neg_k = small("neg_k")
-            nc.gpsimd.tensor_scalar(out=neg_k[:], in0=part[0][:], scalar1=part[1][:], scalar2=rec[:], op0=ALU.add, op1=ALU.mult)
-            st["coef", i] = small("coef")
-            nc.gpsimd.tensor_scalar(out=st["coef", i][:], in0=neg_k[:], scalar1=1.0, scalar2=-0.5, op0=ALU.mult, op1=ALU.add)
+        def invert(i):
+            live["rec", i] = small("rec", i)
+            nc.vector.reciprocal(out=live["rec", i][:], in_=live["den", i][:])
 
-        def combine(i):
+        def gh_sum(i, gd):
+            if ("gh", i) not in live:
+                live["gh", i] = small("gh", i, 2)
+            nc.vector.scalar_tensor_tensor(
+                out=products_out[:, gd, :], in0=live["g_bank", i, gd][:], scalar=-1.0, in1=h_cols(i, gd),
+                op0=ALU.mult, op1=ALU.mult, accum_out=live["gh", i][:, gd:gd + 1])
+
+        def coefficient(i):
+            live["coef", i] = small("coef", i)
+            parts = small("parts", i, 2)
+            nc.vector.tensor_scalar(out=parts[:], in0=live["gh", i][:], scalar1=live["rec", i][:], scalar2=-0.5,
+                                    op0=ALU.mult, op1=ALU.add, accum_out=live["coef", i][:])
+
+        def combine(i, gd):
             h, tn = divmod(i, 4)
-            if tn == 0:
-                st["o", h] = sb.tile([P, 4, W], F32, name="o", tag="big%d" % h)
-            for gd in range(2):
-                c = slice(gd * H, (gd + 1) * H)
-                nc.vector.scalar_tensor_tensor(
-                    out=by4(st["o", h][:, tn, c]), in0=by4(st["h", i][:, c]), scalar=st["coef", i][:], in1=natural(st["g", i, gd]),
-                    op0=ALU.mult, op1=ALU.add)
-            nc.sync.dma_start(out=rows(out_0, h)[:, tn, :], in_=st["o", h][:, tn, :])
+            if ("out", h) not in live:
+                live["out", h] = sb.tile([P, 4, W], F32, name="o", tag="big%d" % h)
+            nc.vector.scalar_tensor_tensor(
+                out=live["out", h][:, tn, gd * H:(gd + 1) * H], in0=h_cols(i, gd), scalar=live["coef", i][:],
+                in1=live["g_bank", i, gd][:], op0=ALU.mult, op1=ALU.add)
 
-        def o_weave(h, c, on_vector):
-            if c % 2 == 0:
-                st["os", h, c // 2] = stage()
-            dst = st["os", h, c // 2][:, (c % 2) * W:(c % 2 + 1) * W].rearrange("p (d t) -> p d t", t=4)
-            src = st["o", h][:, :, c * 256:(c + 1) * 256].rearrange("p t d -> p d t")
-            if on_vector:
-                nc.vector.tensor_copy(out=dst, in_=src)
-            else:
-                nc.scalar.copy(out=dst, in_=src)
+        def o_store(i):
+            h, tn = divmod(i, 4)
+            nc.sync.dma_start(out=rows(out_0, h)[:, tn, :], in_=live["out", h][:, tn, :])
 
-        def o_quant(h, gd):
-            quantize(oq, h, gd * H, st["os", h, gd][:])
-            c = slice(gd * H, (gd + 1) * H)
+        def o_cols(h, c0, c1):
+            return live["out_woven", h, c0 // 4][:, (c0 % 4) * H:(c0 % 4 + c1 - c0) * H]
+
+        def o_weave(h, c0, c1, engine):
+            gd = c0 // 4
+            if ("out_woven", h, gd) not in live:
+                live["out_woven", h, gd] = stage(2 * h + gd)
+            move(engine, o_cols(h, c0, c1).rearrange("p (d t) -> p d t", t=4),
+                 live["out", h][:, :, c0 * P:c1 * P].rearrange("p t d -> p d t"))
+
+        def o_quant(h, c0, c1):
+            quantize(oq, h, c0 * P, o_cols(h, c0, c1))
+            c = slice(c0 * P, c1 * P)
             nc.sync.dma_start(out=out_1[h].rearrange("p m t -> p (m t)").bitcast(I32)[:, c], in_=oq[0][:, h, c].bitcast(I32))
 
         def o_scales(h):
             for quad in range(4):
                 eng = nc.sync if quad % 2 == 0 else nc.scalar
-                eng.dma_start(out=out_2[h, 4 * quad:4 * quad + 4, :].bitcast(I32), in_=oq[1][32 * quad:32 * quad + 4, h, :].bitcast(I32))
+                eng.dma_start(out=out_2[h, 4 * quad:4 * quad + 4, :].bitcast(I32),
+                              in_=oq[1][32 * quad:32 * quad + 4, h, :].bitcast(I32))
 
-        x_turn(0, 0, 0, 6)
-        x_turn(0, 1, 0, 7)
-        spread_z()
-        x_scale(0, 0, 0)
-        x_scale(0, 1, 0)
-        w_weave(0, 0, 0, 2, False)
-        w_weave(0, 0, 2, 4, True)
-        x_turn(0, 0, 1, 2)
-        x_turn(0, 1, 1, 3)
-        turn_ab()
-        x_scale(0, 0, 1)
-        w_quant(0, 0)
-        x_scale(0, 1, 1)
-        x_quant(0, 0)
-        w_weave(0, 1, 0, 2, False)
-        w_weave(0, 1, 2, 4, True)
-        x_quant(0, 1)
-        w_quant(0, 1)
-        s_mm(0)
 
-        extra = {
-            0: [lambda: w_weave(1, 0, 0, 4, True)],
-            1: [lambda: w_weave(1, 1, 0, 4, True), lambda: w_quant(1, 0), lambda: wt_turn(0, 0, 0, 6)],
-            2: [lambda: w_quant(1, 1), lambda: wt_turn(0, 0, 1, 7)],
-            3: [lambda: x_turn(1, 0, 0, 6), lambda: x_turn(1, 0, 1, 7), lambda: wt_quant(0, 0), lambda: x_scale(1, 0, 0), lambda: x_scale(1, 0, 1)],
-            4: [lambda: x_turn(1, 1, 0, 6), lambda: x_turn(1, 1, 1, 7), lambda: x_scale(1, 1, 0), lambda: x_quant(1, 0), lambda: x_scale(1, 1, 1)],
-            5: [lambda: wt_turn(0, 1, 0, 7), lambda: x_quant(1, 1)],
-            7: [lambda: wt_turn(0, 1, 1, 7)],
-            8: [lambda: wt_quant(0, 1)],
-            9: [lambda: wt_turn(1, 0, 0, 7)],
-            11: [lambda: wt_turn(1, 0, 1, 7)],
-            12: [lambda: wt_quant(1, 0)],
-            13: [lambda: wt_turn(1, 1, 0, 7)],
-            15: [lambda: wt_turn(1, 1, 1, 7), lambda: wt_quant(1, 1)],
-        }
-        for s in range(20):
-            b, t = divmod(s, 4)
-            if s + 1 < 16:
-                s_mm(s + 1)
-            if s < 16:
-                acts(s)
-                p_mm(s)
-            if s >= 4:
-                n_mm(s - 4)
-            if 1 <= s <= 16:
-                u_step(s - 1)
-            if s >= 4:
-                n_scale(s - 4)
-            if b >= 2 and t == 0:
-                r1_turn(b - 2, 1, 6)
-            if b >= 1 and t == 2:
-                r1_turn(b - 1, 0, 6)
-            if b >= 1 and t in (1, 2):
-                r2_weave(b - 1, t - 1)
-            if b >= 2 and t == 1:
-                r1_quant(b - 2)
-            if b >= 1 and t == 3:
-                r2_quant(b - 1)
-            for f in extra.get(s, []):
-                f()
-            if s >= 16:
-                gt_unit(0, 2 * t)
-                gt_unit(0, 2 * t + 1)
-        h_mm(0)
-        r1_turn(3, 1, 0)
-        g_turn(0)
-        gt_next = [[0, 1], [2, 3, 4], [5, 6, 7]]
-        for i in range(8):
-            h_scale(i)
-            hh_sum(i)
-            if i == 0:
-                r1_quant(3)
-            if i + 1 < 8:
-                h_mm(i + 1)
-            if i < 3:
-                for jd in gt_next[i]:
-                    gt_unit(1, jd)
-            if i >= 1:
-                combine(i - 1)
-            if i + 1 < 8:
-                g_turn(i + 1)
-            if i >= 4:
-                o_weave(0, i - 4, False)
-            gh_sum(i)
-            if i == 6:
-                o_quant(0, 0)
-        o_quant(0, 1)
-        o_scales(0)
-        combine(7)
-        o_weave(1, 0, False)
-        o_weave(1, 1, True)
-        o_weave(1, 2, True)
-        o_weave(1, 3, False)
-        o_quant(1, 0)
-        o_quant(1, 1)
-        o_scales(1)
+        warm_pe(); warm_pe(); load_x(0, 0, 512, 1024); warm_pe(); x_turn(0, 1, 0, 7); x_scale(0, 1, 0)
+        load_x(0, 0, 0, 512); x_turn(0, 0, 0, 6); load_x(0, 1, 0, 512); x_turn(0, 0, 1, 2); load_w(0, 0)
+        x_scale(0, 0, 0); x_scale(0, 0, 1); turn_ab(7); w_weave(0, 0, 2, 4, "scalar"); spread_z(6); z_copy()
+        load_x(0, 1, 512, 1024); load_w(0, 1); x_turn(0, 1, 1, 3); wt_turn(0, 0, 0, 4); ab_copy(); x_scale(0, 1, 1)
+        load_w(1, 1); load_x(1, 1, 0, 1024); load_gamma_rows(); w_weave(0, 0, 0, 2, "vector"); x_quant(0, 0)
+        wt_turn(0, 0, 1, 5); w_quant(0, 0, 0, 2); w_weave(0, 1, 0, 2, "scalar"); wt_copy(0, 0, 1); p_mm(1)
+        x_quant(0, 1); p_mm(0); wt_copy(0, 0, 0); w_quant(0, 1, 0, 2)
+
+        s_mm(0); w_weave(0, 1, 2, 4, "scalar"); act(0, "q"); act(0, "sig"); s_mm(1); act(1, "sig"); x_turn(1, 0, 1, 7)
+        w_weave(1, 1, 0, 2, "vector"); wt_turn(0, 1, 1, 5); wt_turn(0, 1, 0, 4); wt_copy(0, 1, 1); w_quant(0, 0, 2, 4)
+        w_weave(1, 1, 2, 4, "vector"); load_x(1, 0, 0, 1024); act(1, "q"); w_quant(0, 1, 2, 4); load_w(1, 0)
+        w_weave(1, 0, 0, 2, "vector"); w_weave(1, 0, 2, 4, "vector"); wt_copy(0, 1, 0); s_mm(2); act(2, "sig")
+        act(2, "q"); load_spread("beta"); w_quant(1, 1, 0, 4); w_quant(1, 0, 0, 4); x_turn(1, 0, 0, 6); x_scale(1, 0, 0)
+        x_turn(1, 1, 1, 5); s_mm(3); x_scale(1, 1, 1); act(3, "q"); act(3, "sig"); square(1, "gpsimd"); x_scale(1, 0, 1)
+        x_turn(1, 1, 0, 4); wt_turn(1, 0, 0, 6); x_scale(1, 1, 0); s_mm(4); load_y(0); n_mm(1); wt_quant(0, 0); s_mm(5)
+        square(2, "scalar"); square(0, "scalar"); x_quant(1, 1); act(4, "sig"); n_mm(0); act(4, "q"); act(5, "sig")
+        act(5, "q"); u_step(1); wt_copy(1, 0, 0); square(5, "scalar"); u_step(0); wt_turn(1, 0, 1, 7); n_scale(1)
+        n_scale(0); s_mm(6); load_y(1); act(6, "sig"); wt_copy(1, 0, 1); x_quant(1, 0); n_mm(3); load_spread("gamma")
+        p_mm(3); s_mm(7); r2_pairs(0, 0); square(3, "gpsimd"); u_step(3); act(7, "sig"); p_mm(2); u_step(2); act(7, "q")
+        n_scale(3); n_mm(2); n_scale(2); r2_pairs(0, 1); r1_turn(0, 0, 6); act(6, "q"); wt_turn(1, 1, 0, 7)
+        square(4, "gpsimd"); r1_copy(0, 0); wt_quant(0, 1); square(6, "scalar"); p_mm(4)
+
+        n_mm(5); n_scale(5); p_mm(5); r2_weave(0, "scalar"); s_mm(9); act(9, "q"); s_mm(8); u_step(4); u_step(5)
+        n_mm(4); act(9, "sig"); r1_turn(0, 1, 6); n_scale(4); p_mm(6); u_step(6); p_mm(7); n_mm(7); square(7, "gpsimd")
+        u_step(7); n_scale(7); square(9, "gpsimd"); wt_copy(1, 1, 0); turn_gamma(7); act(8, "q"); r2_pairs(1, 1)
+        r2_pairs(1, 0); act(8, "sig"); s_mm(11); r1_copy(0, 1); r1_quant(0); r2_quant(0); s_mm(10); n_mm(6)
+        gamma_copy(); wt_turn(1, 1, 1, 7); act(11, "sig"); act(10, "sig"); n_mm(9); n_scale(6); act(10, "q")
+        r1_turn(1, 0, 6); p_mm(9); wt_copy(1, 1, 1); act(11, "q"); p_mm(8); s_mm(13); square(8, "scalar"); s_mm(12)
+        n_mm(8); r1_copy(1, 0); r1_turn(1, 1, 6); u_step(9); r2_weave(1, "scalar"); square(10, "gpsimd"); n_scale(9)
+        u_step(8); p_mm(10); wt_quant(1, 1); n_mm(11); r2_quant(1); act(13, "q"); wt_quant(1, 0); u_step(10)
+        h_mm(0, 7, 1); p_mm(11); act(12, "q"); act(12, "sig"); s_mm(14); n_scale(8); p_mm(12); n_scale(11)
+        square(11, "scalar"); act(13, "sig"); s_mm(15); n_mm(10); r1_copy(1, 1); r1_turn(2, 0, 6); u_step(11); p_mm(13)
+        act(14, "q"); act(14, "sig"); act(15, "sig"); square(13, "gpsimd"); r1_quant(1); act(15, "q"); h_copy(0, 1)
+
+        gt_mm(0, 0); square(12, "scalar"); square(14, "scalar"); r2_pairs(2, 0); n_mm(13); gt_mm(0, 1); r2_pairs(2, 1)
+        gt_scale(0, 1); n_scale(10); h_mm(1, 7, 1); h_copy(1, 1); u_step(13); u_step(12); n_mm(12); gt_scale(0, 0)
+        n_scale(13); square(15, "gpsimd"); r1_copy(2, 0); p_mm(15); n_scale(12); h_finish(0, 1); p_mm(14); u_step(14)
+        u_step(15); h_mm(0, 7, 0); r2_weave(2, "scalar"); gt_mm(0, 2); gt_scale(0, 2); gt_mm(0, 3); gt_scale(0, 3)
+        n_mm(14); r1_turn(2, 1, 6); h_scale(0, 0); gt_mm(0, 4); r2_pairs(3, 1); hh_sum(0); r1_copy(2, 1); r2_quant(2)
+        r2_pairs(3, 0); h_mm(1, 7, 0); h_scale(1, 0); invert(0); gt_mm(0, 5); n_scale(14); n_mm(15); n_scale(15)
+        g_turn(0, 0); gh_sum(0, 0); r1_turn(3, 0, 6); gt_scale(0, 4); gt_mm(0, 6); gt_scale(0, 5); r2_weave(3, "scalar")
+        gt_mm(0, 7); r1_quant(2); h_mm(2, 7, 1); r2_quant(3); g_turn(1, 0); gt_scale(0, 6); r1_turn(3, 1, 0)
+        gt_scale(0, 7); g_turn(0, 1); h_scale(2, 1); gh_sum(0, 1); r1_copy(3, 0); r1_copy(3, 1); r1_quant(3)
+        coefficient(0); g_turn(1, 1); h_mm(2, 6, 0); h_scale(2, 0); h_finish(1, 1); hh_sum(1); gh_sum(1, 1)
+        gh_sum(1, 0); invert(1); h_mm(3, 7, 1); h_copy(3, 1); h_finish(3, 1)
+
+        gt_mm(1, 1); gt_scale(1, 1); gt_mm(1, 0); h_mm(3, 6, 0); combine(0, 0); gt_mm(1, 3); h_mm(4, 7, 1)
+        coefficient(1); gt_scale(1, 0); h_copy(3, 0); hh_sum(2); h_finish(3, 0); h_mm(4, 6, 0); combine(0, 1)
+        g_turn(2, 0); g_turn(2, 1); h_copy(4, 0); gt_mm(1, 2); gt_scale(1, 3); h_copy(4, 1); gt_scale(1, 2)
+        h_mm(5, 6, 0); combine(1, 0); g_turn(3, 0); combine(1, 1); g_turn(3, 1); gh_sum(2, 0); o_store(1); hh_sum(3)
+        gt_mm(1, 5); gt_scale(1, 5); gt_mm(1, 4); gt_scale(1, 4); invert(2); gh_sum(2, 1); h_mm(5, 7, 1); h_finish(4, 0)
+        h_scale(5, 0); coefficient(2); h_mm(6, 6, 0); gh_sum(3, 1); gh_sum(3, 0); gt_mm(1, 7); h_finish(4, 1); invert(3)
+        gt_mm(1, 6); combine(2, 1); h_copy(5, 1); coefficient(3); combine(2, 0); o_store(2); combine(3, 0)
+        h_mm(6, 7, 1); gt_scale(1, 7); h_scale(6, 0); combine(3, 1); g_turn(4, 0); gt_scale(1, 6); gh_sum(4, 0)
+        g_turn(4, 1); gh_sum(4, 1); h_finish(5, 1); g_turn(5, 0); gh_sum(5, 0); h_mm(7, 6, 0); h_copy(6, 1)
+        h_finish(6, 1); hh_sum(4); h_copy(7, 0); h_finish(7, 0); invert(4); g_turn(5, 1); g_turn(6, 0); gh_sum(5, 1)
+        o_store(0); coefficient(4); gh_sum(6, 0); hh_sum(5); invert(5); h_mm(7, 7, 1); h_copy(7, 1); combine(4, 0)
+        h_finish(7, 1); combine(4, 1); coefficient(5); o_store(4); g_turn(6, 1); gh_sum(6, 1); g_turn(7, 0); hh_sum(6)
+        combine(5, 1)
+
+        o_weave(0, 4, 6, "scalar"); invert(6); g_turn(7, 1); gh_sum(7, 0); gh_sum(7, 1); o_store(3); combine(5, 0)
+        hh_sum(7); invert(7); o_weave(0, 2, 4, "scalar"); o_weave(0, 6, 8, "gpsimd"); coefficient(6); coefficient(7)
+        combine(6, 1); combine(7, 1); o_weave(0, 0, 2, "scalar"); o_weave(1, 4, 6, "scalar"); o_store(5); combine(7, 0)
+        o_weave(1, 6, 7, "scalar"); o_store(7); combine(6, 0); o_store(6); o_quant(0, 4, 8); o_quant(0, 0, 4)
+        o_weave(1, 3, 4, "vector"); o_scales(0); o_weave(1, 7, 8, "vector"); o_weave(1, 2, 3, "vector")
+        o_quant(1, 4, 8); o_quant(1, 2, 4); o_weave(1, 0, 2, "scalar"); o_quant(1, 0, 2); o_scales(1)

@@ -252,8 +252,8 @@ def tile_adversarialdebiasingprojectedrepresentat_x1_kernel(tc, x, gamma, w, bet
 
         def r2_weave(b, engine):
             live["r2_woven", b] = stage(4 + b % 2)
-            move(engine, live["r2_woven", b][:].rearrange("p (n u e) -> p n u e", u=2, e=2),
-                 live["r2_pairs", b][:].rearrange("p (u n e) -> p n u e", u=2, e=2))
+            move(engine, live["r2_woven", b][:].bitcast(F32).rearrange("p (n u) -> p n u", u=2),
+                 live["r2_pairs", b][:].bitcast(F32).rearrange("p (u n) -> p n u", u=2))
 
         def r2_quant(b):
             quantize(r2q, b % 2, (b // 2) * H, live["r2_woven", b][:])
@@ -390,69 +390,69 @@ def tile_adversarialdebiasingprojectedrepresentat_x1_kernel(tc, x, gamma, w, bet
                               in_=oq[1][32 * quad:32 * quad + 4, h, :].bitcast(I32))
 
 
-        warm_pe(); warm_pe(); load_x(0, 0, 512, 1024); warm_pe(); x_turn(0, 1, 0, 7); x_scale(0, 1, 0)
-        load_x(0, 0, 0, 512); x_turn(0, 0, 0, 6); load_x(0, 1, 0, 512); x_turn(0, 0, 1, 2); load_w(0, 0)
-        x_scale(0, 0, 0); x_scale(0, 0, 1); turn_ab(7); w_weave(0, 0, 2, 4, "scalar"); spread_z(6); z_copy()
-        load_x(0, 1, 512, 1024); load_w(0, 1); x_turn(0, 1, 1, 3); wt_turn(0, 0, 0, 4); ab_copy(); x_scale(0, 1, 1)
-        load_w(1, 1); load_x(1, 1, 0, 1024); load_gamma_rows(); w_weave(0, 0, 0, 2, "vector"); x_quant(0, 0)
-        wt_turn(0, 0, 1, 5); w_quant(0, 0, 0, 2); w_weave(0, 1, 0, 2, "scalar"); wt_copy(0, 0, 1); p_mm(1)
-        x_quant(0, 1); p_mm(0); wt_copy(0, 0, 0); w_quant(0, 1, 0, 2)
+        load_x(0, 0, 0, 512); load_x(0, 0, 512, 1024); load_x(0, 1, 0, 1024); load_w(0, 0); load_w(0, 1); load_w(1, 0)
+        load_w(1, 1); load_x(1, 0, 0, 1024); load_x(1, 1, 0, 1024); load_y(0); load_spread("beta"); load_y(1)
+        load_spread("gamma"); load_gamma_rows(); w_weave(0, 0, 0, 2, "scalar"); warm_pe(); warm_pe(); x_turn(0, 0, 0, 6)
+        warm_pe(); x_turn(0, 1, 0, 7); x_scale(0, 0, 0); x_turn(0, 1, 1, 3); x_scale(0, 1, 0); x_scale(0, 1, 1)
+        x_turn(0, 0, 1, 2); x_scale(0, 0, 1); x_quant(0, 0); wt_turn(0, 0, 0, 4); w_weave(0, 1, 0, 2, "scalar")
+        w_quant(0, 0, 0, 2); wt_turn(0, 0, 1, 5); spread_z(6); x_quant(0, 1); z_copy(); w_quant(0, 1, 0, 2); turn_ab(7)
 
-        s_mm(0); w_weave(0, 1, 2, 4, "scalar"); act(0, "q"); act(0, "sig"); s_mm(1); act(1, "sig"); x_turn(1, 0, 1, 7)
-        w_weave(1, 1, 0, 2, "vector"); wt_turn(0, 1, 1, 5); wt_turn(0, 1, 0, 4); wt_copy(0, 1, 1); w_quant(0, 0, 2, 4)
-        w_weave(1, 1, 2, 4, "vector"); load_x(1, 0, 0, 1024); act(1, "q"); w_quant(0, 1, 2, 4); load_w(1, 0)
-        w_weave(1, 0, 0, 2, "vector"); w_weave(1, 0, 2, 4, "vector"); wt_copy(0, 1, 0); s_mm(2); act(2, "sig")
-        act(2, "q"); load_spread("beta"); w_quant(1, 1, 0, 4); w_quant(1, 0, 0, 4); x_turn(1, 0, 0, 6); x_scale(1, 0, 0)
-        x_turn(1, 1, 1, 5); s_mm(3); x_scale(1, 1, 1); act(3, "q"); act(3, "sig"); square(1, "gpsimd"); x_scale(1, 0, 1)
-        x_turn(1, 1, 0, 4); wt_turn(1, 0, 0, 6); x_scale(1, 1, 0); s_mm(4); load_y(0); n_mm(1); wt_quant(0, 0); s_mm(5)
-        square(2, "scalar"); square(0, "scalar"); x_quant(1, 1); act(4, "sig"); n_mm(0); act(4, "q"); act(5, "sig")
-        act(5, "q"); u_step(1); wt_copy(1, 0, 0); square(5, "scalar"); u_step(0); wt_turn(1, 0, 1, 7); n_scale(1)
-        n_scale(0); s_mm(6); load_y(1); act(6, "sig"); wt_copy(1, 0, 1); x_quant(1, 0); n_mm(3); load_spread("gamma")
-        p_mm(3); s_mm(7); r2_pairs(0, 0); square(3, "gpsimd"); u_step(3); act(7, "sig"); p_mm(2); u_step(2); act(7, "q")
-        n_scale(3); n_mm(2); n_scale(2); r2_pairs(0, 1); r1_turn(0, 0, 6); act(6, "q"); wt_turn(1, 1, 0, 7)
-        square(4, "gpsimd"); r1_copy(0, 0); wt_quant(0, 1); square(6, "scalar"); p_mm(4)
+        s_mm(1); ab_copy(); w_weave(0, 0, 2, 4, "vector"); w_weave(0, 1, 2, 4, "vector"); p_mm(0)
+        w_weave(1, 1, 2, 4, "vector"); wt_copy(0, 0, 1); w_quant(0, 0, 2, 4); wt_copy(0, 0, 0); act(1, "sig"); p_mm(1)
+        w_quant(0, 1, 2, 4); act(1, "q"); s_mm(0); wt_turn(0, 1, 0, 4); act(0, "sig"); x_turn(1, 0, 1, 7)
+        w_weave(1, 1, 0, 2, "vector"); wt_turn(0, 1, 1, 5); s_mm(3); wt_copy(0, 1, 0); x_turn(1, 1, 0, 4)
+        wt_copy(0, 1, 1); w_weave(1, 0, 2, 4, "vector"); act(0, "q"); w_weave(1, 0, 0, 2, "vector"); x_turn(1, 0, 0, 6)
+        wt_quant(0, 0); w_quant(1, 0, 0, 4); x_turn(1, 1, 1, 5); s_mm(2); act(3, "sig"); act(3, "q")
+        w_quant(1, 1, 0, 4); s_mm(5); square(1, "gpsimd"); x_scale(1, 1, 0); square(0, "scalar"); x_scale(1, 0, 0)
+        x_scale(1, 0, 1); act(2, "sig"); x_scale(1, 1, 1); act(2, "q"); n_mm(0); x_quant(1, 0); wt_turn(1, 0, 0, 6)
+        x_quant(1, 1); n_scale(0); s_mm(4); n_mm(1); wt_turn(1, 0, 1, 7); act(5, "sig"); act(5, "q"); s_mm(7)
+        wt_copy(1, 0, 0); u_step(0); p_mm(2); act(4, "q"); act(4, "sig"); s_mm(6); square(2, "scalar"); wt_copy(1, 0, 1)
+        square(3, "gpsimd"); n_scale(1); n_mm(3); u_step(1); wt_turn(1, 1, 0, 7); wt_quant(0, 1); p_mm(3); u_step(2)
+        p_mm(4); n_mm(2); square(4, "scalar"); r2_pairs(0, 0); act(6, "q"); u_step(3); act(7, "q"); r1_turn(0, 0, 6)
+        act(7, "sig"); s_mm(9); act(6, "sig"); s_mm(8); wt_copy(1, 1, 0); n_scale(3); p_mm(5); square(7, "scalar")
+        n_scale(2)
 
-        n_mm(5); n_scale(5); p_mm(5); r2_weave(0, "scalar"); s_mm(9); act(9, "q"); s_mm(8); u_step(4); u_step(5)
-        n_mm(4); act(9, "sig"); r1_turn(0, 1, 6); n_scale(4); p_mm(6); u_step(6); p_mm(7); n_mm(7); square(7, "gpsimd")
-        u_step(7); n_scale(7); square(9, "gpsimd"); wt_copy(1, 1, 0); turn_gamma(7); act(8, "q"); r2_pairs(1, 1)
-        r2_pairs(1, 0); act(8, "sig"); s_mm(11); r1_copy(0, 1); r1_quant(0); r2_quant(0); s_mm(10); n_mm(6)
-        gamma_copy(); wt_turn(1, 1, 1, 7); act(11, "sig"); act(10, "sig"); n_mm(9); n_scale(6); act(10, "q")
-        r1_turn(1, 0, 6); p_mm(9); wt_copy(1, 1, 1); act(11, "q"); p_mm(8); s_mm(13); square(8, "scalar"); s_mm(12)
-        n_mm(8); r1_copy(1, 0); r1_turn(1, 1, 6); u_step(9); r2_weave(1, "scalar"); square(10, "gpsimd"); n_scale(9)
-        u_step(8); p_mm(10); wt_quant(1, 1); n_mm(11); r2_quant(1); act(13, "q"); wt_quant(1, 0); u_step(10)
-        h_mm(0, 7, 1); p_mm(11); act(12, "q"); act(12, "sig"); s_mm(14); n_scale(8); p_mm(12); n_scale(11)
-        square(11, "scalar"); act(13, "sig"); s_mm(15); n_mm(10); r1_copy(1, 1); r1_turn(2, 0, 6); u_step(11); p_mm(13)
-        act(14, "q"); act(14, "sig"); act(15, "sig"); square(13, "gpsimd"); r1_quant(1); act(15, "q"); h_copy(0, 1)
+        n_mm(5); turn_gamma(7); n_mm(4); square(5, "scalar"); u_step(4); act(8, "sig"); r2_pairs(0, 1); u_step(5)
+        r1_copy(0, 0); r2_weave(0, "vector"); wt_quant(1, 0); r1_turn(0, 1, 6); p_mm(7); n_scale(4); p_mm(6); n_scale(5)
+        square(6, "gpsimd"); u_step(7); u_step(6); act(8, "q"); s_mm(10); act(9, "q"); act(9, "sig"); s_mm(11); n_mm(6)
+        r1_copy(0, 1); r1_turn(1, 0, 6); p_mm(9); r2_pairs(1, 0); act(10, "sig"); act(10, "q"); r2_pairs(1, 1); n_mm(7)
+        n_scale(7); gamma_copy(); wt_turn(1, 1, 1, 7); act(11, "sig"); square(9, "gpsimd"); n_scale(6); act(11, "q")
+        square(11, "scalar"); square(8, "scalar"); p_mm(8); u_step(9); s_mm(13); s_mm(12); n_mm(9); n_mm(8)
+        r1_copy(1, 0); r1_turn(1, 1, 6); wt_copy(1, 1, 1); u_step(8); p_mm(10); act(12, "sig"); act(12, "q")
+        r2_quant(0); r1_quant(0); s_mm(14); r2_weave(1, "scalar"); act(13, "sig"); n_scale(9); n_mm(11); r1_copy(1, 1)
+        wt_quant(1, 1); r2_quant(1); h_mm(0, 7, 1); n_scale(8); r1_quant(1); p_mm(11); act(13, "q")
+        square(10, "gpsimd"); u_step(10); act(14, "sig"); h_copy(0, 1); u_step(11); act(14, "q"); s_mm(15); n_scale(11)
+        act(15, "q"); n_mm(10); n_scale(10); act(15, "sig"); r1_turn(2, 0, 6); r1_copy(2, 0); r2_pairs(2, 1)
+        h_mm(1, 7, 1); square(15, "scalar")
 
-        gt_mm(0, 0); square(12, "scalar"); square(14, "scalar"); r2_pairs(2, 0); n_mm(13); gt_mm(0, 1); r2_pairs(2, 1)
-        gt_scale(0, 1); n_scale(10); h_mm(1, 7, 1); h_copy(1, 1); u_step(13); u_step(12); n_mm(12); gt_scale(0, 0)
-        n_scale(13); square(15, "gpsimd"); r1_copy(2, 0); p_mm(15); n_scale(12); h_finish(0, 1); p_mm(14); u_step(14)
-        u_step(15); h_mm(0, 7, 0); r2_weave(2, "scalar"); gt_mm(0, 2); gt_scale(0, 2); gt_mm(0, 3); gt_scale(0, 3)
-        n_mm(14); r1_turn(2, 1, 6); h_scale(0, 0); gt_mm(0, 4); r2_pairs(3, 1); hh_sum(0); r1_copy(2, 1); r2_quant(2)
-        r2_pairs(3, 0); h_mm(1, 7, 0); h_scale(1, 0); invert(0); gt_mm(0, 5); n_scale(14); n_mm(15); n_scale(15)
-        g_turn(0, 0); gh_sum(0, 0); r1_turn(3, 0, 6); gt_scale(0, 4); gt_mm(0, 6); gt_scale(0, 5); r2_weave(3, "scalar")
-        gt_mm(0, 7); r1_quant(2); h_mm(2, 7, 1); r2_quant(3); g_turn(1, 0); gt_scale(0, 6); r1_turn(3, 1, 0)
-        gt_scale(0, 7); g_turn(0, 1); h_scale(2, 1); gh_sum(0, 1); r1_copy(3, 0); r1_copy(3, 1); r1_quant(3)
-        coefficient(0); g_turn(1, 1); h_mm(2, 6, 0); h_scale(2, 0); h_finish(1, 1); hh_sum(1); gh_sum(1, 1)
-        gh_sum(1, 0); invert(1); h_mm(3, 7, 1); h_copy(3, 1); h_finish(3, 1)
+        gt_mm(0, 0); square(13, "scalar"); n_mm(13); square(14, "scalar"); r1_turn(2, 1, 6); gt_mm(0, 1); r1_copy(2, 1)
+        r2_pairs(2, 0); gt_scale(0, 0); gt_scale(0, 1); h_scale(1, 1); n_scale(13); p_mm(13); u_step(13); n_mm(12)
+        p_mm(12); r2_weave(2, "scalar"); square(12, "gpsimd"); u_step(12); h_mm(0, 7, 0); gt_mm(0, 2); h_scale(0, 0)
+        gt_mm(0, 3); h_finish(0, 1); p_mm(15); n_scale(12); h_mm(1, 7, 0); p_mm(14); r2_pairs(3, 0); gt_scale(0, 2)
+        gt_mm(0, 4); n_mm(14); hh_sum(0); gt_scale(0, 3); u_step(14); gt_scale(0, 4); r1_turn(3, 0, 6); r1_copy(3, 0)
+        gt_mm(0, 5); u_step(15); gt_mm(0, 6); n_mm(15); g_turn(0, 0); h_copy(1, 0); h_mm(2, 7, 1); gt_scale(0, 6)
+        gt_scale(0, 5); r1_quant(2); r2_quant(2); r2_pairs(3, 1); r2_weave(3, "scalar"); n_scale(14); gt_mm(0, 7)
+        gt_scale(0, 7); n_scale(15); h_scale(2, 1); r1_turn(3, 1, 0); r1_copy(3, 1); h_finish(1, 0); gh_sum(0, 0)
+        h_mm(2, 6, 0); g_turn(1, 0); r2_quant(3); g_turn(0, 1); r1_quant(3); gh_sum(1, 0); gh_sum(0, 1); invert(0)
+        h_copy(2, 0); hh_sum(1); invert(1); g_turn(1, 1); h_mm(3, 7, 1); h_copy(3, 1)
 
-        gt_mm(1, 1); gt_scale(1, 1); gt_mm(1, 0); h_mm(3, 6, 0); combine(0, 0); gt_mm(1, 3); h_mm(4, 7, 1)
-        coefficient(1); gt_scale(1, 0); h_copy(3, 0); hh_sum(2); h_finish(3, 0); h_mm(4, 6, 0); combine(0, 1)
-        g_turn(2, 0); g_turn(2, 1); h_copy(4, 0); gt_mm(1, 2); gt_scale(1, 3); h_copy(4, 1); gt_scale(1, 2)
-        h_mm(5, 6, 0); combine(1, 0); g_turn(3, 0); combine(1, 1); g_turn(3, 1); gh_sum(2, 0); o_store(1); hh_sum(3)
-        gt_mm(1, 5); gt_scale(1, 5); gt_mm(1, 4); gt_scale(1, 4); invert(2); gh_sum(2, 1); h_mm(5, 7, 1); h_finish(4, 0)
-        h_scale(5, 0); coefficient(2); h_mm(6, 6, 0); gh_sum(3, 1); gh_sum(3, 0); gt_mm(1, 7); h_finish(4, 1); invert(3)
-        gt_mm(1, 6); combine(2, 1); h_copy(5, 1); coefficient(3); combine(2, 0); o_store(2); combine(3, 0)
-        h_mm(6, 7, 1); gt_scale(1, 7); h_scale(6, 0); combine(3, 1); g_turn(4, 0); gt_scale(1, 6); gh_sum(4, 0)
-        g_turn(4, 1); gh_sum(4, 1); h_finish(5, 1); g_turn(5, 0); gh_sum(5, 0); h_mm(7, 6, 0); h_copy(6, 1)
-        h_finish(6, 1); hh_sum(4); h_copy(7, 0); h_finish(7, 0); invert(4); g_turn(5, 1); g_turn(6, 0); gh_sum(5, 1)
-        o_store(0); coefficient(4); gh_sum(6, 0); hh_sum(5); invert(5); h_mm(7, 7, 1); h_copy(7, 1); combine(4, 0)
-        h_finish(7, 1); combine(4, 1); coefficient(5); o_store(4); g_turn(6, 1); gh_sum(6, 1); g_turn(7, 0); hh_sum(6)
-        combine(5, 1)
+        gt_mm(1, 1); gh_sum(1, 1); coefficient(0); gt_scale(1, 1); h_mm(3, 6, 0); h_copy(3, 0); coefficient(1)
+        gt_mm(1, 0); h_finish(2, 0); h_mm(4, 7, 1); combine(0, 1); combine(1, 1); combine(0, 0); gt_mm(1, 3); hh_sum(2)
+        h_mm(4, 6, 0); h_finish(3, 1); gt_scale(1, 0); g_turn(2, 1); g_turn(3, 1); combine(1, 0); g_turn(2, 0)
+        gh_sum(2, 1); gh_sum(2, 0); invert(2); h_copy(4, 1); gt_mm(1, 2); h_copy(4, 0); gt_scale(1, 3); gh_sum(3, 1)
+        g_turn(3, 0); h_finish(3, 0); gh_sum(3, 0); gt_scale(1, 2); h_mm(5, 6, 0); h_scale(5, 0); gt_mm(1, 5)
+        gt_mm(1, 4); h_mm(5, 7, 1); hh_sum(3); invert(3); h_finish(4, 1); coefficient(2); coefficient(3); combine(2, 0)
+        h_mm(6, 6, 0); gt_scale(1, 5); gt_mm(1, 7); gt_scale(1, 4); gt_mm(1, 6); combine(2, 1); h_copy(5, 1)
+        h_finish(4, 0); h_mm(6, 7, 1); gt_scale(1, 7); combine(3, 0); gt_scale(1, 6); combine(3, 1); g_turn(4, 0)
+        g_turn(5, 0); g_turn(4, 1); h_scale(6, 1); h_mm(7, 7, 1); h_copy(6, 0); gh_sum(4, 0); o_store(3); gh_sum(4, 1)
+        gh_sum(5, 0); g_turn(5, 1); hh_sum(4); h_finish(5, 1); o_store(1); g_turn(6, 0); invert(4); h_mm(7, 6, 0)
+        h_copy(7, 1); o_store(0); hh_sum(5); h_finish(6, 0); h_copy(7, 0); gh_sum(5, 1); hh_sum(6); coefficient(4)
+        g_turn(6, 1); h_finish(7, 1); gh_sum(6, 0); invert(5); combine(4, 1); gh_sum(6, 1); h_finish(7, 0); o_store(2)
+        coefficient(5); invert(6); g_turn(7, 1)
 
-        o_weave(0, 4, 6, "scalar"); invert(6); g_turn(7, 1); gh_sum(7, 0); gh_sum(7, 1); o_store(3); combine(5, 0)
-        hh_sum(7); invert(7); o_weave(0, 2, 4, "scalar"); o_weave(0, 6, 8, "gpsimd"); coefficient(6); coefficient(7)
-        combine(6, 1); combine(7, 1); o_weave(0, 0, 2, "scalar"); o_weave(1, 4, 6, "scalar"); o_store(5); combine(7, 0)
-        o_weave(1, 6, 7, "scalar"); o_store(7); combine(6, 0); o_store(6); o_quant(0, 4, 8); o_quant(0, 0, 4)
-        o_weave(1, 3, 4, "vector"); o_scales(0); o_weave(1, 7, 8, "vector"); o_weave(1, 2, 3, "vector")
-        o_quant(1, 4, 8); o_quant(1, 2, 4); o_weave(1, 0, 2, "scalar"); o_quant(1, 0, 2); o_scales(1)
+        o_weave(0, 0, 2, "gpsimd"); o_weave(0, 2, 4, "scalar"); combine(4, 0); o_store(4); g_turn(7, 0); combine(5, 1)
+        o_weave(0, 4, 6, "scalar"); hh_sum(7); coefficient(6); combine(5, 0); o_store(5); combine(6, 0); combine(6, 1)
+        o_store(6); gh_sum(7, 1); gh_sum(7, 0); invert(7); o_quant(0, 0, 4); coefficient(7); o_weave(0, 6, 8, "scalar")
+        o_quant(0, 4, 8); o_scales(0); combine(7, 1); combine(7, 0); o_weave(1, 6, 8, "vector")
+        o_weave(1, 0, 3, "vector"); o_store(7); o_weave(1, 4, 6, "scalar"); o_quant(1, 4, 8); o_weave(1, 3, 4, "scalar")
+        o_quant(1, 0, 4); o_scales(1)

@@ -3,456 +3,508 @@ from contextlib import ExitStack
 import concourse.mybir as mybir
 from concourse.masks import make_identity
 
+N, D, C = 1024, 1024, 1024
+FLOPS = 3 * 2 * N * D * C
+
 F32 = mybir.dt.float32
 BF16 = mybir.dt.bfloat16
 U32 = mybir.dt.uint32
 I32 = mybir.dt.int32
 U8 = mybir.dt.uint8
 FP8X4 = mybir.dt.float8_e4m3fn_x4
-ALU = mybir.AluOpType
 ACT = mybir.ActivationFunctionType
+ALU = mybir.AluOpType
 
 P = 128
-W = 1024
-H = 512
-FLOPS = 3 * 2 * W * W * W
-
-G_BANKS = [2, 4, 2, 4, 2, 4, 0, 2]
-GT_SLOTS = [0, 2, 1, 3]
-H_TILES = 4
+PACK = 4
+GROUP = P * PACK
+GROUPS = 2
+EPS = 1e-6
 
 
-def tile_adversarialdebiasingprojectedrepresentat_x1_kernel(tc, x, gamma, w, beta, y, z, a, out_0, out_1, out_2):
+def tile_adversarialdebiasingprojectedrepresentat_x1_kernel(
+    tc, x, gamma, w, beta, y, z, a, out_0, out_1, out_2
+):
     nc = tc.nc
     with ExitStack() as ctx:
-        sb = ctx.enter_context(tc.tile_pool(name="sb", bufs=1))
-        ps = ctx.enter_context(tc.psum_pool(name="ps", bufs=1))
+        const = ctx.enter_context(tc.tile_pool(name="const", bufs=1))
+        raw = ctx.enter_context(tc.tile_pool(name="raw", bufs=1))
+        mx = ctx.enter_context(tc.tile_pool(name="mx", bufs=1))
+        work = ctx.enter_context(tc.tile_pool(name="work", bufs=1))
+        small = ctx.enter_context(tc.tile_pool(name="small", bufs=4))
+        psum = ctx.enter_context(tc.psum_pool(name="psum", bufs=1))
+
         ctx.enter_context(tc.manual_schedule())
 
-        def bank(n, dtype=F32):
-            return ps.tile([P, H if dtype is F32 else W], dtype, name="bank%d" % n, tag="bank%d" % n)
+        def bank(i):
+            return psum.tile([P, GROUP], F32, tag="bank%d" % i, name="bank%d" % i)
 
-        def stage(n):
-            return sb.tile([P, 4 * H], BF16, name="stage%d" % n, tag="stage%d" % n, align_bytes=64)
+        def load_rows(src, rg, cg, tag, bufs):
+            rows = raw.tile([P, PACK, GROUP], BF16, tag=tag, name=tag, bufs=bufs)
+            view = src[rg * GROUP : (rg + 1) * GROUP, cg * GROUP : (cg + 1) * GROUP]
+            nc.sync.dma_start(out=rows[:], in_=view.rearrange("(p t) c -> p t c", t=PACK))
+            return rows
 
-        def slot(n):
-            return sb.tile([P, 4, H], F32, name="slot%d" % n, tag="slot%d" % n)
+        def load_slots(vec, name):
+            slots = const.tile([P, GROUPS, PACK], BF16, name=name)
+            nc.scalar.dma_start(out=slots[:], in_=vec.rearrange("(g p t) -> p g t", g=GROUPS, t=PACK))
+            return slots
 
-        def operand(name):
-            codes = sb.tile([P, 2, W], U32, name=name + "_codes", align_bytes=64)
-            scales = sb.tile([P, 2, W], U8, name=name + "_scales", align_bytes=64)
+        gamma_s = load_slots(gamma, "gamma_s")
+        beta_s = load_slots(beta, "beta_s")
+        a_s = load_slots(a, "a_s")
+        w_rows, x_rows, y_rows = {}, {}, {}
+        for dg in range(GROUPS):
+            x_rows[0, dg] = load_rows(x, 0, dg, "xy_rows", 6)
+            w_rows[dg, 0] = load_rows(w, dg, 0, "w_rows", 4)
+        y_rows[0, 0] = load_rows(y, 0, 0, "xy_rows", 6)
+        z_all = const.tile([P, N], BF16, name="z_all")
+        nc.sync.dma_start(out=z_all[:], in_=z.partition_broadcast(P))
+        for dg in range(GROUPS):
+            w_rows[dg, 1] = load_rows(w, dg, 1, "w_rows", 4)
+        for dg in range(GROUPS):
+            x_rows[1, dg] = load_rows(x, 1, dg, "xy_rows", 6)
+        y_rows[0, 1] = load_rows(y, 0, 1, "xy_rows", 6)
+        gamma_all = const.tile([P, D], BF16, name="gamma_all")
+        nc.sync.dma_start(out=gamma_all[:], in_=gamma.partition_broadcast(P))
+
+        ident = const.tile([P, P], F32)
+        make_identity(nc, ident[:])
+
+        gamma_f = const.tile([P, GROUPS, PACK], F32)
+        beta_f = const.tile([P, GROUPS, PACK], F32)
+        a_f = const.tile([P, GROUPS, PACK], F32)
+        ab_f = const.tile([P, GROUPS, PACK], F32)
+        neg_ab_f = const.tile([P, GROUPS, PACK], F32)
+        nc.vector.tensor_copy(out=gamma_f[:], in_=gamma_s[:])
+        nc.vector.tensor_copy(out=beta_f[:], in_=beta_s[:])
+        nc.vector.tensor_copy(out=a_f[:], in_=a_s[:])
+        nc.vector.tensor_tensor(out=ab_f[:], in0=a_s[:], in1=beta_s[:], op=ALU.mult)
+        nc.vector.tensor_scalar(out=neg_ab_f[:], in0=ab_f[:], scalar1=-1.0, scalar2=None, op0=ALU.mult)
+
+        def stage_tile():
+            return work.tile([P, GROUP * PACK], BF16, tag="stage", name="stage", bufs=4, align_bytes=64)
+
+        def quantize(stage, name):
+            codes = mx.tile([P, GROUP], U32, name=name + "_codes", align_bytes=64)
+            scales = mx.tile([P, GROUP], U8, name=name + "_scales", align_bytes=64)
+            nc.vector.quantize_mx(out=codes[:].bitcast(FP8X4), scales=scales[:], in_=stage[:])
             return codes, scales
 
-        def quantize(op, g, first, src):
-            n = src.shape[1] // 4
-            nc.vector.quantize_mx(out=op[0][:, g, first:first + n].bitcast(FP8X4), scales=op[1][:, g, first:first + n], in_=src)
+        def mx_pass(acc, lhs, t, rhs, g):
+            cols = slice(t * P, (t + 1) * P)
+            nc.tensor.matmul_mx(
+                out=acc[:],
+                lhsT=lhs[0][:, cols].bitcast(FP8X4),
+                lhsT_scale=lhs[1][:, cols],
+                rhs=rhs[0][:].bitcast(FP8X4),
+                rhs_scale=rhs[1][:],
+                start=(g == 0),
+                stop=(g == GROUPS - 1),
+            )
 
-        def mx(out, lhs, l0, rhs, r0):
-            for g in range(2):
-                nc.tensor.matmul_mx(
-                    out=out,
-                    lhsT=lhs[0][:, g, l0:l0 + P].bitcast(FP8X4), lhsT_scale=lhs[1][:, g, l0:l0 + P],
-                    rhs=rhs[0][:, g, r0:r0 + H].bitcast(FP8X4), rhs_scale=rhs[1][:, g, r0:r0 + H],
-                    start=(g == 0), stop=(g == 1))
+        opened = {}
 
-        def move(engine, dst, src):
-            if engine == "vector":
-                nc.vector.tensor_copy(out=dst, in_=src)
-            elif engine == "scalar":
-                nc.scalar.copy(out=dst, in_=src)
-            else:
-                nc.gpsimd.tensor_scalar(out=dst, in0=src, scalar1=1.0, scalar2=0.0, op0=ALU.mult, op1=ALU.add)
-
-        vec = {}
-        for name in ("gamma", "z", "beta", "a"):
-            vec[name] = sb.tile([P, 2, 4], BF16, name="vec_" + name)
-        for name, src in (("gamma", gamma), ("z", z), ("beta", beta), ("a", a)):
-            nc.scalar.dma_start(out=vec[name][:], in_=src.rearrange("(g p t) -> p g t", g=2, t=4))
-        x_raw = sb.tile([P, 8, W], BF16, name="x_raw", tag="big0")
-        w_raw = sb.tile([P, 4, 4, H], BF16, name="w_raw", tag="big1")
-        y_raw = sb.tile([P, 8, W], BF16, name="y_raw")
-        beta_b = sb.tile([P, W], BF16, name="beta_b")
-        gamma_b = sb.tile([P, W], BF16, name="gamma_b")
-
-        def rows(src, h):
-            return src[h * H:(h + 1) * H, :].rearrange("(p t) d -> p t d", t=4)
-
-        def load_x(h, tp, c0, c1):
-            nc.sync.dma_start(out=x_raw[:, 4 * h + 2 * tp:4 * h + 2 * tp + 2, c0:c1], in_=rows(x, h)[:, 2 * tp:2 * tp + 2, c0:c1])
-
-        def load_w(g, gd):
-            nc.sync.dma_start(out=w_raw[:, 2 * g + gd, :, :], in_=rows(w, gd)[:, :, g * H:(g + 1) * H])
-
-        def load_y(h):
-            nc.sync.dma_start(out=y_raw[:, 4 * h:4 * h + 4, :], in_=rows(y, h))
-
-        def load_spread(name):
-            dst, src = {"beta": (beta_b, beta), "gamma": (gamma_b, gamma)}[name]
-            nc.sync.dma_start(out=dst[:], in_=src.partition_broadcast(P))
-
-        ident_f = sb.tile([P, P], F32, name="ident_f")
-        ident_b = sb.tile([P, P], BF16, name="ident_b")
-        neg_ident = sb.tile([P, P], BF16, name="neg_ident")
-        ab_cols = sb.tile([P, 8, P], BF16, name="ab_cols")
-        zeros = sb.tile([P, H], BF16, name="zeros")
-        nc.vector.memset(zeros[:], 0.0)
-        make_identity(nc, ident_f[:])
-        make_identity(nc, ident_b[:])
-        nc.gpsimd.memset(ab_cols[:], 0.0)
-        nc.gpsimd.tensor_scalar(out=neg_ident[:], in0=ident_b[:], scalar1=-1.0, scalar2=0.0, op0=ALU.mult, op1=ALU.add)
-        warm = sb.tile([P, 1], F32, name="warm")
-        nc.scalar.activation(out=warm[:], in_=ident_f[:, 0:1], func=ACT.Sigmoid)
-
-        def col8(name):
-            return vec[name][:].rearrange("p g t -> p (g t)")
-
-        gamma_f = sb.tile([P, 8], F32, name="gamma_f")
-        beta_f = sb.tile([P, 8], F32, name="beta_f")
-        ab = sb.tile([P, 8], F32, name="ab")
-        neg_a = sb.tile([P, 8], F32, name="neg_a")
-        neg_aab = sb.tile([P, 8], F32, name="neg_aab")
-        nc.gpsimd.tensor_tensor(out=ab[:], in0=col8("a"), in1=col8("beta"), op=ALU.mult)
-        nc.gpsimd.tensor_copy(out=ab_cols[:, :, 0], in_=ab[:])
-        nc.gpsimd.tensor_tensor(out=ab_cols[:, :, 1], in0=ab[:], in1=ab_cols[:, :, 0], op=ALU.subtract)
-        nc.gpsimd.tensor_copy(out=beta_f[:], in_=col8("beta"))
-        nc.gpsimd.tensor_scalar(out=neg_a[:], in0=col8("a"), scalar1=-1.0, scalar2=0.0, op0=ALU.mult, op1=ALU.add)
-        nc.gpsimd.tensor_tensor(out=neg_aab[:], in0=neg_a[:], in1=ab[:], op=ALU.mult)
-        gamma_rows = sb.tile([P, P], BF16, name="gamma_rows")
-        nc.gpsimd.memset(gamma_rows[:], 0.0)
-
-        def load_gamma_rows():
-            nc.sync.dma_start(out=gamma_rows[0:8, :], in_=gamma.rearrange("(j p) -> j p", j=8))
-
-        live = {}
-        z_rows = sb.tile([P, W], BF16, name="z_rows")
-        ab_rows = sb.tile([P, W], BF16, name="ab_rows")
-
-        def warm_pe():
-            for n in range(2):
-                b = bank(n)
-                nc.tensor.matmul(b[:], lhsT=zeros[:, 0:P], rhs=zeros[:], start=True, stop=True)
-
-        def turn_gamma(n):
-            live["gamma_bank"] = bank(n, BF16)
-            nc.tensor.transpose(live["gamma_bank"][:, 0:P], gamma_rows[:], ident_b[:])
-
-        def gamma_copy():
-            nc.scalar.copy(out=gamma_f[:], in_=live["gamma_bank"][:, 0:8])
-
-        def spread_z(n):
-            live["z_bank"] = bank(n, BF16)
-            for i in range(8):
-                nc.tensor.transpose(live["z_bank"][:, i * P:(i + 1) * P], col8("z")[:, i:i + 1].to_broadcast([P, P]), ident_b[:])
-
-        def z_copy():
-            nc.scalar.copy(out=z_rows[:], in_=live["z_bank"][:])
-
-        def turn_ab(n):
-            live["ab_bank"] = bank(n, BF16)
-            for col in range(8):
-                nc.tensor.transpose(live["ab_bank"][:, col * P:(col + 1) * P], ab_cols[:, col, :], ident_b[:])
-
-        def ab_copy():
-            nc.scalar.copy(out=ab_rows[:], in_=live["ab_bank"][:])
-
-        xq, wq, wtq, r1q, r2q, oq = [operand(name) for name in ("xq", "wq", "wtq", "r1q", "r2q", "oq")]
-
-        def turn_words(n, words):
-            b = bank(n)
+        def transpose_half(rows, half, acc):
             for u in range(2):
-                for v in range(2):
-                    nc.tensor.transpose(b[:, (2 * u + v) * P:(2 * u + v + 1) * P], words(u, v), ident_f[:])
-            return b
+                for tt in range(2):
+                    words = rows[:, 2 * half + tt, :].bitcast(F32)
+                    col = (2 * u + tt) * P
+                    nc.tensor.transpose(acc[:, col : col + P], words[:, u::2], ident[:])
 
-        def x_turn(h, gd, tp, n):
-            live["x_bank", h, gd, tp] = turn_words(
-                n, lambda u, v: x_raw[:, 4 * h + 2 * tp + v, :].bitcast(F32)[:, 256 * gd + u:256 * gd + 256:2])
+        w_q, x_q, wt_q, r1_q, r2_q = {}, {}, {}, {}, {}
+        staged = {}
 
-        def x_scale(h, gd, tp):
-            if ("x_woven", h, gd) not in live:
-                live["x_woven", h, gd] = stage(1 + gd - h)
+        def sort_w(dg, cg, copy, slots):
+            if ("w", dg, cg) not in staged:
+                staged["w", dg, cg] = stage_tile()
+            stage = staged["w", dg, cg]
+            copy(
+                out=stage[:].rearrange("p (t m j) -> p t m j", t=PACK, j=PACK)[:, slots],
+                in_=w_rows[dg, cg][:].rearrange("p j (m t) -> p t m j", t=PACK)[:, slots],
+            )
+
+        def quant_w(dg, cg):
+            w_q[dg, cg] = quantize(staged["w", dg, cg], "w%d%d" % (dg, cg))
+
+        def turn_x(ng, dg):
+            stage = stage_tile()
+            staged["x", ng, dg] = stage
+            for half in range(2):
+                acc = bank(4 + 2 * dg + half)
+                transpose_half(x_rows[ng, dg], half, acc)
+                nc.vector.tensor_tensor(
+                    out=stage[:, half * 1024 : (half + 1) * 1024].rearrange("p (n u e) -> p n u e", u=2, e=2),
+                    in0=acc[:].bitcast(BF16).rearrange("p (u n e) -> p n u e", u=2, e=2),
+                    in1=gamma_s[:, dg, :].rearrange("p (u e) -> p u e", e=2).unsqueeze(1).to_broadcast([P, 256, 2, 2]),
+                    op=ALU.mult,
+                )
+
+        def quant_x(ng, dg):
+            x_q[ng, dg] = quantize(staged["x", ng, dg], "x%d%d" % (ng, dg))
+
+        def turn_w(cg, dg):
+            stage = stage_tile()
+            staged["wt", cg, dg] = stage
+            for half in range(2):
+                acc = bank(4 + 2 * dg + half)
+                transpose_half(w_rows[dg, cg], half, acc)
+                nc.scalar.copy(
+                    out=stage[:, half * 1024 : (half + 1) * 1024].bitcast(F32).rearrange("p (n u) -> p n u", u=2),
+                    in_=acc[:].rearrange("p (u n) -> p n u", u=2),
+                )
+
+        def quant_wt(cg, dg):
+            wt_q[cg, dg] = quantize(staged["wt", cg, dg], "wt%d%d" % (cg, dg))
+
+        act_out, y_turned, slopes, resid = {}, {}, {}, {}
+        pending = []
+
+        def flush_slope():
+            ng, cg, t, qq = pending.pop()
+            if t == 0:
+                slopes[ng, cg] = work.tile([P, PACK, GROUP], F32, tag="slope", name="slope", bufs=2)
+            nc.scalar.activation(
+                out=slopes[ng, cg][:, t, :], in_=qq[:], func=ACT.Identity,
+                scale=neg_ab_f[:, cg, t : t + 1], bias=ab_f[:, cg, t : t + 1],
+            )
+
+        def turn_y(ng, cg, u):
+            y_t = bank(2 + u)
+            y_turned[ng, cg, u] = y_t
+            for tn in range(PACK):
+                words = y_rows[ng, cg][:, tn, :].bitcast(F32)
+                nc.tensor.transpose(y_t[:, tn * P : (tn + 1) * P], words[:, u::2], ident[:])
+
+        def score(ng, cg, t):
+            acc = bank(t % 2)
+            for dg in range(GROUPS):
+                mx_pass(acc, w_q[dg, cg], t, x_q[ng, dg], dg)
+            sig = work.tile([P, GROUP], F32, tag="sig", name="sig", bufs=4)
+            q = work.tile([P, GROUP], F32, tag="q", name="q", bufs=4)
+            qq = work.tile([P, GROUP], F32, tag="qq", name="qq", bufs=2)
+            beta_t = beta_f[:, cg, t : t + 1]
+            nc.scalar.activation(out=sig[:], in_=acc[:], func=ACT.Sigmoid, scale=beta_t)
+            nc.scalar.activation(out=q[:], in_=acc[:], func=ACT.Tanh, scale=beta_t)
+            if pending:
+                flush_slope()
+            nc.scalar.activation(out=qq[:], in_=q[:], func=ACT.Square)
+            pending.append((ng, cg, t, qq))
+            act_out[ng, cg, t] = (sig, q)
+
+        def residuals(ng, cg, t):
+            if t == 0:
+                r1_new = work.tile([P, PACK, GROUP], F32, tag="r1", name="r1")
+                lin_new = work.tile([P, PACK, GROUP], F32, tag="lin", name="lin")
+                resid[ng, cg] = (r1_new, lin_new)
+            r1, lin = resid[ng, cg]
+            sig, q = act_out[ng, cg, t]
+            y_t = y_turned[ng, cg, t // 2]
+            nc.vector.tensor_tensor(out=r1[:, t, :], in0=sig[:], in1=y_t[:].bitcast(BF16)[:, t % 2 :: 2], op=ALU.subtract)
+            nc.vector.scalar_tensor_tensor(
+                out=lin[:, t, :], in0=q[:], scalar=a_f[:, cg, t : t + 1],
+                in1=z_cols[:, ng * GROUP : (ng + 1) * GROUP], op0=ALU.mult, op1=ALU.subtract,
+            )
+
+        def pairs_out(stage_ap):
+            return stage_ap.rearrange("p (c i t) -> p c t i", i=2, t=PACK)
+
+        def pairs_in(src):
+            return src.rearrange("p t (c i) -> p c t i", i=2)
+
+        def final_r1(ng, cg):
+            stage = stage_tile()
+            staged["r1", ng, cg] = stage
             nc.vector.tensor_tensor(
-                out=live["x_woven", h, gd][:, tp * W:(tp + 1) * W].rearrange("p (n u e) -> p n u e", u=2, e=2),
-                in0=live["x_bank", h, gd, tp][:].bitcast(BF16).rearrange("p (u n e) -> p n u e", u=2, e=2),
-                in1=vec["gamma"][:, gd, :].rearrange("p (u e) -> p u e", u=2).unsqueeze(1).to_broadcast([P, 256, 2, 2]),
-                op=ALU.mult)
+                out=pairs_out(stage[:]), in0=pairs_in(resid[ng, cg][0][:]),
+                in1=beta_f[:, cg, :].unsqueeze(1).unsqueeze(3).to_broadcast([P, GROUP // 2, PACK, 2]),
+                op=ALU.mult,
+            )
 
-        def x_quant(h, gd):
-            quantize(xq, gd, h * H, live["x_woven", h, gd][:])
-
-        def w_weave(g, gd, t0, t1, engine):
-            if ("w_woven", g, gd) not in live:
-                live["w_woven", g, gd] = stage(6 + gd if g else 3 * gd)
-            dst = live["w_woven", g, gd][:].rearrange("p (t m j) -> p t m j", t=4, j=4)[:, t0:t1]
-            src = w_raw[:, 2 * g + gd, :, :].rearrange("p j (m t) -> p t m j", t=4)[:, t0:t1]
-            move(engine, dst, src)
-
-        def w_quant(g, gd, t0, t1):
-            quantize(wq, gd, g * H + t0 * P, live["w_woven", g, gd][:, t0 * H:t1 * H])
-
-        def wt_turn(g, gd, jp, n):
-            live["wt_bank", g, gd, jp] = turn_words(n, lambda u, v: w_raw[:, 2 * g + gd, 2 * jp + v, :].bitcast(F32)[:, u:256:2])
-
-        def wt_copy(g, gd, jp):
-            if ("wt_woven", g, gd) not in live:
-                live["wt_woven", g, gd] = stage(4 - 2 * g + gd)
-            words = live["wt_woven", g, gd][:].bitcast(F32).rearrange("p (m j u) -> p m j u", j=4, u=2)
-            nc.scalar.copy(out=words[:, :, 2 * jp:2 * jp + 2, :],
-                           in_=live["wt_bank", g, gd, jp][:].rearrange("p (u j m) -> p m j u", u=2, j=2))
-
-        def wt_quant(g, gd):
-            quantize(wtq, g, gd * H, live["wt_woven", g, gd][:])
-
-        def unit(s):
-            return s // 8, (s // 4) % 2, s % 4
-
-        def s_mm(s):
-            h, g, t = unit(s)
-            live["s_bank", s] = bank(s % 2)
-            mx(live["s_bank", s][:], wq, g * H + t * P, xq, h * H)
-
-        def act(s, name):
-            h, g, t = unit(s)
-            b = s // 4
-            if (name, b) not in live:
-                live[name, b] = slot(3 * (b % 2) + (0 if name == "q" else 1))
-            nc.scalar.activation(out=live[name, b][:, t, :], in_=live["s_bank", s][:],
-                                 func=ACT.Tanh if name == "q" else ACT.Sigmoid, scale=beta_f[:, 4 * g + t:4 * g + t + 1])
-
-        def square(s, engine):
-            b, t = divmod(s, 4)
-            if ("qq", b) not in live:
-                live["qq", b] = slot(3 * (b % 2) + 2)
-            q = live["q", b][:, t, :]
-            if engine == "scalar":
-                nc.scalar.activation(out=live["qq", b][:, t, :], in_=q, func=ACT.Square)
-            else:
-                nc.gpsimd.tensor_tensor(out=live["qq", b][:, t, :], in0=q, in1=q, op=ALU.mult)
-
-        def p_mm(s):
-            h, g, t = unit(s)
-            live["p_bank", s] = bank(2 + s % 2)
-            col = 4 * g + t
-            nc.tensor.matmul(live["p_bank", s][:], lhsT=ab_rows[:, col * P:(col + 1) * P], rhs=z_rows[:, h * H:(h + 1) * H],
-                             start=True, stop=True)
-
-        def u_step(s):
-            h, g, t = unit(s)
-            q = live["q", s // 4][:, t, :]
-            nc.vector.scalar_tensor_tensor(out=q, in0=q, scalar=neg_aab[:, 4 * g + t:4 * g + t + 1], in1=live["p_bank", s][:],
-                                           op0=ALU.mult, op1=ALU.add)
-
-        def r2_pairs(b, u):
-            if ("r2_pairs", b) not in live:
-                live["r2_pairs", b] = stage(8)
-            nc.vector.scalar_tensor_tensor(
-                out=live["r2_pairs", b][:, u * W:(u + 1) * W].rearrange("p (n e) -> p n e", e=2),
-                in0=live["qq", b][:, 2 * u:2 * u + 2, :].rearrange("p e n -> p n e"), scalar=1.0,
-                in1=live["q", b][:, 2 * u:2 * u + 2, :].rearrange("p e n -> p n e"), op0=ALU.subtract, op1=ALU.mult)
-
-        def r2_weave(b, engine):
-            live["r2_woven", b] = stage(4 + b % 2)
-            move(engine, live["r2_woven", b][:].bitcast(F32).rearrange("p (n u) -> p n u", u=2),
-                 live["r2_pairs", b][:].bitcast(F32).rearrange("p (u n) -> p n u", u=2))
-
-        def r2_quant(b):
-            quantize(r2q, b % 2, (b // 2) * H, live["r2_woven", b][:])
-
-        def n_mm(r):
-            h, g, tn = unit(r)
-            b = bank(4 + r % 2)
-            live["n_bank", r] = b
-            nc.tensor.matmul(b[:].rearrange("p (t m) -> p t m", t=4), lhsT=neg_ident[:],
-                             rhs=y_raw[:, 4 * h + tn, g * H:(g + 1) * H].rearrange("p (m t) -> p t m", t=4), start=True, stop=False)
-            for t in range(4):
-                nc.tensor.matmul(b[:, t * P:(t + 1) * P], lhsT=live["sig", r // 4][:, t, tn * P:(tn + 1) * P], rhs=ident_f[:],
-                                 start=False, stop=(t == 3), is_transpose=True)
-
-        def n_scale(r):
-            h, g, tn = unit(r)
-            live["r1_rows", r] = sb.tile([P, H], BF16, name="r1n%d" % tn, tag="r1n%d" % tn)
+        def final_r2(ng, cg):
+            stage = stage_tile()
+            staged["r2", ng, cg] = stage
             nc.vector.tensor_tensor(
-                out=live["r1_rows", r][:].rearrange("p (u m e) -> p u m e", u=2, e=2),
-                in0=live["n_bank", r][:].rearrange("p (u e m) -> p u m e", u=2, e=2),
-                in1=beta_b[:, g * H:(g + 1) * H].rearrange("p (m u e) -> p u m e", u=2, e=2), op=ALU.mult)
+                out=pairs_out(stage[:]), in0=pairs_in(resid[ng, cg][1][:]), in1=pairs_in(slopes[ng, cg][:]), op=ALU.mult
+            )
 
-        def r1_turn(b, tp, n):
-            live["r1_bank", b, tp] = turn_words(
-                n, lambda u, v: live["r1_rows", 4 * b + 2 * tp + v][:].bitcast(F32)[:, u * P:(u + 1) * P])
+        def quant_r1(ng, cg):
+            r1_q[ng, cg] = quantize(staged["r1", ng, cg], "r1_%d%d" % (ng, cg))
 
-        def r1_copy(b, tp):
-            if ("r1_woven", b) not in live:
-                live["r1_woven", b] = stage(6 + b % 2)
-            words = live["r1_woven", b][:].bitcast(F32)[:, tp * H:(tp + 1) * H]
-            nc.scalar.copy(out=words.rearrange("p (n u) -> p n u", u=2),
-                           in_=live["r1_bank", b, tp][:].rearrange("p (u n) -> p n u", u=2))
+        def quant_r2(ng, cg):
+            r2_q[ng, cg] = quantize(staged["r2", ng, cg], "r2_%d%d" % (ng, cg))
 
-        def r1_quant(b):
-            quantize(r1q, b % 2, (b // 2) * H, live["r1_woven", b][:])
+        g_t, h_rows, hh_sum, hh_inv, g_rows, coefs, result, out_q = {}, {}, {}, {}, {}, {}, {}, {}
 
-        def gt_mm(h, jd):
-            live["gt_bank", h, jd] = bank(jd % 2)
-            mx(live["gt_bank", h, jd][:], wtq, jd * P, r1q, h * H)
+        def open_g(ng, dg, j):
+            acc = bank((4 if ng == 0 else 0) + j)
+            mx_pass(acc, wt_q[0, dg], j, r1_q[ng, 0], 0)
+            opened["g", ng, dg, j] = acc
 
-        def gt_scale(h, jd):
-            gd, j = divmod(jd, 4)
-            if ("gt", h, gd) not in live:
-                live["gt", h, gd] = slot(GT_SLOTS[2 * h + gd])
-            nc.scalar.activation(out=live["gt", h, gd][:, j, :], in_=live["gt_bank", h, jd][:], func=ACT.Copy,
-                                 scale=gamma_f[:, jd:jd + 1])
+        def open_h(ng, t, dg, first_bank):
+            acc = bank(first_bank + dg)
+            mx_pass(acc, r2_q[ng, 0], t, wt_q[0, dg], 0)
+            opened["h", ng, t, dg] = acc
 
-        def g_turn(i, gd):
-            h, tn = divmod(i, 4)
-            b = bank(G_BANKS[i] + gd)
-            live["g_bank", i, gd] = b
-            for j in range(4):
-                nc.tensor.transpose(b[:, j * P:(j + 1) * P], live["gt", h, gd][:, j, tn * P:(tn + 1) * P], ident_f[:])
+        def make_g(ng, dg):
+            for j in range(PACK):
+                if ("g", ng, dg, j) not in opened:
+                    open_g(ng, dg, j)
+                acc = opened["g", ng, dg, j]
+                mx_pass(acc, wt_q[1, dg], j, r1_q[ng, 1], 1)
+                g_dj = work.tile([P, GROUP], F32, tag="g_t", name="g_t", bufs=8)
+                nc.scalar.activation(out=g_dj[:], in_=acc[:], func=ACT.Copy, scale=gamma_f[:, dg, j : j + 1])
+                g_t[ng, dg, j] = g_dj
 
-        def h_mm(i, n, gd):
-            live["h_bank", i, gd] = bank(n)
-            mx(live["h_bank", i, gd][:], r2q, i * P, wtq, gd * H)
+        def natural(acc):
+            return acc[:].rearrange("p (j m) -> p m j", j=PACK)
 
-        h_rows = [sb.tile([P, W + 8], F32, name="h_rows%d" % n) for n in range(H_TILES)]
-        for tile in h_rows:
-            nc.gpsimd.tensor_scalar(out=tile[:, W:W + 1], in0=ident_f[:, 0:1], scalar1=0.0, scalar2=1e-3, op0=ALU.mult, op1=ALU.add)
+        def split(row_ap):
+            return row_ap.rearrange("p (m j) -> p m j", j=PACK)
 
-        def h_cols(i, gd):
-            return h_rows[i % H_TILES][:, gd * H:(gd + 1) * H]
+        def make_h(ng, t, first_bank):
+            h = work.tile([P, D], F32, tag="h", name="h", bufs=4)
+            for dg in range(GROUPS):
+                if ("h", ng, t, dg) not in opened:
+                    open_h(ng, t, dg, first_bank)
+                acc = opened["h", ng, t, dg]
+                mx_pass(acc, r2_q[ng, 1], t, wt_q[1, dg], 1)
+                cols = slice(dg * GROUP, (dg + 1) * GROUP)
+                nc.vector.tensor_tensor(out=split(h[:, cols]), in0=natural(acc), in1=split(gamma_all[:, cols]), op=ALU.mult)
+            h_rows[ng, t] = h
 
-        def h_scale(i, gd):
-            nc.vector.tensor_tensor(out=h_cols(i, gd), in0=live["h_bank", i, gd][:], in1=gamma_b[:, gd * H:(gd + 1) * H], op=ALU.mult)
+        def norm_h(ng, t):
+            squares = work.tile([P, D], BF16, tag="squares", name="squares", bufs=2)
+            hh = small.tile([P, 1], F32, tag="hh", name="hh")
+            nc.scalar.activation(out=squares[:], in_=h_rows[ng, t][:], func=ACT.Square, accum_out=hh[:])
+            hh_sum[ng, t] = hh
 
-        def h_copy(i, gd):
-            nc.scalar.copy(out=h_cols(i, gd), in_=live["h_bank", i, gd][:])
+        def turn_g(ng, t, first_bank):
+            for dg in range(GROUPS):
+                acc = bank(first_bank + dg)
+                for j in range(PACK):
+                    nc.tensor.transpose(acc[:, j * P : (j + 1) * P], g_t[ng, dg, j][:, t * P : (t + 1) * P], ident[:])
+                g_rows[ng, t, dg] = acc
 
-        def h_finish(i, gd):
-            nc.gpsimd.tensor_tensor(out=h_cols(i, gd), in0=h_cols(i, gd), in1=gamma_b[:, gd * H:(gd + 1) * H], op=ALU.mult)
+        def dot_gh(ng, t):
+            h = h_rows[ng, t]
+            den = small.tile([P, 1], F32, tag="den", name="den")
+            inv = small.tile([P, 1], F32, tag="inv", name="inv")
+            part = small.tile([P, 1], F32, tag="part", name="part")
+            sums = []
+            nc.vector.tensor_scalar(out=den[:], in0=hh_sum[ng, t][:], scalar1=-1.0, scalar2=-EPS, op0=ALU.mult, op1=ALU.add)
+            for dg in range(GROUPS):
+                products = work.tile([P, GROUP], BF16, tag="products", name="products", bufs=2)
+                gh = small.tile([P, 1], F32, tag="gh%d" % dg, name="gh")
+                nc.vector.scalar_tensor_tensor(
+                    out=split(products[:]), in0=natural(g_rows[ng, t, dg]), scalar=1.0,
+                    in1=split(h[:, dg * GROUP : (dg + 1) * GROUP]), op0=ALU.mult, op1=ALU.mult, accum_out=gh[:],
+                )
+                sums.append(gh)
+                if dg == 0:
+                    nc.vector.reciprocal(out=inv[:], in_=den[:])
+            nc.vector.tensor_scalar(out=part[:], in0=sums[0][:], scalar1=inv[:], scalar2=-0.5, op0=ALU.mult, op1=ALU.add)
+            hh_inv[ng, t] = (inv, part, sums[1])
 
-        squares_out = sb.tile([P, W + 8], BF16, name="junk_s")
-        products_out = sb.tile([P, 2, H], BF16, name="junk_v")
+        def make_coef(ng, t):
+            inv, part, gh = hh_inv[ng, t]
+            coef = small.tile([P, 1], F32, tag="coef", name="coef")
+            nc.vector.tensor_scalar(out=coef[:], in0=gh[:], scalar1=inv[:], scalar2=part[:], op0=ALU.mult, op1=ALU.add)
+            coefs[ng, t] = coef
 
-        def small(name, i, n=1):
-            return sb.tile([P, n], F32, name="%s%d" % (name, i))
+        def project(ng, t):
+            if t == 0:
+                result[ng] = work.tile([P, PACK, D], F32, tag="result", name="result")
+            res = result[ng]
+            rows = out_0[ng * GROUP : (ng + 1) * GROUP, :].rearrange("(p t) d -> p t d", t=PACK)
+            for dg in range(GROUPS):
+                cols = slice(dg * GROUP, (dg + 1) * GROUP)
+                nc.vector.scalar_tensor_tensor(
+                    out=split(res[:, t, cols]), in0=split(h_rows[ng, t][:, cols]), scalar=coefs[ng, t][:],
+                    in1=natural(g_rows[ng, t, dg]), op0=ALU.mult, op1=ALU.add,
+                )
+                nc.sync.dma_start(out=rows[:, t, cols], in_=res[:, t, cols])
 
-        def hh_sum(i):
-            live["den", i] = small("den", i)
-            nc.scalar.activation(out=squares_out[:, 0:W + 1], in_=h_rows[i % H_TILES][:, 0:W + 1], func=ACT.Square,
-                                 accum_out=live["den", i][:])
+        def round_out(ng, dg, copy, first, width):
+            if ("out", ng, dg) not in staged:
+                staged["out", ng, dg] = stage_tile()
+            stage = staged["out", ng, dg]
+            col = dg * GROUP + first
+            copy(
+                out=pairs_out(stage[:, PACK * first : PACK * (first + width)]),
+                in_=pairs_in(result[ng][:, :, col : col + width]),
+            )
 
-        def invert(i):
-            live["rec", i] = small("rec", i)
-            nc.vector.reciprocal(out=live["rec", i][:], in_=live["den", i][:])
+        def quant_out(ng, dg):
+            if dg == 0:
+                codes_new = mx.tile([P, D], U32, tag="out_codes", name="out_codes", align_bytes=64)
+                scales_new = mx.tile([P, D], U8, tag="out_scales", name="out_scales", align_bytes=64)
+                out_q[ng] = (codes_new, scales_new)
+            codes, scales = out_q[ng]
+            words = out_1[ng].rearrange("p m t -> p (m t)").bitcast(I32)
+            cols = slice(dg * GROUP, (dg + 1) * GROUP)
+            nc.vector.quantize_mx(out=codes[:, cols].bitcast(FP8X4), scales=scales[:, cols], in_=staged["out", ng, dg][:])
+            nc.sync.dma_start(out=words[:, cols], in_=codes[:, cols].bitcast(I32))
 
-        def gh_sum(i, gd):
-            if ("gh", i) not in live:
-                live["gh", i] = small("gh", i, 2)
-            nc.vector.scalar_tensor_tensor(
-                out=products_out[:, gd, :], in0=live["g_bank", i, gd][:], scalar=-1.0, in1=h_cols(i, gd),
-                op0=ALU.mult, op1=ALU.mult, accum_out=live["gh", i][:, gd:gd + 1])
-
-        def coefficient(i):
-            live["coef", i] = small("coef", i)
-            parts = small("parts", i, 2)
-            nc.vector.tensor_scalar(out=parts[:], in0=live["gh", i][:], scalar1=live["rec", i][:], scalar2=-0.5,
-                                    op0=ALU.mult, op1=ALU.add, accum_out=live["coef", i][:])
-
-        def combine(i, gd):
-            h, tn = divmod(i, 4)
-            if ("out", h) not in live:
-                live["out", h] = sb.tile([P, 4, W], F32, name="o", tag="big%d" % h)
-            nc.vector.scalar_tensor_tensor(
-                out=live["out", h][:, tn, gd * H:(gd + 1) * H], in0=h_cols(i, gd), scalar=live["coef", i][:],
-                in1=live["g_bank", i, gd][:], op0=ALU.mult, op1=ALU.add)
-
-        def o_store(i):
-            h, tn = divmod(i, 4)
-            nc.sync.dma_start(out=rows(out_0, h)[:, tn, :], in_=live["out", h][:, tn, :])
-
-        def o_cols(h, c0, c1):
-            return live["out_woven", h, c0 // 4][:, (c0 % 4) * H:(c0 % 4 + c1 - c0) * H]
-
-        def o_weave(h, c0, c1, engine):
-            gd = c0 // 4
-            if ("out_woven", h, gd) not in live:
-                live["out_woven", h, gd] = stage(2 * h + gd)
-            move(engine, o_cols(h, c0, c1).rearrange("p (d t) -> p d t", t=4),
-                 live["out", h][:, :, c0 * P:c1 * P].rearrange("p t d -> p d t"))
-
-        def o_quant(h, c0, c1):
-            quantize(oq, h, c0 * P, o_cols(h, c0, c1))
-            c = slice(c0 * P, c1 * P)
-            nc.sync.dma_start(out=out_1[h].rearrange("p m t -> p (m t)").bitcast(I32)[:, c], in_=oq[0][:, h, c].bitcast(I32))
-
-        def o_scales(h):
+        def store_scales(ng, queues):
+            scales = out_q[ng][1]
             for quad in range(4):
-                eng = nc.sync if quad % 2 == 0 else nc.scalar
-                eng.dma_start(out=out_2[h, 4 * quad:4 * quad + 4, :].bitcast(I32),
-                              in_=oq[1][32 * quad:32 * quad + 4, h, :].bitcast(I32))
+                queues[quad % len(queues)].dma_start(
+                    out=out_2[ng, 4 * quad : 4 * quad + 4, :].bitcast(I32),
+                    in_=scales[32 * quad : 32 * quad + 4, :].bitcast(I32),
+                )
 
+        on_scalar, on_vector = nc.scalar.copy, nc.vector.tensor_copy
+        every_slot = slice(0, PACK)
 
-        load_x(0, 0, 0, 512); load_x(0, 0, 512, 1024); load_x(0, 1, 0, 1024); load_w(0, 0); load_w(0, 1); load_w(1, 0)
-        load_w(1, 1); load_x(1, 0, 0, 1024); load_x(1, 1, 0, 1024); load_y(0); load_spread("beta"); load_y(1)
-        load_spread("gamma"); load_gamma_rows(); w_weave(0, 0, 0, 2, "scalar"); warm_pe(); warm_pe(); x_turn(0, 0, 0, 6)
-        warm_pe(); x_turn(0, 1, 0, 7); x_scale(0, 0, 0); x_turn(0, 1, 1, 3); x_scale(0, 1, 0); x_scale(0, 1, 1)
-        x_turn(0, 0, 1, 2); x_scale(0, 0, 1); x_quant(0, 0); wt_turn(0, 0, 0, 4); w_weave(0, 1, 0, 2, "scalar")
-        w_quant(0, 0, 0, 2); wt_turn(0, 0, 1, 5); spread_z(6); x_quant(0, 1); z_copy(); w_quant(0, 1, 0, 2); turn_ab(7)
-
-        s_mm(1); ab_copy(); w_weave(0, 0, 2, 4, "vector"); w_weave(0, 1, 2, 4, "vector"); p_mm(0)
-        w_weave(1, 1, 2, 4, "vector"); wt_copy(0, 0, 1); w_quant(0, 0, 2, 4); wt_copy(0, 0, 0); act(1, "sig"); p_mm(1)
-        w_quant(0, 1, 2, 4); act(1, "q"); s_mm(0); wt_turn(0, 1, 0, 4); act(0, "sig"); x_turn(1, 0, 1, 7)
-        w_weave(1, 1, 0, 2, "vector"); wt_turn(0, 1, 1, 5); s_mm(3); wt_copy(0, 1, 0); x_turn(1, 1, 0, 4)
-        wt_copy(0, 1, 1); w_weave(1, 0, 2, 4, "vector"); act(0, "q"); w_weave(1, 0, 0, 2, "vector"); x_turn(1, 0, 0, 6)
-        wt_quant(0, 0); w_quant(1, 0, 0, 4); x_turn(1, 1, 1, 5); s_mm(2); act(3, "sig"); act(3, "q")
-        w_quant(1, 1, 0, 4); s_mm(5); square(1, "gpsimd"); x_scale(1, 1, 0); square(0, "scalar"); x_scale(1, 0, 0)
-        x_scale(1, 0, 1); act(2, "sig"); x_scale(1, 1, 1); act(2, "q"); n_mm(0); x_quant(1, 0); wt_turn(1, 0, 0, 6)
-        x_quant(1, 1); n_scale(0); s_mm(4); n_mm(1); wt_turn(1, 0, 1, 7); act(5, "sig"); act(5, "q"); s_mm(7)
-        wt_copy(1, 0, 0); u_step(0); p_mm(2); act(4, "q"); act(4, "sig"); s_mm(6); square(2, "scalar"); wt_copy(1, 0, 1)
-        square(3, "gpsimd"); n_scale(1); n_mm(3); u_step(1); wt_turn(1, 1, 0, 7); wt_quant(0, 1); p_mm(3); u_step(2)
-        p_mm(4); n_mm(2); square(4, "scalar"); r2_pairs(0, 0); act(6, "q"); u_step(3); act(7, "q"); r1_turn(0, 0, 6)
-        act(7, "sig"); s_mm(9); act(6, "sig"); s_mm(8); wt_copy(1, 1, 0); n_scale(3); p_mm(5); square(7, "scalar")
-        n_scale(2)
-
-        n_mm(5); turn_gamma(7); n_mm(4); square(5, "scalar"); u_step(4); act(8, "sig"); r2_pairs(0, 1); u_step(5)
-        r1_copy(0, 0); r2_weave(0, "vector"); wt_quant(1, 0); r1_turn(0, 1, 6); p_mm(7); n_scale(4); p_mm(6); n_scale(5)
-        square(6, "gpsimd"); u_step(7); u_step(6); act(8, "q"); s_mm(10); act(9, "q"); act(9, "sig"); s_mm(11); n_mm(6)
-        r1_copy(0, 1); r1_turn(1, 0, 6); p_mm(9); r2_pairs(1, 0); act(10, "sig"); act(10, "q"); r2_pairs(1, 1); n_mm(7)
-        n_scale(7); gamma_copy(); wt_turn(1, 1, 1, 7); act(11, "sig"); square(9, "gpsimd"); n_scale(6); act(11, "q")
-        square(11, "scalar"); square(8, "scalar"); p_mm(8); u_step(9); s_mm(13); s_mm(12); n_mm(9); n_mm(8)
-        r1_copy(1, 0); r1_turn(1, 1, 6); wt_copy(1, 1, 1); u_step(8); p_mm(10); act(12, "sig"); act(12, "q")
-        r2_quant(0); r1_quant(0); s_mm(14); r2_weave(1, "scalar"); act(13, "sig"); n_scale(9); n_mm(11); r1_copy(1, 1)
-        wt_quant(1, 1); r2_quant(1); h_mm(0, 7, 1); n_scale(8); r1_quant(1); p_mm(11); act(13, "q")
-        square(10, "gpsimd"); u_step(10); act(14, "sig"); h_copy(0, 1); u_step(11); act(14, "q"); s_mm(15); n_scale(11)
-        act(15, "q"); n_mm(10); n_scale(10); act(15, "sig"); r1_turn(2, 0, 6); r1_copy(2, 0); r2_pairs(2, 1)
-        h_mm(1, 7, 1); square(15, "scalar")
-
-        gt_mm(0, 0); square(13, "scalar"); n_mm(13); square(14, "scalar"); r1_turn(2, 1, 6); gt_mm(0, 1); r1_copy(2, 1)
-        r2_pairs(2, 0); gt_scale(0, 0); gt_scale(0, 1); h_scale(1, 1); n_scale(13); p_mm(13); u_step(13); n_mm(12)
-        p_mm(12); r2_weave(2, "scalar"); square(12, "gpsimd"); u_step(12); h_mm(0, 7, 0); gt_mm(0, 2); h_scale(0, 0)
-        gt_mm(0, 3); h_finish(0, 1); p_mm(15); n_scale(12); h_mm(1, 7, 0); p_mm(14); r2_pairs(3, 0); gt_scale(0, 2)
-        gt_mm(0, 4); n_mm(14); hh_sum(0); gt_scale(0, 3); u_step(14); gt_scale(0, 4); r1_turn(3, 0, 6); r1_copy(3, 0)
-        gt_mm(0, 5); u_step(15); gt_mm(0, 6); n_mm(15); g_turn(0, 0); h_copy(1, 0); h_mm(2, 7, 1); gt_scale(0, 6)
-        gt_scale(0, 5); r1_quant(2); r2_quant(2); r2_pairs(3, 1); r2_weave(3, "scalar"); n_scale(14); gt_mm(0, 7)
-        gt_scale(0, 7); n_scale(15); h_scale(2, 1); r1_turn(3, 1, 0); r1_copy(3, 1); h_finish(1, 0); gh_sum(0, 0)
-        h_mm(2, 6, 0); g_turn(1, 0); r2_quant(3); g_turn(0, 1); r1_quant(3); gh_sum(1, 0); gh_sum(0, 1); invert(0)
-        h_copy(2, 0); hh_sum(1); invert(1); g_turn(1, 1); h_mm(3, 7, 1); h_copy(3, 1)
-
-        gt_mm(1, 1); gh_sum(1, 1); coefficient(0); gt_scale(1, 1); h_mm(3, 6, 0); h_copy(3, 0); coefficient(1)
-        gt_mm(1, 0); h_finish(2, 0); h_mm(4, 7, 1); combine(0, 1); combine(1, 1); combine(0, 0); gt_mm(1, 3); hh_sum(2)
-        h_mm(4, 6, 0); h_finish(3, 1); gt_scale(1, 0); g_turn(2, 1); g_turn(3, 1); combine(1, 0); g_turn(2, 0)
-        gh_sum(2, 1); gh_sum(2, 0); invert(2); h_copy(4, 1); gt_mm(1, 2); h_copy(4, 0); gt_scale(1, 3); gh_sum(3, 1)
-        g_turn(3, 0); h_finish(3, 0); gh_sum(3, 0); gt_scale(1, 2); h_mm(5, 6, 0); h_scale(5, 0); gt_mm(1, 5)
-        gt_mm(1, 4); h_mm(5, 7, 1); hh_sum(3); invert(3); h_finish(4, 1); coefficient(2); coefficient(3); combine(2, 0)
-        h_mm(6, 6, 0); gt_scale(1, 5); gt_mm(1, 7); gt_scale(1, 4); gt_mm(1, 6); combine(2, 1); h_copy(5, 1)
-        h_finish(4, 0); h_mm(6, 7, 1); gt_scale(1, 7); combine(3, 0); gt_scale(1, 6); combine(3, 1); g_turn(4, 0)
-        g_turn(5, 0); g_turn(4, 1); h_scale(6, 1); h_mm(7, 7, 1); h_copy(6, 0); gh_sum(4, 0); o_store(3); gh_sum(4, 1)
-        gh_sum(5, 0); g_turn(5, 1); hh_sum(4); h_finish(5, 1); o_store(1); g_turn(6, 0); invert(4); h_mm(7, 6, 0)
-        h_copy(7, 1); o_store(0); hh_sum(5); h_finish(6, 0); h_copy(7, 0); gh_sum(5, 1); hh_sum(6); coefficient(4)
-        g_turn(6, 1); h_finish(7, 1); gh_sum(6, 0); invert(5); combine(4, 1); gh_sum(6, 1); h_finish(7, 0); o_store(2)
-        coefficient(5); invert(6); g_turn(7, 1)
-
-        o_weave(0, 0, 2, "gpsimd"); o_weave(0, 2, 4, "scalar"); combine(4, 0); o_store(4); g_turn(7, 0); combine(5, 1)
-        o_weave(0, 4, 6, "scalar"); hh_sum(7); coefficient(6); combine(5, 0); o_store(5); combine(6, 0); combine(6, 1)
-        o_store(6); gh_sum(7, 1); gh_sum(7, 0); invert(7); o_quant(0, 0, 4); coefficient(7); o_weave(0, 6, 8, "scalar")
-        o_quant(0, 4, 8); o_scales(0); combine(7, 1); combine(7, 0); o_weave(1, 6, 8, "vector")
-        o_weave(1, 0, 3, "vector"); o_store(7); o_weave(1, 4, 6, "scalar"); o_quant(1, 4, 8); o_weave(1, 3, 4, "scalar")
-        o_quant(1, 0, 4); o_scales(1)
+        turn_x(0, 0)
+        sort_w(0, 0, on_scalar, every_slot)
+        quant_x(0, 0)
+        turn_x(0, 1)
+        quant_w(0, 0)
+        sort_w(1, 0, on_scalar, slice(0, 2))
+        sort_w(1, 0, on_vector, slice(2, 4))
+        quant_x(0, 1)
+        quant_w(1, 0)
+        turn_y(0, 0, 0)
+        z_cols = const.tile([P, N], BF16, name="z_cols")
+        nc.vector.tensor_copy(
+            out=z_cols[:].rearrange("p (g t m) -> p g t m", g=GROUPS, t=PACK),
+            in_=z_all[:].rearrange("p (g m t) -> p g t m", g=GROUPS, t=PACK),
+        )
+        for cg in range(GROUPS):
+            y_rows[1, cg] = load_rows(y, 1, cg, "xy_rows", 6)
+        score(0, 0, 0)
+        score(0, 0, 1)
+        turn_y(0, 0, 1)
+        residuals(0, 0, 0)
+        sort_w(1, 1, on_vector, every_slot)
+        sort_w(0, 1, on_scalar, every_slot)
+        score(0, 0, 2)
+        residuals(0, 0, 1)
+        quant_w(1, 1)
+        turn_x(1, 0)
+        score(0, 0, 3)
+        quant_w(0, 1)
+        quant_x(1, 0)
+        turn_x(1, 1)
+        residuals(0, 0, 2)
+        quant_x(1, 1)
+        score(0, 1, 0)
+        turn_y(0, 1, 0)
+        residuals(0, 0, 3)
+        score(0, 1, 1)
+        turn_y(0, 1, 1)
+        final_r1(0, 0)
+        final_r2(0, 0)
+        score(0, 1, 2)
+        quant_r1(0, 0)
+        residuals(0, 1, 0)
+        score(0, 1, 3)
+        quant_r2(0, 0)
+        residuals(0, 1, 1)
+        turn_y(1, 0, 0)
+        score(1, 0, 0)
+        residuals(0, 1, 2)
+        residuals(0, 1, 3)
+        score(1, 0, 1)
+        turn_y(1, 0, 1)
+        final_r1(0, 1)
+        final_r2(0, 1)
+        turn_w(0, 0)
+        turn_w(0, 1)
+        quant_r1(0, 1)
+        residuals(1, 0, 0)
+        quant_r2(0, 1)
+        quant_wt(0, 0)
+        quant_wt(0, 1)
+        turn_w(1, 0)
+        turn_w(1, 1)
+        score(1, 0, 2)
+        residuals(1, 0, 1)
+        quant_wt(1, 0)
+        quant_wt(1, 1)
+        score(1, 0, 3)
+        make_h(0, 0, 4)
+        make_h(0, 1, 6)
+        norm_h(0, 0)
+        flush_slope()
+        residuals(1, 0, 2)
+        make_g(0, 0)
+        turn_y(1, 1, 0)
+        residuals(1, 0, 3)
+        make_g(0, 1)
+        final_r1(1, 0)
+        turn_y(1, 1, 1)
+        score(1, 1, 0)
+        turn_g(0, 0, 6)
+        final_r2(1, 0)
+        norm_h(0, 1)
+        score(1, 1, 1)
+        dot_gh(0, 0)
+        quant_r1(1, 0)
+        make_coef(0, 0)
+        quant_r2(1, 0)
+        project(0, 0)
+        make_h(0, 2, 4)
+        turn_g(0, 1, 6)
+        norm_h(0, 2)
+        score(1, 1, 2)
+        dot_gh(0, 1)
+        residuals(1, 1, 0)
+        make_coef(0, 1)
+        score(1, 1, 3)
+        make_h(0, 3, 4)
+        project(0, 1)
+        turn_g(0, 2, 6)
+        flush_slope()
+        norm_h(0, 3)
+        residuals(1, 1, 1)
+        turn_g(0, 3, 4)
+        dot_gh(0, 2)
+        dot_gh(0, 3)
+        make_coef(0, 2)
+        residuals(1, 1, 2)
+        make_coef(0, 3)
+        project(0, 2)
+        project(0, 3)
+        round_out(0, 0, on_scalar, 0, GROUP)
+        round_out(0, 1, on_scalar, 0, GROUP)
+        residuals(1, 1, 3)
+        for t in range(2):
+            for dg in range(GROUPS):
+                open_h(1, t, dg, 4 + 2 * t)
+        for j in range(PACK):
+            open_g(1, 0, j)
+        final_r1(1, 1)
+        quant_out(0, 0)
+        quant_r1(1, 1)
+        make_g(1, 0)
+        make_g(1, 1)
+        final_r2(1, 1)
+        quant_out(0, 1)
+        quant_r2(1, 1)
+        store_scales(0, [nc.sync])
+        for t in range(PACK):
+            make_h(1, t, 4 + 2 * (t % 2))
+            norm_h(1, t)
+        turn_g(1, 0, 0)
+        turn_g(1, 1, 2)
+        dot_gh(1, 0)
+        for t in range(PACK):
+            if t + 1 < PACK:
+                dot_gh(1, t + 1)
+            if t + 1 < PACK:
+                make_coef(1, t)
+            if t + 2 == PACK:
+                make_coef(1, t + 1)
+            project(1, t)
+            if t + 2 < PACK:
+                turn_g(1, t + 2, 2 * (t % 2))
+        round_out(1, 0, on_scalar, 0, GROUP // 2)
+        round_out(1, 0, on_vector, GROUP // 2, GROUP // 2)
+        round_out(1, 1, on_scalar, 0, GROUP // 2)
+        round_out(1, 1, on_vector, GROUP // 2, GROUP // 2)
+        quant_out(1, 0)
+        quant_out(1, 1)
+        store_scales(1, [nc.scalar, nc.sync])

@@ -55,18 +55,14 @@ def tile_adversarialdebiasingprojectedrepresentat_x1_kernel(
         a_s = load_slots(a, "a_s")
         w_rows, x_rows, y_rows = {}, {}, {}
         for dg in range(GROUPS):
-            x_rows[0, dg] = load_rows(x, 0, dg, "xy_rows", 6)
+            x_rows[0, dg] = load_rows(x, 0, dg, "xy_rows", 4)
             w_rows[dg, 0] = load_rows(w, dg, 0, "w_rows", 4)
-        y_rows[0, 0] = load_rows(y, 0, 0, "xy_rows", 6)
         z_all = const.tile([P, N], BF16, name="z_all")
         nc.sync.dma_start(out=z_all[:], in_=z.partition_broadcast(P))
+        y_rows[0, 0] = load_rows(y, 0, 0, "xy_rows", 4)
         for dg in range(GROUPS):
             w_rows[dg, 1] = load_rows(w, dg, 1, "w_rows", 4)
-        for dg in range(GROUPS):
-            x_rows[1, dg] = load_rows(x, 1, dg, "xy_rows", 6)
-        y_rows[0, 1] = load_rows(y, 0, 1, "xy_rows", 6)
-        gamma_all = const.tile([P, D], BF16, name="gamma_all")
-        nc.sync.dma_start(out=gamma_all[:], in_=gamma.partition_broadcast(P))
+        x_rows[1, 0] = load_rows(x, 1, 0, "xy_rows", 4)
 
         ident = const.tile([P, P], F32)
         make_identity(nc, ident[:])
@@ -103,7 +99,7 @@ def tile_adversarialdebiasingprojectedrepresentat_x1_kernel(
                 stop=(g == GROUPS - 1),
             )
 
-        opened = {}
+        opened, closed = {}, {}
 
         def transpose_half(rows, half, acc):
             for u in range(2):
@@ -127,15 +123,19 @@ def tile_adversarialdebiasingprojectedrepresentat_x1_kernel(
         def quant_w(dg, cg):
             w_q[dg, cg] = quantize(staged["w", dg, cg], "w%d%d" % (dg, cg))
 
-        def turn_x(ng, dg):
+        def turn(kind, rows, key, first_bank):
+            for half in range(2):
+                acc = bank(first_bank + half)
+                transpose_half(rows[key], half, acc)
+                closed[kind, key, half] = acc
+
+        def scale_x(ng, dg):
             stage = stage_tile()
             staged["x", ng, dg] = stage
             for half in range(2):
-                acc = bank(4 + 2 * dg + half)
-                transpose_half(x_rows[ng, dg], half, acc)
                 nc.vector.tensor_tensor(
                     out=stage[:, half * 1024 : (half + 1) * 1024].rearrange("p (n u e) -> p n u e", u=2, e=2),
-                    in0=acc[:].bitcast(BF16).rearrange("p (u n e) -> p n u e", u=2, e=2),
+                    in0=closed["x", (ng, dg), half][:].bitcast(BF16).rearrange("p (u n e) -> p n u e", u=2, e=2),
                     in1=gamma_s[:, dg, :].rearrange("p (u e) -> p u e", e=2).unsqueeze(1).to_broadcast([P, 256, 2, 2]),
                     op=ALU.mult,
                 )
@@ -143,21 +143,19 @@ def tile_adversarialdebiasingprojectedrepresentat_x1_kernel(
         def quant_x(ng, dg):
             x_q[ng, dg] = quantize(staged["x", ng, dg], "x%d%d" % (ng, dg))
 
-        def turn_w(cg, dg):
+        def copy_wt(cg, dg):
             stage = stage_tile()
             staged["wt", cg, dg] = stage
             for half in range(2):
-                acc = bank(4 + 2 * dg + half)
-                transpose_half(w_rows[dg, cg], half, acc)
                 nc.scalar.copy(
                     out=stage[:, half * 1024 : (half + 1) * 1024].bitcast(F32).rearrange("p (n u) -> p n u", u=2),
-                    in_=acc[:].rearrange("p (u n) -> p n u", u=2),
+                    in_=closed["w", (dg, cg), half][:].rearrange("p (u n) -> p n u", u=2),
                 )
 
         def quant_wt(cg, dg):
             wt_q[cg, dg] = quantize(staged["wt", cg, dg], "wt%d%d" % (cg, dg))
 
-        act_out, y_turned, slopes, resid = {}, {}, {}, {}
+        tanhs, sigs, r1_acc, slopes, lins, y_turned = {}, {}, {}, {}, {}, {}
         pending = []
 
         def flush_slope():
@@ -176,33 +174,39 @@ def tile_adversarialdebiasingprojectedrepresentat_x1_kernel(
                 words = y_rows[ng, cg][:, tn, :].bitcast(F32)
                 nc.tensor.transpose(y_t[:, tn * P : (tn + 1) * P], words[:, u::2], ident[:])
 
-        def score(ng, cg, t):
+        def subtract_y(ng, cg, t):
+            sig = sigs[ng, cg][:, t, :]
+            y_t = y_turned[ng, cg, t // 2]
+            nc.vector.tensor_tensor(out=sig, in0=sig, in1=y_t[:].bitcast(BF16)[:, t % 2 :: 2], op=ALU.subtract)
+
+        def score_mm(ng, cg, t):
             acc = bank(t % 2)
             for dg in range(GROUPS):
                 mx_pass(acc, w_q[dg, cg], t, x_q[ng, dg], dg)
-            sig = work.tile([P, GROUP], F32, tag="sig", name="sig", bufs=4)
+            closed["s", ng, cg, t] = acc
+
+        def score(ng, cg, t):
+            if ("s", ng, cg, t) not in closed:
+                score_mm(ng, cg, t)
+            acc = closed["s", ng, cg, t]
+            if t == 0:
+                sigs[ng, cg] = work.tile([P, PACK, GROUP], F32, tag="sig", name="sig", bufs=2)
             q = work.tile([P, GROUP], F32, tag="q", name="q", bufs=4)
             qq = work.tile([P, GROUP], F32, tag="qq", name="qq", bufs=2)
             beta_t = beta_f[:, cg, t : t + 1]
-            nc.scalar.activation(out=sig[:], in_=acc[:], func=ACT.Sigmoid, scale=beta_t)
+            nc.scalar.activation(out=sigs[ng, cg][:, t, :], in_=acc[:], func=ACT.Sigmoid, scale=beta_t)
             nc.scalar.activation(out=q[:], in_=acc[:], func=ACT.Tanh, scale=beta_t)
             if pending:
                 flush_slope()
             nc.scalar.activation(out=qq[:], in_=q[:], func=ACT.Square)
             pending.append((ng, cg, t, qq))
-            act_out[ng, cg, t] = (sig, q)
+            tanhs[ng, cg, t] = q
 
-        def residuals(ng, cg, t):
+        def linear(ng, cg, t):
             if t == 0:
-                r1_new = work.tile([P, PACK, GROUP], F32, tag="r1", name="r1")
-                lin_new = work.tile([P, PACK, GROUP], F32, tag="lin", name="lin")
-                resid[ng, cg] = (r1_new, lin_new)
-            r1, lin = resid[ng, cg]
-            sig, q = act_out[ng, cg, t]
-            y_t = y_turned[ng, cg, t // 2]
-            nc.vector.tensor_tensor(out=r1[:, t, :], in0=sig[:], in1=y_t[:].bitcast(BF16)[:, t % 2 :: 2], op=ALU.subtract)
+                lins[ng, cg] = work.tile([P, PACK, GROUP], F32, tag="lin", name="lin")
             nc.vector.scalar_tensor_tensor(
-                out=lin[:, t, :], in0=q[:], scalar=a_f[:, cg, t : t + 1],
+                out=lins[ng, cg][:, t, :], in0=tanhs[ng, cg, t][:], scalar=a_f[:, cg, t : t + 1],
                 in1=z_cols[:, ng * GROUP : (ng + 1) * GROUP], op0=ALU.mult, op1=ALU.subtract,
             )
 
@@ -212,20 +216,40 @@ def tile_adversarialdebiasingprojectedrepresentat_x1_kernel(
         def pairs_in(src):
             return src.rearrange("p t (c i) -> p c t i", i=2)
 
-        def final_r1(ng, cg):
+        def scale_r1(ng, cg):
             stage = stage_tile()
             staged["r1", ng, cg] = stage
             nc.vector.tensor_tensor(
-                out=pairs_out(stage[:]), in0=pairs_in(resid[ng, cg][0][:]),
+                out=pairs_out(stage[:]), in0=pairs_in(sigs[ng, cg][:]),
                 in1=beta_f[:, cg, :].unsqueeze(1).unsqueeze(3).to_broadcast([P, GROUP // 2, PACK, 2]),
                 op=ALU.mult,
             )
+
+        def scale_r1_slot(ng, cg, t):
+            if t == 0:
+                staged["r1_slots", ng, cg] = stage_tile()
+            nc.scalar.activation(
+                out=staged["r1_slots", ng, cg][:, t * GROUP : (t + 1) * GROUP], in_=sigs[ng, cg][:, t, :],
+                func=ACT.Copy, scale=beta_f[:, cg, t : t + 1],
+            )
+
+        def weave_r1(ng, cg):
+            stage = stage_tile()
+            staged["r1", ng, cg] = stage
+            nc.scalar.copy(
+                out=stage[:].rearrange("p (c i t) -> p c t i", i=4, t=PACK),
+                in_=staged["r1_slots", ng, cg][:].rearrange("p (t c i) -> p c t i", i=4, t=PACK),
+            )
+
+        def residuals(ng, cg, t):
+            subtract_y(ng, cg, t)
+            linear(ng, cg, t)
 
         def final_r2(ng, cg):
             stage = stage_tile()
             staged["r2", ng, cg] = stage
             nc.vector.tensor_tensor(
-                out=pairs_out(stage[:]), in0=pairs_in(resid[ng, cg][1][:]), in1=pairs_in(slopes[ng, cg][:]), op=ALU.mult
+                out=pairs_out(stage[:]), in0=pairs_in(lins[ng, cg][:]), in1=pairs_in(slopes[ng, cg][:]), op=ALU.mult
             )
 
         def quant_r1(ng, cg):
@@ -236,25 +260,37 @@ def tile_adversarialdebiasingprojectedrepresentat_x1_kernel(
 
         g_t, h_rows, hh_sum, hh_inv, g_rows, coefs, result, out_q = {}, {}, {}, {}, {}, {}, {}, {}
 
-        def open_g(ng, dg, j):
-            acc = bank((4 if ng == 0 else 0) + j)
-            mx_pass(acc, wt_q[0, dg], j, r1_q[ng, 0], 0)
+        def open_g(ng, dg, j, which):
+            acc = bank(which)
+            mx_pass(acc, wt_q[ng, dg], j, r1_q[ng, ng], 0)
             opened["g", ng, dg, j] = acc
+
+        def g_mm(ng, dg, j, which):
+            if ("g", ng, dg, j) not in opened:
+                open_g(ng, dg, j, which)
+            mx_pass(opened["g", ng, dg, j], wt_q[1 - ng, dg], j, r1_q[ng, 1 - ng], 1)
+
+        def g_scale(ng, dg, j):
+            g_dj = work.tile([P, GROUP], F32, tag="g_t", name="g_t", bufs=8)
+            nc.scalar.activation(
+                out=g_dj[:], in_=opened["g", ng, dg, j][:], func=ACT.Copy, scale=gamma_f[:, dg, j : j + 1]
+            )
+            g_t[ng, dg, j] = g_dj
+
+        def make_g(ng, dg, j, which):
+            g_mm(ng, dg, j, which)
+            g_scale(ng, dg, j)
 
         def open_h(ng, t, dg, first_bank):
             acc = bank(first_bank + dg)
             mx_pass(acc, r2_q[ng, 0], t, wt_q[0, dg], 0)
             opened["h", ng, t, dg] = acc
 
-        def make_g(ng, dg):
-            for j in range(PACK):
-                if ("g", ng, dg, j) not in opened:
-                    open_g(ng, dg, j)
-                acc = opened["g", ng, dg, j]
-                mx_pass(acc, wt_q[1, dg], j, r1_q[ng, 1], 1)
-                g_dj = work.tile([P, GROUP], F32, tag="g_t", name="g_t", bufs=8)
-                nc.scalar.activation(out=g_dj[:], in_=acc[:], func=ACT.Copy, scale=gamma_f[:, dg, j : j + 1])
-                g_t[ng, dg, j] = g_dj
+        def h_mm(ng, t, first_bank):
+            for dg in range(GROUPS):
+                if ("h", ng, t, dg) not in opened:
+                    open_h(ng, t, dg, first_bank)
+                mx_pass(opened["h", ng, t, dg], r2_q[ng, 1], t, wt_q[1, dg], 1)
 
         def natural(acc):
             return acc[:].rearrange("p (j m) -> p m j", j=PACK)
@@ -262,16 +298,18 @@ def tile_adversarialdebiasingprojectedrepresentat_x1_kernel(
         def split(row_ap):
             return row_ap.rearrange("p (m j) -> p m j", j=PACK)
 
-        def make_h(ng, t, first_bank):
+        def h_scale(ng, t):
             h = work.tile([P, D], F32, tag="h", name="h", bufs=4)
             for dg in range(GROUPS):
-                if ("h", ng, t, dg) not in opened:
-                    open_h(ng, t, dg, first_bank)
-                acc = opened["h", ng, t, dg]
-                mx_pass(acc, r2_q[ng, 1], t, wt_q[1, dg], 1)
                 cols = slice(dg * GROUP, (dg + 1) * GROUP)
-                nc.vector.tensor_tensor(out=split(h[:, cols]), in0=natural(acc), in1=split(gamma_all[:, cols]), op=ALU.mult)
+                nc.vector.tensor_tensor(
+                    out=split(h[:, cols]), in0=natural(opened["h", ng, t, dg]), in1=split(gamma_all[:, cols]), op=ALU.mult
+                )
             h_rows[ng, t] = h
+
+        def make_h(ng, t, first_bank):
+            h_mm(ng, t, first_bank)
+            h_scale(ng, t)
 
         def norm_h(ng, t):
             squares = work.tile([P, D], BF16, tag="squares", name="squares", bufs=2)
@@ -314,7 +352,7 @@ def tile_adversarialdebiasingprojectedrepresentat_x1_kernel(
 
         def project(ng, t):
             if t == 0:
-                result[ng] = work.tile([P, PACK, D], F32, tag="result", name="result")
+                result[ng] = work.tile([P, PACK, D], F32, tag="result", name="result", bufs=2)
             res = result[ng]
             rows = out_0[ng * GROUP : (ng + 1) * GROUP, :].rearrange("(p t) d -> p t d", t=PACK)
             for dg in range(GROUPS):
@@ -337,8 +375,8 @@ def tile_adversarialdebiasingprojectedrepresentat_x1_kernel(
 
         def quant_out(ng, dg):
             if dg == 0:
-                codes_new = mx.tile([P, D], U32, tag="out_codes", name="out_codes", align_bytes=64)
-                scales_new = mx.tile([P, D], U8, tag="out_scales", name="out_scales", align_bytes=64)
+                codes_new = mx.tile([P, D], U32, tag="out_codes", name="out_codes", bufs=2, align_bytes=64)
+                scales_new = mx.tile([P, D], U8, tag="out_scales", name="out_scales", bufs=2, align_bytes=64)
                 out_q[ng] = (codes_new, scales_new)
             codes, scales = out_q[ng]
             words = out_1[ng].rearrange("p m t -> p (m t)").bitcast(I32)
@@ -357,150 +395,205 @@ def tile_adversarialdebiasingprojectedrepresentat_x1_kernel(
         on_scalar, on_vector = nc.scalar.copy, nc.vector.tensor_copy
         every_slot = slice(0, PACK)
 
-        turn_x(0, 0)
         sort_w(0, 0, on_scalar, every_slot)
+        turn("x", x_rows, (0, 0), 4)
+        turn("x", x_rows, (0, 1), 6)
+        scale_x(0, 0)
+        sort_w(1, 0, on_scalar, every_slot)
+        scale_x(0, 1)
         quant_x(0, 0)
-        turn_x(0, 1)
         quant_w(0, 0)
-        sort_w(1, 0, on_scalar, slice(0, 2))
-        sort_w(1, 0, on_vector, slice(2, 4))
         quant_x(0, 1)
         quant_w(1, 0)
-        turn_y(0, 0, 0)
         z_cols = const.tile([P, N], BF16, name="z_cols")
-        nc.vector.tensor_copy(
+        nc.scalar.copy(
             out=z_cols[:].rearrange("p (g t m) -> p g t m", g=GROUPS, t=PACK),
             in_=z_all[:].rearrange("p (g m t) -> p g t m", g=GROUPS, t=PACK),
         )
-        for cg in range(GROUPS):
-            y_rows[1, cg] = load_rows(y, 1, cg, "xy_rows", 6)
-        score(0, 0, 0)
-        score(0, 0, 1)
+        x_rows[1, 1] = load_rows(x, 1, 1, "xy_rows", 4)
+        y_rows[0, 1] = load_rows(y, 0, 1, "xy_rows", 4)
+        gamma_all = const.tile([P, D], BF16, name="gamma_all")
+        nc.sync.dma_start(out=gamma_all[:], in_=gamma.partition_broadcast(P))
+        turn_y(0, 0, 0)
+        score_mm(0, 0, 0)
+        score_mm(0, 0, 1)
         turn_y(0, 0, 1)
+        y_rows[1, 0] = load_rows(y, 1, 0, "xy_rows", 4)
+        sort_w(0, 1, on_vector, every_slot)
+        score(0, 0, 0)
+        score_mm(0, 0, 2)
+        turn("x", x_rows, (1, 0), 4)
+        y_rows[1, 1] = load_rows(y, 1, 1, "xy_rows", 4)
         residuals(0, 0, 0)
         sort_w(1, 1, on_vector, every_slot)
-        sort_w(0, 1, on_scalar, every_slot)
-        score(0, 0, 2)
+        score(0, 0, 1)
+        score_mm(0, 0, 3)
+        turn("x", x_rows, (1, 1), 6)
+        quant_w(0, 1)
         residuals(0, 0, 1)
         quant_w(1, 1)
-        turn_x(1, 0)
-        score(0, 0, 3)
-        quant_w(0, 1)
-        quant_x(1, 0)
-        turn_x(1, 1)
+        score(0, 0, 2)
+        score_mm(0, 1, 0)
+        turn_y(0, 1, 0)
+        scale_x(1, 0)
         residuals(0, 0, 2)
+        quant_x(1, 0)
+        score(0, 0, 3)
+        score_mm(0, 1, 1)
+        turn("w", w_rows, (0, 0), 4)
+        scale_x(1, 1)
+        residuals(0, 0, 3)
         quant_x(1, 1)
         score(0, 1, 0)
-        turn_y(0, 1, 0)
-        residuals(0, 0, 3)
-        score(0, 1, 1)
+        score_mm(0, 1, 2)
         turn_y(0, 1, 1)
-        final_r1(0, 0)
+        turn("w", w_rows, (1, 0), 6)
+        scale_r1(0, 0)
+        score(0, 1, 1)
+        score_mm(0, 1, 3)
+        copy_wt(0, 0)
+        turn("w", w_rows, (0, 1), 4)
         final_r2(0, 0)
         score(0, 1, 2)
+        score_mm(1, 0, 0)
+        copy_wt(0, 1)
+        turn("w", w_rows, (1, 1), 6)
         quant_r1(0, 0)
         residuals(0, 1, 0)
-        score(0, 1, 3)
         quant_r2(0, 0)
         residuals(0, 1, 1)
         turn_y(1, 0, 0)
-        score(1, 0, 0)
-        residuals(0, 1, 2)
-        residuals(0, 1, 3)
-        score(1, 0, 1)
-        turn_y(1, 0, 1)
-        final_r1(0, 1)
-        final_r2(0, 1)
-        turn_w(0, 0)
-        turn_w(0, 1)
-        quant_r1(0, 1)
-        residuals(1, 0, 0)
-        quant_r2(0, 1)
+        score(0, 1, 3)
+        score_mm(1, 0, 1)
         quant_wt(0, 0)
+        residuals(0, 1, 2)
         quant_wt(0, 1)
-        turn_w(1, 0)
-        turn_w(1, 1)
-        score(1, 0, 2)
-        residuals(1, 0, 1)
+        copy_wt(1, 0)
+        for dg in range(GROUPS):
+            open_h(0, 0, dg, 4)
+        score(1, 0, 0)
+        score_mm(1, 0, 2)
+        residuals(0, 1, 3)
+        turn_y(1, 0, 1)
+        copy_wt(1, 1)
+        open_g(0, 0, 0, 6)
+        open_g(0, 0, 1, 7)
+        scale_r1(0, 1)
+        score(1, 0, 1)
+        score_mm(1, 0, 3)
         quant_wt(1, 0)
+        final_r2(0, 1)
+        score(1, 0, 2)
+        quant_r1(0, 1)
+        g_mm(0, 0, 0, 6)
+        g_mm(0, 0, 1, 7)
         quant_wt(1, 1)
-        score(1, 0, 3)
-        make_h(0, 0, 4)
-        make_h(0, 1, 6)
-        norm_h(0, 0)
+        quant_r2(0, 1)
         flush_slope()
+        h_mm(0, 0, 4)
+        residuals(1, 0, 0)
+        h_scale(0, 0)
+        g_scale(0, 0, 0)
+        g_scale(0, 0, 1)
+        h_mm(0, 1, 4)
+        make_g(0, 0, 2, 0)
+        make_g(0, 0, 3, 6)
+        norm_h(0, 0)
+        residuals(1, 0, 1)
+        h_scale(0, 1)
+        make_g(0, 1, 0, 7)
+        h_mm(0, 2, 4)
+        make_g(0, 1, 1, 2)
+        make_g(0, 1, 2, 0)
+        make_g(0, 1, 3, 6)
         residuals(1, 0, 2)
-        make_g(0, 0)
-        turn_y(1, 1, 0)
-        residuals(1, 0, 3)
-        make_g(0, 1)
-        final_r1(1, 0)
-        turn_y(1, 1, 1)
-        score(1, 1, 0)
+        h_scale(0, 2)
+        h_mm(0, 3, 4)
         turn_g(0, 0, 6)
-        final_r2(1, 0)
+        score(1, 0, 3)
         norm_h(0, 1)
-        score(1, 1, 1)
+        score_mm(1, 1, 0)
+        turn_y(1, 1, 0)
+        h_scale(0, 3)
+        turn_g(0, 1, 4)
         dot_gh(0, 0)
-        quant_r1(1, 0)
+        residuals(1, 0, 3)
         make_coef(0, 0)
-        quant_r2(1, 0)
+        score(1, 1, 0)
+        score(1, 1, 1)
+        turn_y(1, 1, 1)
+        dot_gh(0, 1)
         project(0, 0)
-        make_h(0, 2, 4)
-        turn_g(0, 1, 6)
+        turn_g(0, 2, 6)
+        make_coef(0, 1)
+        final_r2(1, 0)
         norm_h(0, 2)
         score(1, 1, 2)
-        dot_gh(0, 1)
-        residuals(1, 1, 0)
-        make_coef(0, 1)
-        score(1, 1, 3)
-        make_h(0, 3, 4)
         project(0, 1)
-        turn_g(0, 2, 6)
-        flush_slope()
-        norm_h(0, 3)
-        residuals(1, 1, 1)
         turn_g(0, 3, 4)
+        quant_r2(1, 0)
+        residuals(1, 1, 0)
+        norm_h(0, 3)
+        score(1, 1, 3)
+        scale_r1_slot(1, 0, 0)
+        flush_slope()
+        for t in range(1, PACK):
+            scale_r1_slot(1, 0, t)
+        weave_r1(1, 0)
         dot_gh(0, 2)
-        dot_gh(0, 3)
+        residuals(1, 1, 1)
         make_coef(0, 2)
         residuals(1, 1, 2)
-        make_coef(0, 3)
         project(0, 2)
+        residuals(1, 1, 3)
+        for dg in range(GROUPS):
+            open_h(1, 0, dg, 6)
+        scale_r1(1, 1)
+        dot_gh(0, 3)
+        quant_r1(1, 1)
+        for j in range(PACK):
+            open_g(1, 0, j, j)
+        quant_r1(1, 0)
+        for j in range(PACK):
+            make_g(1, 0, j, j)
+        make_g(1, 1, 0, 0)
+        make_g(1, 1, 1, 1)
+        final_r2(1, 1)
+        make_coef(0, 3)
+        quant_r2(1, 1)
+        make_g(1, 1, 2, 2)
+        h_mm(1, 0, 6)
+        make_g(1, 1, 3, 3)
         project(0, 3)
+        h_mm(1, 1, 4)
+        h_scale(1, 0)
+        norm_h(1, 0)
+        h_mm(1, 2, 6)
+        h_scale(1, 1)
+        norm_h(1, 1)
+        h_mm(1, 3, 4)
+        for t in range(2, PACK):
+            h_scale(1, t)
+            norm_h(1, t)
         round_out(0, 0, on_scalar, 0, GROUP)
         round_out(0, 1, on_scalar, 0, GROUP)
-        residuals(1, 1, 3)
-        for t in range(2):
-            for dg in range(GROUPS):
-                open_h(1, t, dg, 4 + 2 * t)
-        for j in range(PACK):
-            open_g(1, 0, j)
-        final_r1(1, 1)
-        quant_out(0, 0)
-        quant_r1(1, 1)
-        make_g(1, 0)
-        make_g(1, 1)
-        final_r2(1, 1)
-        quant_out(0, 1)
-        quant_r2(1, 1)
-        store_scales(0, [nc.sync])
         for t in range(PACK):
-            make_h(1, t, 4 + 2 * (t % 2))
-            norm_h(1, t)
-        turn_g(1, 0, 0)
-        turn_g(1, 1, 2)
+            turn_g(1, t, (0, 2, 6, 4)[t])
         dot_gh(1, 0)
-        for t in range(PACK):
-            if t + 1 < PACK:
-                dot_gh(1, t + 1)
-            if t + 1 < PACK:
-                make_coef(1, t)
-            if t + 2 == PACK:
-                make_coef(1, t + 1)
-            project(1, t)
-            if t + 2 < PACK:
-                turn_g(1, t + 2, 2 * (t % 2))
+        dot_gh(1, 1)
+        make_coef(1, 0)
+        dot_gh(1, 2)
+        make_coef(1, 1)
+        project(1, 0)
+        dot_gh(1, 3)
+        make_coef(1, 2)
+        project(1, 1)
+        make_coef(1, 3)
+        quant_out(0, 0)
+        project(1, 2)
+        quant_out(0, 1)
+        store_scales(0, [nc.sync])
+        project(1, 3)
         round_out(1, 0, on_scalar, 0, GROUP // 2)
         round_out(1, 0, on_vector, GROUP // 2, GROUP // 2)
         round_out(1, 1, on_scalar, 0, GROUP // 2)

@@ -67,6 +67,15 @@ def tile_adversarialdebiasingprojectedrepresentat_x1_kernel(
         ident = const.tile([P, P], F32)
         make_identity(nc, ident[:])
 
+        warm = const.tile([P, 1], F32, name="warm")
+        nc.scalar.activation(out=warm[:], in_=ident[:, 0:1], func=ACT.Sigmoid)
+
+        neg_ident = const.tile([P, P], BF16, name="neg_ident")
+        nc.vector.tensor_scalar(out=neg_ident[:], in0=ident[:], scalar1=-1.0, scalar2=None, op0=ALU.mult)
+
+        neg_half = const.tile([P, 1], F32, name="neg_half")
+        nc.vector.memset(neg_half[:], -0.5)
+
         gamma_f = const.tile([P, GROUPS, PACK], F32)
         beta_f = const.tile([P, GROUPS, PACK], F32)
         a_f = const.tile([P, GROUPS, PACK], F32)
@@ -167,6 +176,34 @@ def tile_adversarialdebiasingprojectedrepresentat_x1_kernel(
                 scale=neg_ab_f[:, cg, t : t + 1], bias=ab_f[:, cg, t : t + 1],
             )
 
+        def open_r1(ng, cg, tn):
+            acc = bank((2 + tn) % 4 if (ng, cg) == (1, 1) else 2 + tn % 2)
+            r1_acc[ng, cg, tn] = acc
+            for t in range(PACK):
+                nc.tensor.matmul(
+                    acc[:, t * P : (t + 1) * P], lhsT=y_rows[ng, cg][:, tn, t::PACK], rhs=neg_ident[:],
+                    start=(t == 0), stop=False,
+                )
+
+        def close_r1(ng, cg, tn):
+            if (ng, cg, tn) not in r1_acc:
+                open_r1(ng, cg, tn)
+            nc.tensor.matmul(
+                r1_acc[ng, cg, tn][:].rearrange("p (t m) -> p t m", t=PACK), lhsT=ident[:],
+                rhs=sigs[ng, cg][:, :, tn * P : (tn + 1) * P], start=False, stop=True,
+            )
+
+        def final_r1(ng, cg, tn):
+            if tn == 0:
+                staged["r1", ng, cg] = stage_tile()
+            stage = staged["r1", ng, cg]
+            nc.vector.tensor_tensor(
+                out=stage[:, tn * GROUP : (tn + 1) * GROUP].rearrange("p (m t) -> p m t", t=PACK),
+                in0=r1_acc[ng, cg, tn][:].rearrange("p (t m) -> p m t", t=PACK),
+                in1=beta_f[:, cg, :].unsqueeze(1).to_broadcast([P, P, PACK]),
+                op=ALU.mult,
+            )
+
         def turn_y(ng, cg, u):
             y_t = bank(2 + u)
             y_turned[ng, cg, u] = y_t
@@ -262,13 +299,13 @@ def tile_adversarialdebiasingprojectedrepresentat_x1_kernel(
 
         def open_g(ng, dg, j, which):
             acc = bank(which)
-            mx_pass(acc, wt_q[ng, dg], j, r1_q[ng, ng], 0)
+            mx_pass(acc, wt_q[0, dg], j, r1_q[ng, 0], 0)
             opened["g", ng, dg, j] = acc
 
         def g_mm(ng, dg, j, which):
             if ("g", ng, dg, j) not in opened:
                 open_g(ng, dg, j, which)
-            mx_pass(opened["g", ng, dg, j], wt_q[1 - ng, dg], j, r1_q[ng, 1 - ng], 1)
+            mx_pass(opened["g", ng, dg, j], wt_q[1, dg], j, r1_q[ng, 1], 1)
 
         def g_scale(ng, dg, j):
             g_dj = work.tile([P, GROUP], F32, tag="g_t", name="g_t", bufs=8)
@@ -324,13 +361,21 @@ def tile_adversarialdebiasingprojectedrepresentat_x1_kernel(
                     nc.tensor.transpose(acc[:, j * P : (j + 1) * P], g_t[ng, dg, j][:, t * P : (t + 1) * P], ident[:])
                 g_rows[ng, t, dg] = acc
 
+        def scale_add(ng, out, value, factor, term):
+            if ng == 0:
+                nc.vector.tensor_scalar(
+                    out=out[:], in0=value[:], scalar1=factor[:], scalar2=term[:], op0=ALU.mult, op1=ALU.add
+                )
+            else:
+                nc.scalar.activation(out=out[:], in_=value[:], func=ACT.Identity, scale=factor[:], bias=term[:])
+
         def dot_gh(ng, t):
             h = h_rows[ng, t]
             den = small.tile([P, 1], F32, tag="den", name="den")
+            nc.vector.tensor_scalar(out=den[:], in0=hh_sum[ng, t][:], scalar1=-1.0, scalar2=-EPS, op0=ALU.mult, op1=ALU.add)
             inv = small.tile([P, 1], F32, tag="inv", name="inv")
             part = small.tile([P, 1], F32, tag="part", name="part")
             sums = []
-            nc.vector.tensor_scalar(out=den[:], in0=hh_sum[ng, t][:], scalar1=-1.0, scalar2=-EPS, op0=ALU.mult, op1=ALU.add)
             for dg in range(GROUPS):
                 products = work.tile([P, GROUP], BF16, tag="products", name="products", bufs=2)
                 gh = small.tile([P, 1], F32, tag="gh%d" % dg, name="gh")
@@ -341,27 +386,30 @@ def tile_adversarialdebiasingprojectedrepresentat_x1_kernel(
                 sums.append(gh)
                 if dg == 0:
                     nc.vector.reciprocal(out=inv[:], in_=den[:])
-            nc.vector.tensor_scalar(out=part[:], in0=sums[0][:], scalar1=inv[:], scalar2=-0.5, op0=ALU.mult, op1=ALU.add)
+            scale_add(ng, part, sums[0], inv, neg_half)
             hh_inv[ng, t] = (inv, part, sums[1])
 
         def make_coef(ng, t):
             inv, part, gh = hh_inv[ng, t]
             coef = small.tile([P, 1], F32, tag="coef", name="coef")
-            nc.vector.tensor_scalar(out=coef[:], in0=gh[:], scalar1=inv[:], scalar2=part[:], op0=ALU.mult, op1=ALU.add)
+            scale_add(ng, coef, gh, inv, part)
             coefs[ng, t] = coef
 
-        def project(ng, t):
-            if t == 0:
-                result[ng] = work.tile([P, PACK, D], F32, tag="result", name="result", bufs=2)
+        def project_half(ng, t, dg):
+            if ng not in result:
+                result[ng] = work.tile([P, PACK, D], F32, tag="result", name="result")
             res = result[ng]
             rows = out_0[ng * GROUP : (ng + 1) * GROUP, :].rearrange("(p t) d -> p t d", t=PACK)
+            cols = slice(dg * GROUP, (dg + 1) * GROUP)
+            nc.vector.scalar_tensor_tensor(
+                out=split(res[:, t, cols]), in0=split(h_rows[ng, t][:, cols]), scalar=coefs[ng, t][:],
+                in1=natural(g_rows[ng, t, dg]), op0=ALU.mult, op1=ALU.add,
+            )
+            nc.sync.dma_start(out=rows[:, t, cols], in_=res[:, t, cols])
+
+        def project(ng, t):
             for dg in range(GROUPS):
-                cols = slice(dg * GROUP, (dg + 1) * GROUP)
-                nc.vector.scalar_tensor_tensor(
-                    out=split(res[:, t, cols]), in0=split(h_rows[ng, t][:, cols]), scalar=coefs[ng, t][:],
-                    in1=natural(g_rows[ng, t, dg]), op0=ALU.mult, op1=ALU.add,
-                )
-                nc.sync.dma_start(out=rows[:, t, cols], in_=res[:, t, cols])
+                project_half(ng, t, dg)
 
         def round_out(ng, dg, copy, first, width):
             if ("out", ng, dg) not in staged:
@@ -375,8 +423,8 @@ def tile_adversarialdebiasingprojectedrepresentat_x1_kernel(
 
         def quant_out(ng, dg):
             if dg == 0:
-                codes_new = mx.tile([P, D], U32, tag="out_codes", name="out_codes", bufs=2, align_bytes=64)
-                scales_new = mx.tile([P, D], U8, tag="out_scales", name="out_scales", bufs=2, align_bytes=64)
+                codes_new = mx.tile([P, D], U32, tag="out_codes", name="out_codes", align_bytes=64)
+                scales_new = mx.tile([P, D], U8, tag="out_scales", name="out_scales", align_bytes=64)
                 out_q[ng] = (codes_new, scales_new)
             codes, scales = out_q[ng]
             words = out_1[ng].rearrange("p m t -> p (m t)").bitcast(I32)
@@ -400,8 +448,8 @@ def tile_adversarialdebiasingprojectedrepresentat_x1_kernel(
         turn("x", x_rows, (0, 1), 6)
         scale_x(0, 0)
         sort_w(1, 0, on_scalar, every_slot)
-        scale_x(0, 1)
         quant_x(0, 0)
+        scale_x(0, 1)
         quant_w(0, 0)
         quant_x(0, 1)
         quant_w(1, 0)
@@ -420,18 +468,18 @@ def tile_adversarialdebiasingprojectedrepresentat_x1_kernel(
         turn_y(0, 0, 1)
         y_rows[1, 0] = load_rows(y, 1, 0, "xy_rows", 4)
         sort_w(0, 1, on_vector, every_slot)
+        sort_w(1, 1, on_vector, every_slot)
         score(0, 0, 0)
         score_mm(0, 0, 2)
         turn("x", x_rows, (1, 0), 4)
         y_rows[1, 1] = load_rows(y, 1, 1, "xy_rows", 4)
         residuals(0, 0, 0)
-        sort_w(1, 1, on_vector, every_slot)
         score(0, 0, 1)
         score_mm(0, 0, 3)
         turn("x", x_rows, (1, 1), 6)
         quant_w(0, 1)
-        residuals(0, 0, 1)
         quant_w(1, 1)
+        residuals(0, 0, 1)
         score(0, 0, 2)
         score_mm(0, 1, 0)
         turn_y(0, 1, 0)
@@ -462,7 +510,6 @@ def tile_adversarialdebiasingprojectedrepresentat_x1_kernel(
         residuals(0, 1, 0)
         quant_r2(0, 0)
         residuals(0, 1, 1)
-        turn_y(1, 0, 0)
         score(0, 1, 3)
         score_mm(1, 0, 1)
         quant_wt(0, 0)
@@ -474,10 +521,11 @@ def tile_adversarialdebiasingprojectedrepresentat_x1_kernel(
         score(1, 0, 0)
         score_mm(1, 0, 2)
         residuals(0, 1, 3)
-        turn_y(1, 0, 1)
         copy_wt(1, 1)
         open_g(0, 0, 0, 6)
         open_g(0, 0, 1, 7)
+        open_g(0, 0, 2, 2)
+        open_g(0, 0, 3, 3)
         scale_r1(0, 1)
         score(1, 0, 1)
         score_mm(1, 0, 3)
@@ -491,113 +539,115 @@ def tile_adversarialdebiasingprojectedrepresentat_x1_kernel(
         quant_r2(0, 1)
         flush_slope()
         h_mm(0, 0, 4)
-        residuals(1, 0, 0)
+        g_mm(0, 0, 2, 2)
+        g_mm(0, 0, 3, 3)
+        linear(1, 0, 0)
         h_scale(0, 0)
-        g_scale(0, 0, 0)
-        g_scale(0, 0, 1)
+        for j in range(PACK):
+            g_scale(0, 0, j)
         h_mm(0, 1, 4)
-        make_g(0, 0, 2, 0)
-        make_g(0, 0, 3, 6)
+        make_g(0, 1, 0, 6)
+        make_g(0, 1, 1, 7)
         norm_h(0, 0)
-        residuals(1, 0, 1)
+        linear(1, 0, 1)
         h_scale(0, 1)
-        make_g(0, 1, 0, 7)
         h_mm(0, 2, 4)
-        make_g(0, 1, 1, 2)
         make_g(0, 1, 2, 0)
         make_g(0, 1, 3, 6)
-        residuals(1, 0, 2)
+        h_mm(0, 3, 2)
+        linear(1, 0, 2)
         h_scale(0, 2)
-        h_mm(0, 3, 4)
-        turn_g(0, 0, 6)
-        score(1, 0, 3)
+        turn_g(0, 0, 4)
+        turn_g(0, 1, 6)
         norm_h(0, 1)
+        score(1, 0, 3)
         score_mm(1, 1, 0)
-        turn_y(1, 1, 0)
         h_scale(0, 3)
-        turn_g(0, 1, 4)
+        close_r1(1, 0, 0)
+        score_mm(1, 1, 1)
+        close_r1(1, 0, 1)
         dot_gh(0, 0)
-        residuals(1, 0, 3)
-        make_coef(0, 0)
-        score(1, 1, 0)
-        score(1, 1, 1)
-        turn_y(1, 1, 1)
         dot_gh(0, 1)
-        project(0, 0)
-        turn_g(0, 2, 6)
+        make_coef(0, 0)
+        linear(1, 0, 3)
+        score(1, 1, 0)
+        score_mm(1, 1, 2)
         make_coef(0, 1)
-        final_r2(1, 0)
+        project(0, 0)
+        turn_g(0, 2, 4)
+        final_r1(1, 0, 0)
+        close_r1(1, 0, 2)
+        final_r1(1, 0, 1)
         norm_h(0, 2)
-        score(1, 1, 2)
+        score(1, 1, 1)
+        score_mm(1, 1, 3)
+        close_r1(1, 0, 3)
         project(0, 1)
-        turn_g(0, 3, 4)
+        turn_g(0, 3, 6)
+        final_r2(1, 0)
+        final_r1(1, 0, 2)
+        open_r1(1, 1, 0)
         quant_r2(1, 0)
-        residuals(1, 1, 0)
+        final_r1(1, 0, 3)
+        open_r1(1, 1, 1)
         norm_h(0, 3)
+        score(1, 1, 2)
         score(1, 1, 3)
-        scale_r1_slot(1, 0, 0)
+        for tn in range(PACK):
+            close_r1(1, 1, tn)
         flush_slope()
-        for t in range(1, PACK):
-            scale_r1_slot(1, 0, t)
-        weave_r1(1, 0)
         dot_gh(0, 2)
-        residuals(1, 1, 1)
-        make_coef(0, 2)
-        residuals(1, 1, 2)
-        project(0, 2)
-        residuals(1, 1, 3)
-        for dg in range(GROUPS):
-            open_h(1, 0, dg, 6)
-        scale_r1(1, 1)
-        dot_gh(0, 3)
-        quant_r1(1, 1)
-        for j in range(PACK):
-            open_g(1, 0, j, j)
         quant_r1(1, 0)
-        for j in range(PACK):
-            make_g(1, 0, j, j)
-        make_g(1, 1, 0, 0)
-        make_g(1, 1, 1, 1)
-        final_r2(1, 1)
+        make_coef(0, 2)
+        dot_gh(0, 3)
+        project(0, 2)
         make_coef(0, 3)
-        quant_r2(1, 1)
-        make_g(1, 1, 2, 2)
-        h_mm(1, 0, 6)
-        make_g(1, 1, 3, 3)
+        linear(1, 1, 0)
         project(0, 3)
-        h_mm(1, 1, 4)
+        for dg in range(GROUPS):
+            round_out(0, dg, on_scalar, 0, GROUP)
+        for t in range(2):
+            for dg in range(GROUPS):
+                open_h(1, t, dg, 4 + 2 * t)
+        for tn in range(PACK):
+            if tn == PACK - 1:
+                linear(1, 1, 1)
+            final_r1(1, 1, tn)
+            open_g(1, 0, (tn + 2) % PACK, (tn + 2) % PACK)
+        linear(1, 1, 2)
+        quant_r1(1, 1)
+        for dg in range(GROUPS):
+            for j in range(PACK):
+                make_g(1, dg, j, j)
+        linear(1, 1, 3)
+        quant_out(0, 0)
+        final_r2(1, 1)
+        quant_r2(1, 1)
+        h_mm(1, 0, 4)
+        h_mm(1, 1, 6)
+        quant_out(0, 1)
+        store_scales(0, [nc.sync])
         h_scale(1, 0)
         norm_h(1, 0)
-        h_mm(1, 2, 6)
+        h_mm(1, 2, 4)
         h_scale(1, 1)
         norm_h(1, 1)
-        h_mm(1, 3, 4)
+        h_mm(1, 3, 6)
         for t in range(2, PACK):
             h_scale(1, t)
             norm_h(1, t)
-        round_out(0, 0, on_scalar, 0, GROUP)
-        round_out(0, 1, on_scalar, 0, GROUP)
         for t in range(PACK):
-            turn_g(1, t, (0, 2, 6, 4)[t])
-        dot_gh(1, 0)
-        dot_gh(1, 1)
-        make_coef(1, 0)
-        dot_gh(1, 2)
-        make_coef(1, 1)
-        project(1, 0)
-        dot_gh(1, 3)
-        make_coef(1, 2)
-        project(1, 1)
-        make_coef(1, 3)
-        quant_out(0, 0)
-        project(1, 2)
-        quant_out(0, 1)
-        store_scales(0, [nc.sync])
-        project(1, 3)
-        round_out(1, 0, on_scalar, 0, GROUP // 2)
-        round_out(1, 0, on_vector, GROUP // 2, GROUP // 2)
-        round_out(1, 1, on_scalar, 0, GROUP // 2)
-        round_out(1, 1, on_vector, GROUP // 2, GROUP // 2)
+            turn_g(1, t, 2 * t)
+        for t in range(PACK):
+            dot_gh(1, t)
+            make_coef(1, t)
+        for t in range(PACK):
+            project_half(1, t, 0)
+        round_out(1, 0, on_scalar, 0, GROUP)
+        for t in range(PACK):
+            project_half(1, t, 1)
+        round_out(1, 1, on_vector, 0, GROUP // 2)
+        round_out(1, 1, on_scalar, GROUP // 2, GROUP // 2)
         quant_out(1, 0)
         quant_out(1, 1)
         store_scales(1, [nc.scalar, nc.sync])

@@ -45,20 +45,21 @@ def tile_adversarialdebiasingprojectedrepresentat_x1_kernel(
             nc.sync.dma_start(out=rows[:], in_=view.rearrange("(p t) c -> p t c", t=PACK))
             return rows
 
-        def load_slots(vec, name):
+        def load_slots(vec, name, queue):
             slots = const.tile([P, GROUPS, PACK], BF16, name=name)
-            nc.scalar.dma_start(out=slots[:], in_=vec.rearrange("(g p t) -> p g t", g=GROUPS, t=PACK))
+            queue.dma_start(out=slots[:], in_=vec.rearrange("(g p t) -> p g t", g=GROUPS, t=PACK))
             return slots
 
-        gamma_s = load_slots(gamma, "gamma_s")
-        beta_s = load_slots(beta, "beta_s")
-        a_s = load_slots(a, "a_s")
+        gamma_s = load_slots(gamma, "gamma_s", nc.scalar)
+        z_row = const.tile([P, N], BF16, name="z_row")
+        nc.vector.memset(z_row[:], 0.0)
+        nc.scalar.dma_start(out=z_row[0:1, :], in_=z.rearrange("(o n) -> o n", o=1))
         w_rows, x_rows, y_rows = {}, {}, {}
         for dg in range(GROUPS):
             x_rows[0, dg] = load_rows(x, 0, dg, "xy_rows", 4)
             w_rows[dg, 0] = load_rows(w, dg, 0, "w_rows", 4)
-        z_all = const.tile([P, N], BF16, name="z_all")
-        nc.sync.dma_start(out=z_all[:], in_=z.partition_broadcast(P))
+        beta_s = load_slots(beta, "beta_s", nc.sync)
+        a_s = load_slots(a, "a_s", nc.sync)
         y_rows[0, 0] = load_rows(y, 0, 0, "xy_rows", 4)
         for dg in range(GROUPS):
             w_rows[dg, 1] = load_rows(w, dg, 1, "w_rows", 4)
@@ -81,11 +82,11 @@ def tile_adversarialdebiasingprojectedrepresentat_x1_kernel(
         a_f = const.tile([P, GROUPS, PACK], F32)
         ab_f = const.tile([P, GROUPS, PACK], F32)
         neg_ab_f = const.tile([P, GROUPS, PACK], F32)
-        nc.vector.tensor_copy(out=gamma_f[:], in_=gamma_s[:])
-        nc.vector.tensor_copy(out=beta_f[:], in_=beta_s[:])
-        nc.vector.tensor_copy(out=a_f[:], in_=a_s[:])
-        nc.vector.tensor_tensor(out=ab_f[:], in0=a_s[:], in1=beta_s[:], op=ALU.mult)
-        nc.vector.tensor_scalar(out=neg_ab_f[:], in0=ab_f[:], scalar1=-1.0, scalar2=None, op0=ALU.mult)
+        nc.gpsimd.tensor_copy(out=gamma_f[:], in_=gamma_s[:])
+        nc.gpsimd.tensor_copy(out=beta_f[:], in_=beta_s[:])
+        nc.gpsimd.tensor_copy(out=a_f[:], in_=a_s[:])
+        nc.gpsimd.tensor_tensor(out=ab_f[:], in0=a_s[:], in1=beta_s[:], op=ALU.mult)
+        nc.gpsimd.tensor_scalar(out=neg_ab_f[:], in0=ab_f[:], scalar1=-1.0, scalar2=0.0, op0=ALU.mult, op1=ALU.add)
 
         def stage_tile():
             return work.tile([P, GROUP * PACK], BF16, tag="stage", name="stage", bufs=4, align_bytes=64)
@@ -244,7 +245,7 @@ def tile_adversarialdebiasingprojectedrepresentat_x1_kernel(
                 lins[ng, cg] = work.tile([P, PACK, GROUP], F32, tag="lin", name="lin")
             nc.vector.scalar_tensor_tensor(
                 out=lins[ng, cg][:, t, :], in0=tanhs[ng, cg, t][:], scalar=a_f[:, cg, t : t + 1],
-                in1=z_cols[:, ng * GROUP : (ng + 1) * GROUP], op0=ALU.mult, op1=ALU.subtract,
+                in1=neg_z[:, ng * GROUP : (ng + 1) * GROUP], op0=ALU.mult, op1=ALU.add,
             )
 
         def pairs_out(stage_ap):
@@ -447,21 +448,27 @@ def tile_adversarialdebiasingprojectedrepresentat_x1_kernel(
         turn("x", x_rows, (0, 0), 4)
         turn("x", x_rows, (0, 1), 6)
         scale_x(0, 0)
-        sort_w(1, 0, on_scalar, every_slot)
+        sort_w(1, 0, on_scalar, slice(0, 3))
+        neg_z = const.tile([P, N], BF16, name="neg_z")
+        for ng in range(GROUPS):
+            acc = bank(4 + ng)
+            cols = slice(ng * GROUP, (ng + 1) * GROUP)
+            nc.tensor.matmul(
+                acc[:], lhsT=neg_ident[:, 0:1].to_broadcast([P, P]), rhs=z_row[:, cols], start=True, stop=True
+            )
+            nc.scalar.copy(
+                out=neg_z[:, cols].rearrange("p (t m) -> p t m", t=PACK),
+                in_=acc[:].rearrange("p (m t) -> p t m", t=PACK),
+            )
+
         quant_x(0, 0)
         scale_x(0, 1)
         quant_w(0, 0)
+        sort_w(1, 0, on_vector, slice(3, 4))
         quant_x(0, 1)
         quant_w(1, 0)
-        z_cols = const.tile([P, N], BF16, name="z_cols")
-        nc.scalar.copy(
-            out=z_cols[:].rearrange("p (g t m) -> p g t m", g=GROUPS, t=PACK),
-            in_=z_all[:].rearrange("p (g m t) -> p g t m", g=GROUPS, t=PACK),
-        )
         x_rows[1, 1] = load_rows(x, 1, 1, "xy_rows", 4)
         y_rows[0, 1] = load_rows(y, 0, 1, "xy_rows", 4)
-        gamma_all = const.tile([P, D], BF16, name="gamma_all")
-        nc.sync.dma_start(out=gamma_all[:], in_=gamma.partition_broadcast(P))
         turn_y(0, 0, 0)
         score_mm(0, 0, 0)
         score_mm(0, 0, 1)
@@ -473,6 +480,8 @@ def tile_adversarialdebiasingprojectedrepresentat_x1_kernel(
         score_mm(0, 0, 2)
         turn("x", x_rows, (1, 0), 4)
         y_rows[1, 1] = load_rows(y, 1, 1, "xy_rows", 4)
+        gamma_all = const.tile([P, D], BF16, name="gamma_all")
+        nc.sync.dma_start(out=gamma_all[:], in_=gamma.partition_broadcast(P))
         residuals(0, 0, 0)
         score(0, 0, 1)
         score_mm(0, 0, 3)
@@ -537,57 +546,59 @@ def tile_adversarialdebiasingprojectedrepresentat_x1_kernel(
         g_mm(0, 0, 1, 7)
         quant_wt(1, 1)
         quant_r2(0, 1)
-        flush_slope()
         h_mm(0, 0, 4)
         g_mm(0, 0, 2, 2)
         g_mm(0, 0, 3, 3)
+        score(1, 0, 3)
         linear(1, 0, 0)
         h_scale(0, 0)
-        for j in range(PACK):
-            g_scale(0, 0, j)
         h_mm(0, 1, 4)
-        make_g(0, 1, 0, 6)
-        make_g(0, 1, 1, 7)
-        norm_h(0, 0)
+        g_scale(0, 0, 0)
+        flush_slope()
+        for j in range(1, PACK):
+            g_scale(0, 0, j)
         linear(1, 0, 1)
         h_scale(0, 1)
         h_mm(0, 2, 4)
-        make_g(0, 1, 2, 0)
-        make_g(0, 1, 3, 6)
-        h_mm(0, 3, 2)
+        make_g(0, 1, 0, 0)
+        make_g(0, 1, 1, 1)
         linear(1, 0, 2)
         h_scale(0, 2)
-        turn_g(0, 0, 4)
-        turn_g(0, 1, 6)
-        norm_h(0, 1)
-        score(1, 0, 3)
-        score_mm(1, 1, 0)
-        h_scale(0, 3)
-        close_r1(1, 0, 0)
-        score_mm(1, 1, 1)
-        close_r1(1, 0, 1)
-        dot_gh(0, 0)
-        dot_gh(0, 1)
-        make_coef(0, 0)
+        h_mm(0, 3, 4)
+        make_g(0, 1, 2, 6)
+        make_g(0, 1, 3, 7)
+        norm_h(0, 0)
         linear(1, 0, 3)
+        h_scale(0, 3)
+        score_mm(1, 1, 0)
+        turn_g(0, 0, 4)
+        score_mm(1, 1, 1)
+        turn_g(0, 1, 6)
+        close_r1(1, 0, 0)
+        close_r1(1, 0, 1)
+        norm_h(0, 1)
         score(1, 1, 0)
         score_mm(1, 1, 2)
-        make_coef(0, 1)
-        project(0, 0)
-        turn_g(0, 2, 4)
+        final_r2(1, 0)
+        dot_gh(0, 0)
+        quant_r2(1, 0)
+        make_coef(0, 0)
+        dot_gh(0, 1)
         final_r1(1, 0, 0)
         close_r1(1, 0, 2)
+        make_coef(0, 1)
         final_r1(1, 0, 1)
         norm_h(0, 2)
         score(1, 1, 1)
         score_mm(1, 1, 3)
+        project(0, 0)
+        turn_g(0, 2, 4)
         close_r1(1, 0, 3)
         project(0, 1)
         turn_g(0, 3, 6)
-        final_r2(1, 0)
         final_r1(1, 0, 2)
         open_r1(1, 1, 0)
-        quant_r2(1, 0)
+        dot_gh(0, 2)
         final_r1(1, 0, 3)
         open_r1(1, 1, 1)
         norm_h(0, 3)
@@ -596,13 +607,11 @@ def tile_adversarialdebiasingprojectedrepresentat_x1_kernel(
         for tn in range(PACK):
             close_r1(1, 1, tn)
         flush_slope()
-        dot_gh(0, 2)
-        quant_r1(1, 0)
         make_coef(0, 2)
         dot_gh(0, 3)
         project(0, 2)
         make_coef(0, 3)
-        linear(1, 1, 0)
+        quant_r1(1, 0)
         project(0, 3)
         for dg in range(GROUPS):
             round_out(0, dg, on_scalar, 0, GROUP)
@@ -610,18 +619,17 @@ def tile_adversarialdebiasingprojectedrepresentat_x1_kernel(
             for dg in range(GROUPS):
                 open_h(1, t, dg, 4 + 2 * t)
         for tn in range(PACK):
-            if tn == PACK - 1:
-                linear(1, 1, 1)
+            if tn < PACK - 1:
+                linear(1, 1, tn)
             final_r1(1, 1, tn)
             open_g(1, 0, (tn + 2) % PACK, (tn + 2) % PACK)
-        linear(1, 1, 2)
+        linear(1, 1, 3)
         quant_r1(1, 1)
         for dg in range(GROUPS):
             for j in range(PACK):
                 make_g(1, dg, j, j)
-        linear(1, 1, 3)
-        quant_out(0, 0)
         final_r2(1, 1)
+        quant_out(0, 0)
         quant_r2(1, 1)
         h_mm(1, 0, 4)
         h_mm(1, 1, 6)

@@ -19,7 +19,11 @@ P = 128
 PACK = 4
 GROUP = P * PACK
 GROUPS = 2
+HALF_STAGE = GROUP * PACK // 2
 EPS = 1e-6
+
+ROW_TILES = 4
+STAGE_TILES = 4
 
 
 def tile_adversarialdebiasingprojectedrepresentat_x1_kernel(
@@ -31,7 +35,7 @@ def tile_adversarialdebiasingprojectedrepresentat_x1_kernel(
         raw = ctx.enter_context(tc.tile_pool(name="raw", bufs=1))
         mx = ctx.enter_context(tc.tile_pool(name="mx", bufs=1))
         work = ctx.enter_context(tc.tile_pool(name="work", bufs=1))
-        small = ctx.enter_context(tc.tile_pool(name="small", bufs=4))
+        small = ctx.enter_context(tc.tile_pool(name="small", bufs=PACK))
         psum = ctx.enter_context(tc.psum_pool(name="psum", bufs=1))
 
         ctx.enter_context(tc.manual_schedule())
@@ -39,9 +43,9 @@ def tile_adversarialdebiasingprojectedrepresentat_x1_kernel(
         def bank(i):
             return psum.tile([P, GROUP], F32, tag="bank%d" % i, name="bank%d" % i)
 
-        def load_rows(src, rg, cg, tag, bufs):
+        def load_rows(src, row_group, col_group, tag, bufs):
             rows = raw.tile([P, PACK, GROUP], BF16, tag=tag, name=tag, bufs=bufs)
-            view = src[rg * GROUP : (rg + 1) * GROUP, cg * GROUP : (cg + 1) * GROUP]
+            view = src[row_group * GROUP : (row_group + 1) * GROUP, col_group * GROUP : (col_group + 1) * GROUP]
             nc.sync.dma_start(out=rows[:], in_=view.rearrange("(p t) c -> p t c", t=PACK))
             return rows
 
@@ -50,31 +54,36 @@ def tile_adversarialdebiasingprojectedrepresentat_x1_kernel(
             queue.dma_start(out=slots[:], in_=vec.rearrange("(g p t) -> p g t", g=GROUPS, t=PACK))
             return slots
 
-        gamma_s = load_slots(gamma, "gamma_s", nc.scalar)
-        z_row = const.tile([P, N], BF16, name="z_row")
+        w_rows, x_rows, y_rows = {}, {}, {}
+
+        def load_w(dg, cg):
+            w_rows[dg, cg] = load_rows(w, dg, cg, "w_rows", GROUPS * GROUPS)
+
+        def load_x(ng, dg):
+            x_rows[ng, dg] = load_rows(x, ng, dg, "xy_rows", ROW_TILES)
+
+        def load_y(ng, cg):
+            y_rows[ng, cg] = load_rows(y, ng, cg, "xy_rows", ROW_TILES)
+
+        gamma_slots = load_slots(gamma, "gamma_slots", nc.scalar)
+        z_row = const.tile([P, N], BF16)
         nc.vector.memset(z_row[:], 0.0)
         nc.scalar.dma_start(out=z_row[0:1, :], in_=z.rearrange("(o n) -> o n", o=1))
-        w_rows, x_rows, y_rows = {}, {}, {}
         for dg in range(GROUPS):
-            x_rows[0, dg] = load_rows(x, 0, dg, "xy_rows", 4)
-            w_rows[dg, 0] = load_rows(w, dg, 0, "w_rows", 4)
-        beta_s = load_slots(beta, "beta_s", nc.sync)
-        a_s = load_slots(a, "a_s", nc.sync)
-        y_rows[0, 0] = load_rows(y, 0, 0, "xy_rows", 4)
+            load_x(0, dg)
+            load_w(dg, 0)
+        beta_slots = load_slots(beta, "beta_slots", nc.sync)
+        a_slots = load_slots(a, "a_slots", nc.sync)
+        load_y(0, 0)
         for dg in range(GROUPS):
-            w_rows[dg, 1] = load_rows(w, dg, 1, "w_rows", 4)
-        x_rows[1, 0] = load_rows(x, 1, 0, "xy_rows", 4)
+            load_w(dg, 1)
+        load_x(1, 0)
 
         ident = const.tile([P, P], F32)
         make_identity(nc, ident[:])
-
-        warm = const.tile([P, 1], F32, name="warm")
-        nc.scalar.activation(out=warm[:], in_=ident[:, 0:1], func=ACT.Sigmoid)
-
-        neg_ident = const.tile([P, P], BF16, name="neg_ident")
+        neg_ident = const.tile([P, P], BF16)
         nc.vector.tensor_scalar(out=neg_ident[:], in0=ident[:], scalar1=-1.0, scalar2=None, op0=ALU.mult)
-
-        neg_half = const.tile([P, 1], F32, name="neg_half")
+        neg_half = const.tile([P, 1], F32)
         nc.vector.memset(neg_half[:], -0.5)
 
         gamma_f = const.tile([P, GROUPS, PACK], F32)
@@ -82,162 +91,123 @@ def tile_adversarialdebiasingprojectedrepresentat_x1_kernel(
         a_f = const.tile([P, GROUPS, PACK], F32)
         ab_f = const.tile([P, GROUPS, PACK], F32)
         neg_ab_f = const.tile([P, GROUPS, PACK], F32)
-        nc.gpsimd.tensor_copy(out=gamma_f[:], in_=gamma_s[:])
-        nc.gpsimd.tensor_copy(out=beta_f[:], in_=beta_s[:])
-        nc.gpsimd.tensor_copy(out=a_f[:], in_=a_s[:])
-        nc.gpsimd.tensor_tensor(out=ab_f[:], in0=a_s[:], in1=beta_s[:], op=ALU.mult)
+        nc.gpsimd.tensor_copy(out=gamma_f[:], in_=gamma_slots[:])
+        nc.gpsimd.tensor_copy(out=beta_f[:], in_=beta_slots[:])
+        nc.gpsimd.tensor_copy(out=a_f[:], in_=a_slots[:])
+        nc.gpsimd.tensor_tensor(out=ab_f[:], in0=a_slots[:], in1=beta_slots[:], op=ALU.mult)
         nc.gpsimd.tensor_scalar(out=neg_ab_f[:], in0=ab_f[:], scalar1=-1.0, scalar2=0.0, op0=ALU.mult, op1=ALU.add)
 
-        def stage_tile():
-            return work.tile([P, GROUP * PACK], BF16, tag="stage", name="stage", bufs=4, align_bytes=64)
+        neg_z = const.tile([P, N], BF16)
+        gamma_all = const.tile([P, D], BF16)
 
-        def quantize(stage, name):
+        def spread_z(first_bank):
+            for ng in range(GROUPS):
+                acc = bank(first_bank + ng)
+                cols = slice(ng * GROUP, (ng + 1) * GROUP)
+                nc.tensor.matmul(
+                    acc[:], lhsT=neg_ident[:, 0:1].to_broadcast([P, P]), rhs=z_row[:, cols], start=True, stop=True
+                )
+                nc.scalar.copy(
+                    out=neg_z[:, cols].rearrange("p (t m) -> p t m", t=PACK),
+                    in_=acc[:].rearrange("p (m t) -> p t m", t=PACK),
+                )
+
+        staged = {}
+        quantised = {}
+
+        def new_stage(key):
+            staged[key] = work.tile(
+                [P, GROUP * PACK], BF16, tag="stage", name="stage", bufs=STAGE_TILES, align_bytes=64
+            )
+            return staged[key]
+
+        def quantize(kind, i, j):
+            name = "%s_%d%d" % (kind, i, j)
             codes = mx.tile([P, GROUP], U32, name=name + "_codes", align_bytes=64)
             scales = mx.tile([P, GROUP], U8, name=name + "_scales", align_bytes=64)
-            nc.vector.quantize_mx(out=codes[:].bitcast(FP8X4), scales=scales[:], in_=stage[:])
-            return codes, scales
+            nc.vector.quantize_mx(out=codes[:].bitcast(FP8X4), scales=scales[:], in_=staged[kind, i, j][:])
+            quantised[kind, i, j] = (codes, scales)
 
-        def mx_pass(acc, lhs, t, rhs, g):
+        def mx_pass(acc, stationary, t, moving, group):
             cols = slice(t * P, (t + 1) * P)
             nc.tensor.matmul_mx(
                 out=acc[:],
-                lhsT=lhs[0][:, cols].bitcast(FP8X4),
-                lhsT_scale=lhs[1][:, cols],
-                rhs=rhs[0][:].bitcast(FP8X4),
-                rhs_scale=rhs[1][:],
-                start=(g == 0),
-                stop=(g == GROUPS - 1),
+                lhsT=quantised[stationary][0][:, cols].bitcast(FP8X4),
+                lhsT_scale=quantised[stationary][1][:, cols],
+                rhs=quantised[moving][0][:].bitcast(FP8X4),
+                rhs_scale=quantised[moving][1][:],
+                start=(group == 0),
+                stop=(group == GROUPS - 1),
             )
 
-        opened, closed = {}, {}
-
-        def transpose_half(rows, half, acc):
-            for u in range(2):
-                for tt in range(2):
-                    words = rows[:, 2 * half + tt, :].bitcast(F32)
-                    col = (2 * u + tt) * P
-                    nc.tensor.transpose(acc[:, col : col + P], words[:, u::2], ident[:])
-
-        w_q, x_q, wt_q, r1_q, r2_q = {}, {}, {}, {}, {}
-        staged = {}
-
         def sort_w(dg, cg, copy, slots):
-            if ("w", dg, cg) not in staged:
-                staged["w", dg, cg] = stage_tile()
-            stage = staged["w", dg, cg]
+            stage = staged[("w", dg, cg)] if ("w", dg, cg) in staged else new_stage(("w", dg, cg))
             copy(
                 out=stage[:].rearrange("p (t m j) -> p t m j", t=PACK, j=PACK)[:, slots],
                 in_=w_rows[dg, cg][:].rearrange("p j (m t) -> p t m j", t=PACK)[:, slots],
             )
 
-        def quant_w(dg, cg):
-            w_q[dg, cg] = quantize(staged["w", dg, cg], "w%d%d" % (dg, cg))
+        turned = {}
 
         def turn(kind, rows, key, first_bank):
             for half in range(2):
                 acc = bank(first_bank + half)
-                transpose_half(rows[key], half, acc)
-                closed[kind, key, half] = acc
+                for u in range(2):
+                    for tt in range(2):
+                        words = rows[key][:, 2 * half + tt, :].bitcast(F32)
+                        col = (2 * u + tt) * P
+                        nc.tensor.transpose(acc[:, col : col + P], words[:, u::2], ident[:])
+                turned[kind, key, half] = acc
 
         def scale_x(ng, dg):
-            stage = stage_tile()
-            staged["x", ng, dg] = stage
+            stage = new_stage(("x", ng, dg))
+            factors = gamma_slots[:, dg, :].rearrange("p (u e) -> p u e", e=2)
             for half in range(2):
                 nc.vector.tensor_tensor(
-                    out=stage[:, half * 1024 : (half + 1) * 1024].rearrange("p (n u e) -> p n u e", u=2, e=2),
-                    in0=closed["x", (ng, dg), half][:].bitcast(BF16).rearrange("p (u n e) -> p n u e", u=2, e=2),
-                    in1=gamma_s[:, dg, :].rearrange("p (u e) -> p u e", e=2).unsqueeze(1).to_broadcast([P, 256, 2, 2]),
+                    out=stage[:, half * HALF_STAGE : (half + 1) * HALF_STAGE].rearrange("p (n u e) -> p n u e", u=2, e=2),
+                    in0=turned["x", (ng, dg), half][:].bitcast(BF16).rearrange("p (u n e) -> p n u e", u=2, e=2),
+                    in1=factors.unsqueeze(1).to_broadcast([P, 2 * P, 2, 2]),
                     op=ALU.mult,
                 )
 
-        def quant_x(ng, dg):
-            x_q[ng, dg] = quantize(staged["x", ng, dg], "x%d%d" % (ng, dg))
-
         def copy_wt(cg, dg):
-            stage = stage_tile()
-            staged["wt", cg, dg] = stage
+            stage = new_stage(("wt", cg, dg))
             for half in range(2):
                 nc.scalar.copy(
-                    out=stage[:, half * 1024 : (half + 1) * 1024].bitcast(F32).rearrange("p (n u) -> p n u", u=2),
-                    in_=closed["w", (dg, cg), half][:].rearrange("p (u n) -> p n u", u=2),
+                    out=stage[:, half * HALF_STAGE : (half + 1) * HALF_STAGE].bitcast(F32).rearrange("p (n u) -> p n u", u=2),
+                    in_=turned["w", (dg, cg), half][:].rearrange("p (u n) -> p n u", u=2),
                 )
 
-        def quant_wt(cg, dg):
-            wt_q[cg, dg] = quantize(staged["wt", cg, dg], "wt%d%d" % (cg, dg))
-
-        tanhs, sigs, r1_acc, slopes, lins, y_turned = {}, {}, {}, {}, {}, {}
-        pending = []
-
-        def flush_slope():
-            ng, cg, t, qq = pending.pop()
-            if t == 0:
-                slopes[ng, cg] = work.tile([P, PACK, GROUP], F32, tag="slope", name="slope", bufs=2)
-            nc.scalar.activation(
-                out=slopes[ng, cg][:, t, :], in_=qq[:], func=ACT.Identity,
-                scale=neg_ab_f[:, cg, t : t + 1], bias=ab_f[:, cg, t : t + 1],
-            )
-
-        def open_r1(ng, cg, tn):
-            acc = bank((2 + tn) % 4 if (ng, cg) == (1, 1) else 2 + tn % 2)
-            r1_acc[ng, cg, tn] = acc
-            for t in range(PACK):
-                nc.tensor.matmul(
-                    acc[:, t * P : (t + 1) * P], lhsT=y_rows[ng, cg][:, tn, t::PACK], rhs=neg_ident[:],
-                    start=(t == 0), stop=False,
-                )
-
-        def close_r1(ng, cg, tn):
-            if (ng, cg, tn) not in r1_acc:
-                open_r1(ng, cg, tn)
-            nc.tensor.matmul(
-                r1_acc[ng, cg, tn][:].rearrange("p (t m) -> p t m", t=PACK), lhsT=ident[:],
-                rhs=sigs[ng, cg][:, :, tn * P : (tn + 1) * P], start=False, stop=True,
-            )
-
-        def final_r1(ng, cg, tn):
-            if tn == 0:
-                staged["r1", ng, cg] = stage_tile()
-            stage = staged["r1", ng, cg]
-            nc.vector.tensor_tensor(
-                out=stage[:, tn * GROUP : (tn + 1) * GROUP].rearrange("p (m t) -> p m t", t=PACK),
-                in0=r1_acc[ng, cg, tn][:].rearrange("p (t m) -> p m t", t=PACK),
-                in1=beta_f[:, cg, :].unsqueeze(1).to_broadcast([P, P, PACK]),
-                op=ALU.mult,
-            )
-
-        def turn_y(ng, cg, u):
-            y_t = bank(2 + u)
-            y_turned[ng, cg, u] = y_t
-            for tn in range(PACK):
-                words = y_rows[ng, cg][:, tn, :].bitcast(F32)
-                nc.tensor.transpose(y_t[:, tn * P : (tn + 1) * P], words[:, u::2], ident[:])
-
-        def subtract_y(ng, cg, t):
-            sig = sigs[ng, cg][:, t, :]
-            y_t = y_turned[ng, cg, t // 2]
-            nc.vector.tensor_tensor(out=sig, in0=sig, in1=y_t[:].bitcast(BF16)[:, t % 2 :: 2], op=ALU.subtract)
+        scores, tanhs, sigs, slopes, lins, y_turned, r1_sums = {}, {}, {}, {}, {}, {}, {}
+        squares_waiting = []
 
         def score_mm(ng, cg, t):
             acc = bank(t % 2)
             for dg in range(GROUPS):
-                mx_pass(acc, w_q[dg, cg], t, x_q[ng, dg], dg)
-            closed["s", ng, cg, t] = acc
+                mx_pass(acc, ("w", dg, cg), t, ("x", ng, dg), dg)
+            scores[ng, cg, t] = acc
 
-        def score(ng, cg, t):
-            if ("s", ng, cg, t) not in closed:
-                score_mm(ng, cg, t)
-            acc = closed["s", ng, cg, t]
+        def finish_slope():
+            ng, cg, t, q_squared = squares_waiting.pop()
+            if t == 0:
+                slopes[ng, cg] = work.tile([P, PACK, GROUP], F32, tag="slope", name="slope", bufs=2)
+            nc.scalar.activation(
+                out=slopes[ng, cg][:, t, :], in_=q_squared[:], func=ACT.Identity,
+                scale=neg_ab_f[:, cg, t : t + 1], bias=ab_f[:, cg, t : t + 1],
+            )
+
+        def activate(ng, cg, t):
             if t == 0:
                 sigs[ng, cg] = work.tile([P, PACK, GROUP], F32, tag="sig", name="sig", bufs=2)
-            q = work.tile([P, GROUP], F32, tag="q", name="q", bufs=4)
-            qq = work.tile([P, GROUP], F32, tag="qq", name="qq", bufs=2)
+            q = work.tile([P, GROUP], F32, tag="q", name="q", bufs=PACK)
+            q_squared = work.tile([P, GROUP], F32, tag="q_squared", name="q_squared", bufs=2)
             beta_t = beta_f[:, cg, t : t + 1]
-            nc.scalar.activation(out=sigs[ng, cg][:, t, :], in_=acc[:], func=ACT.Sigmoid, scale=beta_t)
-            nc.scalar.activation(out=q[:], in_=acc[:], func=ACT.Tanh, scale=beta_t)
-            if pending:
-                flush_slope()
-            nc.scalar.activation(out=qq[:], in_=q[:], func=ACT.Square)
-            pending.append((ng, cg, t, qq))
+            nc.scalar.activation(out=sigs[ng, cg][:, t, :], in_=scores[ng, cg, t][:], func=ACT.Sigmoid, scale=beta_t)
+            nc.scalar.activation(out=q[:], in_=scores[ng, cg, t][:], func=ACT.Tanh, scale=beta_t)
+            if squares_waiting:
+                finish_slope()
+            nc.scalar.activation(out=q_squared[:], in_=q[:], func=ACT.Square)
+            squares_waiting.append((ng, cg, t, q_squared))
             tanhs[ng, cg, t] = q
 
         def linear(ng, cg, t):
@@ -248,193 +218,197 @@ def tile_adversarialdebiasingprojectedrepresentat_x1_kernel(
                 in1=neg_z[:, ng * GROUP : (ng + 1) * GROUP], op0=ALU.mult, op1=ALU.add,
             )
 
-        def pairs_out(stage_ap):
-            return stage_ap.rearrange("p (c i t) -> p c t i", i=2, t=PACK)
+        def pairs_out(stage_part):
+            return stage_part.rearrange("p (c i t) -> p c t i", i=2, t=PACK)
 
-        def pairs_in(src):
-            return src.rearrange("p t (c i) -> p c t i", i=2)
+        def pairs_in(slot_tile):
+            return slot_tile.rearrange("p t (c i) -> p c t i", i=2)
 
-        def scale_r1(ng, cg):
-            stage = stage_tile()
-            staged["r1", ng, cg] = stage
-            nc.vector.tensor_tensor(
-                out=pairs_out(stage[:]), in0=pairs_in(sigs[ng, cg][:]),
-                in1=beta_f[:, cg, :].unsqueeze(1).unsqueeze(3).to_broadcast([P, GROUP // 2, PACK, 2]),
-                op=ALU.mult,
-            )
-
-        def scale_r1_slot(ng, cg, t):
-            if t == 0:
-                staged["r1_slots", ng, cg] = stage_tile()
-            nc.scalar.activation(
-                out=staged["r1_slots", ng, cg][:, t * GROUP : (t + 1) * GROUP], in_=sigs[ng, cg][:, t, :],
-                func=ACT.Copy, scale=beta_f[:, cg, t : t + 1],
-            )
-
-        def weave_r1(ng, cg):
-            stage = stage_tile()
-            staged["r1", ng, cg] = stage
-            nc.scalar.copy(
-                out=stage[:].rearrange("p (c i t) -> p c t i", i=4, t=PACK),
-                in_=staged["r1_slots", ng, cg][:].rearrange("p (t c i) -> p c t i", i=4, t=PACK),
-            )
-
-        def residuals(ng, cg, t):
-            subtract_y(ng, cg, t)
-            linear(ng, cg, t)
-
-        def final_r2(ng, cg):
-            stage = stage_tile()
-            staged["r2", ng, cg] = stage
+        def stage_r2(ng, cg):
+            stage = new_stage(("r2", ng, cg))
             nc.vector.tensor_tensor(
                 out=pairs_out(stage[:]), in0=pairs_in(lins[ng, cg][:]), in1=pairs_in(slopes[ng, cg][:]), op=ALU.mult
             )
 
-        def quant_r1(ng, cg):
-            r1_q[ng, cg] = quantize(staged["r1", ng, cg], "r1_%d%d" % (ng, cg))
+        def turn_y(cg, u):
+            acc = bank(2 + u)
+            for tn in range(PACK):
+                words = y_rows[0, cg][:, tn, :].bitcast(F32)
+                nc.tensor.transpose(acc[:, tn * P : (tn + 1) * P], words[:, u::2], ident[:])
+            y_turned[cg, u] = acc
 
-        def quant_r2(ng, cg):
-            r2_q[ng, cg] = quantize(staged["r2", ng, cg], "r2_%d%d" % (ng, cg))
+        def residuals(cg, t):
+            sig = sigs[0, cg][:, t, :]
+            y_slot = y_turned[cg, t // 2][:].bitcast(BF16)[:, t % 2 :: 2]
+            nc.vector.tensor_tensor(out=sig, in0=sig, in1=y_slot, op=ALU.subtract)
+            linear(0, cg, t)
 
-        g_t, h_rows, hh_sum, hh_inv, g_rows, coefs, result, out_q = {}, {}, {}, {}, {}, {}, {}, {}
-
-        def open_g(ng, dg, j, which):
-            acc = bank(which)
-            mx_pass(acc, wt_q[0, dg], j, r1_q[ng, 0], 0)
-            opened["g", ng, dg, j] = acc
-
-        def g_mm(ng, dg, j, which):
-            if ("g", ng, dg, j) not in opened:
-                open_g(ng, dg, j, which)
-            mx_pass(opened["g", ng, dg, j], wt_q[1, dg], j, r1_q[ng, 1], 1)
-
-        def g_scale(ng, dg, j):
-            g_dj = work.tile([P, GROUP], F32, tag="g_t", name="g_t", bufs=8)
-            nc.scalar.activation(
-                out=g_dj[:], in_=opened["g", ng, dg, j][:], func=ACT.Copy, scale=gamma_f[:, dg, j : j + 1]
+        def stage_r1(cg):
+            stage = new_stage(("r1", 0, cg))
+            nc.vector.tensor_tensor(
+                out=pairs_out(stage[:]), in0=pairs_in(sigs[0, cg][:]),
+                in1=beta_f[:, cg, :].unsqueeze(1).unsqueeze(3).to_broadcast([P, GROUP // 2, PACK, 2]),
+                op=ALU.mult,
             )
-            g_t[ng, dg, j] = g_dj
 
-        def make_g(ng, dg, j, which):
-            g_mm(ng, dg, j, which)
-            g_scale(ng, dg, j)
+        def open_r1(cg, tn, which_bank):
+            acc = bank(which_bank)
+            for t in range(PACK):
+                nc.tensor.matmul(
+                    acc[:, t * P : (t + 1) * P], lhsT=y_rows[1, cg][:, tn, t::PACK], rhs=neg_ident[:],
+                    start=(t == 0), stop=False,
+                )
+            r1_sums[cg, tn] = acc
+
+        def close_r1(cg, tn):
+            nc.tensor.matmul(
+                r1_sums[cg, tn][:].rearrange("p (t m) -> p t m", t=PACK), lhsT=ident[:],
+                rhs=sigs[1, cg][:, :, tn * P : (tn + 1) * P], start=False, stop=True,
+            )
+
+        def sum_r1(cg, tn, which_bank):
+            open_r1(cg, tn, which_bank)
+            close_r1(cg, tn)
+
+        def stage_r1_sum(cg, tn):
+            stage = new_stage(("r1", 1, cg)) if tn == 0 else staged["r1", 1, cg]
+            nc.vector.tensor_tensor(
+                out=stage[:, tn * GROUP : (tn + 1) * GROUP].rearrange("p (m t) -> p m t", t=PACK),
+                in0=r1_sums[cg, tn][:].rearrange("p (t m) -> p m t", t=PACK),
+                in1=beta_f[:, cg, :].unsqueeze(1).to_broadcast([P, P, PACK]),
+                op=ALU.mult,
+            )
+
+        g_sums, h_sums, g_cols, g_rows, h_rows = {}, {}, {}, {}, {}
+        neg_dens, coef_parts, coefs, result, out_planes = {}, {}, {}, {}, {}
+
+        def open_g(ng, dg, j, which_bank):
+            g_sums[ng, dg, j] = bank(which_bank)
+            mx_pass(g_sums[ng, dg, j], ("wt", 0, dg), j, ("r1", ng, 0), 0)
+
+        def close_g(ng, dg, j):
+            mx_pass(g_sums[ng, dg, j], ("wt", 1, dg), j, ("r1", ng, 1), 1)
+
+        def scale_g(ng, dg, j):
+            g_cols[ng, dg, j] = work.tile([P, GROUP], F32, tag="g_cols", name="g_cols", bufs=GROUPS * PACK)
+            nc.scalar.activation(
+                out=g_cols[ng, dg, j][:], in_=g_sums[ng, dg, j][:], func=ACT.Copy, scale=gamma_f[:, dg, j : j + 1]
+            )
+
+        def make_g(ng, dg, j, which_bank):
+            open_g(ng, dg, j, which_bank)
+            close_g(ng, dg, j)
+            scale_g(ng, dg, j)
 
         def open_h(ng, t, dg, first_bank):
-            acc = bank(first_bank + dg)
-            mx_pass(acc, r2_q[ng, 0], t, wt_q[0, dg], 0)
-            opened["h", ng, t, dg] = acc
+            h_sums[ng, t, dg] = bank(first_bank + dg)
+            mx_pass(h_sums[ng, t, dg], ("r2", ng, 0), t, ("wt", 0, dg), 0)
+
+        def close_h(ng, t, dg):
+            mx_pass(h_sums[ng, t, dg], ("r2", ng, 1), t, ("wt", 1, dg), 1)
 
         def h_mm(ng, t, first_bank):
             for dg in range(GROUPS):
-                if ("h", ng, t, dg) not in opened:
-                    open_h(ng, t, dg, first_bank)
-                mx_pass(opened["h", ng, t, dg], r2_q[ng, 1], t, wt_q[1, dg], 1)
+                open_h(ng, t, dg, first_bank)
+                close_h(ng, t, dg)
 
-        def natural(acc):
+        def in_order(acc):
             return acc[:].rearrange("p (j m) -> p m j", j=PACK)
 
-        def split(row_ap):
-            return row_ap.rearrange("p (m j) -> p m j", j=PACK)
+        def split(row_part):
+            return row_part.rearrange("p (m j) -> p m j", j=PACK)
 
-        def h_scale(ng, t):
-            h = work.tile([P, D], F32, tag="h", name="h", bufs=4)
+        def scale_h(ng, t):
+            h = work.tile([P, D], F32, tag="h", name="h", bufs=PACK)
             for dg in range(GROUPS):
                 cols = slice(dg * GROUP, (dg + 1) * GROUP)
                 nc.vector.tensor_tensor(
-                    out=split(h[:, cols]), in0=natural(opened["h", ng, t, dg]), in1=split(gamma_all[:, cols]), op=ALU.mult
+                    out=split(h[:, cols]), in0=in_order(h_sums[ng, t, dg]), in1=split(gamma_all[:, cols]), op=ALU.mult
                 )
             h_rows[ng, t] = h
 
-        def make_h(ng, t, first_bank):
-            h_mm(ng, t, first_bank)
-            h_scale(ng, t)
-
         def norm_h(ng, t):
-            squares = work.tile([P, D], BF16, tag="squares", name="squares", bufs=2)
+            h_squared = work.tile([P, D], BF16, tag="h_squared", name="h_squared", bufs=2)
             hh = small.tile([P, 1], F32, tag="hh", name="hh")
-            nc.scalar.activation(out=squares[:], in_=h_rows[ng, t][:], func=ACT.Square, accum_out=hh[:])
-            hh_sum[ng, t] = hh
+            nc.scalar.activation(out=h_squared[:], in_=h_rows[ng, t][:], func=ACT.Square, accum_out=hh[:])
+            neg_den = small.tile([P, 1], F32, tag="neg_den", name="neg_den")
+            nc.gpsimd.tensor_scalar(out=neg_den[:], in0=hh[:], scalar1=-1.0, scalar2=-EPS, op0=ALU.mult, op1=ALU.add)
+            neg_dens[ng, t] = neg_den
 
         def turn_g(ng, t, first_bank):
             for dg in range(GROUPS):
                 acc = bank(first_bank + dg)
                 for j in range(PACK):
-                    nc.tensor.transpose(acc[:, j * P : (j + 1) * P], g_t[ng, dg, j][:, t * P : (t + 1) * P], ident[:])
+                    nc.tensor.transpose(acc[:, j * P : (j + 1) * P], g_cols[ng, dg, j][:, t * P : (t + 1) * P], ident[:])
                 g_rows[ng, t, dg] = acc
 
         def scale_add(ng, out, value, factor, term):
             if ng == 0:
-                nc.vector.tensor_scalar(
+                nc.gpsimd.tensor_scalar(
                     out=out[:], in0=value[:], scalar1=factor[:], scalar2=term[:], op0=ALU.mult, op1=ALU.add
                 )
             else:
                 nc.scalar.activation(out=out[:], in_=value[:], func=ACT.Identity, scale=factor[:], bias=term[:])
 
         def dot_gh(ng, t):
-            h = h_rows[ng, t]
-            den = small.tile([P, 1], F32, tag="den", name="den")
-            nc.vector.tensor_scalar(out=den[:], in0=hh_sum[ng, t][:], scalar1=-1.0, scalar2=-EPS, op0=ALU.mult, op1=ALU.add)
-            inv = small.tile([P, 1], F32, tag="inv", name="inv")
+            neg_inv = small.tile([P, 1], F32, tag="neg_inv", name="neg_inv")
             part = small.tile([P, 1], F32, tag="part", name="part")
             sums = []
             for dg in range(GROUPS):
                 products = work.tile([P, GROUP], BF16, tag="products", name="products", bufs=2)
                 gh = small.tile([P, 1], F32, tag="gh%d" % dg, name="gh")
                 nc.vector.scalar_tensor_tensor(
-                    out=split(products[:]), in0=natural(g_rows[ng, t, dg]), scalar=1.0,
-                    in1=split(h[:, dg * GROUP : (dg + 1) * GROUP]), op0=ALU.mult, op1=ALU.mult, accum_out=gh[:],
+                    out=split(products[:]), in0=in_order(g_rows[ng, t, dg]), scalar=1.0,
+                    in1=split(h_rows[ng, t][:, dg * GROUP : (dg + 1) * GROUP]),
+                    op0=ALU.mult, op1=ALU.mult, accum_out=gh[:],
                 )
                 sums.append(gh)
                 if dg == 0:
-                    nc.vector.reciprocal(out=inv[:], in_=den[:])
-            scale_add(ng, part, sums[0], inv, neg_half)
-            hh_inv[ng, t] = (inv, part, sums[1])
+                    nc.vector.reciprocal(out=neg_inv[:], in_=neg_dens[ng, t][:])
+            scale_add(ng, part, sums[0], neg_inv, neg_half)
+            coef_parts[ng, t] = (neg_inv, part, sums[1])
 
         def make_coef(ng, t):
-            inv, part, gh = hh_inv[ng, t]
-            coef = small.tile([P, 1], F32, tag="coef", name="coef")
-            scale_add(ng, coef, gh, inv, part)
-            coefs[ng, t] = coef
+            neg_inv, part, gh = coef_parts[ng, t]
+            coefs[ng, t] = small.tile([P, 1], F32, tag="coef", name="coef")
+            scale_add(ng, coefs[ng, t], gh, neg_inv, part)
 
         def project_half(ng, t, dg):
             if ng not in result:
                 result[ng] = work.tile([P, PACK, D], F32, tag="result", name="result")
-            res = result[ng]
             rows = out_0[ng * GROUP : (ng + 1) * GROUP, :].rearrange("(p t) d -> p t d", t=PACK)
             cols = slice(dg * GROUP, (dg + 1) * GROUP)
             nc.vector.scalar_tensor_tensor(
-                out=split(res[:, t, cols]), in0=split(h_rows[ng, t][:, cols]), scalar=coefs[ng, t][:],
-                in1=natural(g_rows[ng, t, dg]), op0=ALU.mult, op1=ALU.add,
+                out=split(result[ng][:, t, cols]), in0=split(h_rows[ng, t][:, cols]), scalar=coefs[ng, t][:],
+                in1=in_order(g_rows[ng, t, dg]), op0=ALU.mult, op1=ALU.add,
             )
-            nc.sync.dma_start(out=rows[:, t, cols], in_=res[:, t, cols])
+            nc.sync.dma_start(out=rows[:, t, cols], in_=result[ng][:, t, cols])
 
         def project(ng, t):
             for dg in range(GROUPS):
                 project_half(ng, t, dg)
 
         def round_out(ng, dg, copy, first, width):
-            if ("out", ng, dg) not in staged:
-                staged["out", ng, dg] = stage_tile()
-            stage = staged["out", ng, dg]
+            stage = new_stage(("out", ng, dg)) if first == 0 else staged["out", ng, dg]
             col = dg * GROUP + first
             copy(
                 out=pairs_out(stage[:, PACK * first : PACK * (first + width)]),
                 in_=pairs_in(result[ng][:, :, col : col + width]),
             )
 
-        def quant_out(ng, dg):
+        def quantize_out(ng, dg):
             if dg == 0:
-                codes_new = mx.tile([P, D], U32, tag="out_codes", name="out_codes", align_bytes=64)
-                scales_new = mx.tile([P, D], U8, tag="out_scales", name="out_scales", align_bytes=64)
-                out_q[ng] = (codes_new, scales_new)
-            codes, scales = out_q[ng]
+                new_codes = mx.tile([P, D], U32, tag="out_codes", name="out_codes", align_bytes=64)
+                new_scales = mx.tile([P, D], U8, tag="out_scales", name="out_scales", align_bytes=64)
+                out_planes[ng] = (new_codes, new_scales)
+            codes, scales = out_planes[ng]
             words = out_1[ng].rearrange("p m t -> p (m t)").bitcast(I32)
             cols = slice(dg * GROUP, (dg + 1) * GROUP)
             nc.vector.quantize_mx(out=codes[:, cols].bitcast(FP8X4), scales=scales[:, cols], in_=staged["out", ng, dg][:])
             nc.sync.dma_start(out=words[:, cols], in_=codes[:, cols].bitcast(I32))
 
         def store_scales(ng, queues):
-            scales = out_q[ng][1]
+            scales = out_planes[ng][1]
             for quad in range(4):
                 queues[quad % len(queues)].dma_start(
                     out=out_2[ng, 4 * quad : 4 * quad + 4, :].bitcast(I32),
@@ -444,206 +418,201 @@ def tile_adversarialdebiasingprojectedrepresentat_x1_kernel(
         on_scalar, on_vector = nc.scalar.copy, nc.vector.tensor_copy
         every_slot = slice(0, PACK)
 
+
         sort_w(0, 0, on_scalar, every_slot)
         turn("x", x_rows, (0, 0), 4)
         turn("x", x_rows, (0, 1), 6)
         scale_x(0, 0)
-        sort_w(1, 0, on_scalar, slice(0, 3))
-        neg_z = const.tile([P, N], BF16, name="neg_z")
-        for ng in range(GROUPS):
-            acc = bank(4 + ng)
-            cols = slice(ng * GROUP, (ng + 1) * GROUP)
-            nc.tensor.matmul(
-                acc[:], lhsT=neg_ident[:, 0:1].to_broadcast([P, P]), rhs=z_row[:, cols], start=True, stop=True
-            )
-            nc.scalar.copy(
-                out=neg_z[:, cols].rearrange("p (t m) -> p t m", t=PACK),
-                in_=acc[:].rearrange("p (m t) -> p t m", t=PACK),
-            )
-
-        quant_x(0, 0)
+        sort_w(1, 0, on_scalar, slice(0, PACK - 1))
+        spread_z(4)
+        quantize("x", 0, 0)
         scale_x(0, 1)
-        quant_w(0, 0)
-        sort_w(1, 0, on_vector, slice(3, 4))
-        quant_x(0, 1)
-        quant_w(1, 0)
-        x_rows[1, 1] = load_rows(x, 1, 1, "xy_rows", 4)
-        y_rows[0, 1] = load_rows(y, 0, 1, "xy_rows", 4)
-        turn_y(0, 0, 0)
+        quantize("w", 0, 0)
+        sort_w(1, 0, on_vector, slice(PACK - 1, PACK))
+        quantize("x", 0, 1)
+        quantize("w", 1, 0)
+        load_x(1, 1)
+        load_y(0, 1)
+
+        turn_y(0, 0)
         score_mm(0, 0, 0)
         score_mm(0, 0, 1)
-        turn_y(0, 0, 1)
-        y_rows[1, 0] = load_rows(y, 1, 0, "xy_rows", 4)
-        sort_w(0, 1, on_vector, every_slot)
-        sort_w(1, 1, on_vector, every_slot)
-        score(0, 0, 0)
+        turn_y(0, 1)
+        load_y(1, 0)
+        for dg in range(GROUPS):
+            sort_w(dg, 1, on_vector, every_slot)
+        activate(0, 0, 0)
         score_mm(0, 0, 2)
         turn("x", x_rows, (1, 0), 4)
-        y_rows[1, 1] = load_rows(y, 1, 1, "xy_rows", 4)
-        gamma_all = const.tile([P, D], BF16, name="gamma_all")
+        load_y(1, 1)
         nc.sync.dma_start(out=gamma_all[:], in_=gamma.partition_broadcast(P))
-        residuals(0, 0, 0)
-        score(0, 0, 1)
+        residuals(0, 0)
+        activate(0, 0, 1)
         score_mm(0, 0, 3)
         turn("x", x_rows, (1, 1), 6)
-        quant_w(0, 1)
-        quant_w(1, 1)
-        residuals(0, 0, 1)
-        score(0, 0, 2)
+        for dg in range(GROUPS):
+            quantize("w", dg, 1)
+        residuals(0, 1)
+        activate(0, 0, 2)
         score_mm(0, 1, 0)
-        turn_y(0, 1, 0)
+        turn_y(1, 0)
         scale_x(1, 0)
-        residuals(0, 0, 2)
-        quant_x(1, 0)
-        score(0, 0, 3)
+        residuals(0, 2)
+        quantize("x", 1, 0)
+        activate(0, 0, 3)
         score_mm(0, 1, 1)
         turn("w", w_rows, (0, 0), 4)
         scale_x(1, 1)
-        residuals(0, 0, 3)
-        quant_x(1, 1)
-        score(0, 1, 0)
+        residuals(0, 3)
+        quantize("x", 1, 1)
+
+        activate(0, 1, 0)
         score_mm(0, 1, 2)
-        turn_y(0, 1, 1)
+        turn_y(1, 1)
         turn("w", w_rows, (1, 0), 6)
-        scale_r1(0, 0)
-        score(0, 1, 1)
+        stage_r1(0)
+        activate(0, 1, 1)
         score_mm(0, 1, 3)
         copy_wt(0, 0)
         turn("w", w_rows, (0, 1), 4)
-        final_r2(0, 0)
-        score(0, 1, 2)
+        stage_r2(0, 0)
+        activate(0, 1, 2)
         score_mm(1, 0, 0)
         copy_wt(0, 1)
         turn("w", w_rows, (1, 1), 6)
-        quant_r1(0, 0)
-        residuals(0, 1, 0)
-        quant_r2(0, 0)
-        residuals(0, 1, 1)
-        score(0, 1, 3)
+        quantize("r1", 0, 0)
+        residuals(1, 0)
+        quantize("r2", 0, 0)
+        residuals(1, 1)
+        activate(0, 1, 3)
         score_mm(1, 0, 1)
-        quant_wt(0, 0)
-        residuals(0, 1, 2)
-        quant_wt(0, 1)
+        quantize("wt", 0, 0)
+        residuals(1, 2)
+        quantize("wt", 0, 1)
         copy_wt(1, 0)
         for dg in range(GROUPS):
             open_h(0, 0, dg, 4)
-        score(1, 0, 0)
+
+        activate(1, 0, 0)
         score_mm(1, 0, 2)
-        residuals(0, 1, 3)
+        residuals(1, 3)
         copy_wt(1, 1)
-        open_g(0, 0, 0, 6)
-        open_g(0, 0, 1, 7)
-        open_g(0, 0, 2, 2)
-        open_g(0, 0, 3, 3)
-        scale_r1(0, 1)
-        score(1, 0, 1)
+        for j, which_bank in enumerate((6, 7, 2, 3)):
+            open_g(0, 0, j, which_bank)
+        stage_r1(1)
+        activate(1, 0, 1)
         score_mm(1, 0, 3)
-        quant_wt(1, 0)
-        final_r2(0, 1)
-        score(1, 0, 2)
-        quant_r1(0, 1)
-        g_mm(0, 0, 0, 6)
-        g_mm(0, 0, 1, 7)
-        quant_wt(1, 1)
-        quant_r2(0, 1)
-        h_mm(0, 0, 4)
-        g_mm(0, 0, 2, 2)
-        g_mm(0, 0, 3, 3)
-        score(1, 0, 3)
+        quantize("wt", 1, 0)
+        stage_r2(0, 1)
+        activate(1, 0, 2)
+        quantize("r1", 0, 1)
+        close_g(0, 0, 0)
+        close_g(0, 0, 1)
+        quantize("wt", 1, 1)
+        quantize("r2", 0, 1)
+        for dg in range(GROUPS):
+            close_h(0, 0, dg)
+        close_g(0, 0, 2)
+        close_g(0, 0, 3)
+        activate(1, 0, 3)
         linear(1, 0, 0)
-        h_scale(0, 0)
+        scale_h(0, 0)
         h_mm(0, 1, 4)
-        g_scale(0, 0, 0)
-        flush_slope()
+        scale_g(0, 0, 0)
+        finish_slope()
         for j in range(1, PACK):
-            g_scale(0, 0, j)
+            scale_g(0, 0, j)
         linear(1, 0, 1)
-        h_scale(0, 1)
+        scale_h(0, 1)
         h_mm(0, 2, 4)
         make_g(0, 1, 0, 0)
         make_g(0, 1, 1, 1)
         linear(1, 0, 2)
-        h_scale(0, 2)
+        scale_h(0, 2)
         h_mm(0, 3, 4)
         make_g(0, 1, 2, 6)
         make_g(0, 1, 3, 7)
         norm_h(0, 0)
         linear(1, 0, 3)
-        h_scale(0, 3)
+        scale_h(0, 3)
+
         score_mm(1, 1, 0)
         turn_g(0, 0, 4)
         score_mm(1, 1, 1)
         turn_g(0, 1, 6)
-        close_r1(1, 0, 0)
-        close_r1(1, 0, 1)
+        sum_r1(0, 0, 2)
+        sum_r1(0, 1, 3)
         norm_h(0, 1)
-        score(1, 1, 0)
+        activate(1, 1, 0)
         score_mm(1, 1, 2)
-        final_r2(1, 0)
+        stage_r2(1, 0)
         dot_gh(0, 0)
-        quant_r2(1, 0)
+        quantize("r2", 1, 0)
         make_coef(0, 0)
         dot_gh(0, 1)
-        final_r1(1, 0, 0)
-        close_r1(1, 0, 2)
+        stage_r1_sum(0, 0)
+        sum_r1(0, 2, 2)
         make_coef(0, 1)
-        final_r1(1, 0, 1)
+        stage_r1_sum(0, 1)
         norm_h(0, 2)
-        score(1, 1, 1)
+        activate(1, 1, 1)
         score_mm(1, 1, 3)
         project(0, 0)
         turn_g(0, 2, 4)
-        close_r1(1, 0, 3)
+        sum_r1(0, 3, 3)
         project(0, 1)
         turn_g(0, 3, 6)
-        final_r1(1, 0, 2)
-        open_r1(1, 1, 0)
+        stage_r1_sum(0, 2)
+        open_r1(1, 0, 2)
         dot_gh(0, 2)
-        final_r1(1, 0, 3)
-        open_r1(1, 1, 1)
+        stage_r1_sum(0, 3)
+        open_r1(1, 1, 3)
         norm_h(0, 3)
-        score(1, 1, 2)
-        score(1, 1, 3)
-        for tn in range(PACK):
-            close_r1(1, 1, tn)
-        flush_slope()
+        activate(1, 1, 2)
+        activate(1, 1, 3)
+        close_r1(1, 0)
+        close_r1(1, 1)
+        sum_r1(1, 2, 0)
+        sum_r1(1, 3, 1)
+        finish_slope()
         make_coef(0, 2)
         dot_gh(0, 3)
         project(0, 2)
         make_coef(0, 3)
-        quant_r1(1, 0)
+        quantize("r1", 1, 0)
         project(0, 3)
         for dg in range(GROUPS):
             round_out(0, dg, on_scalar, 0, GROUP)
+
         for t in range(2):
             for dg in range(GROUPS):
                 open_h(1, t, dg, 4 + 2 * t)
         for tn in range(PACK):
             if tn < PACK - 1:
                 linear(1, 1, tn)
-            final_r1(1, 1, tn)
+            stage_r1_sum(1, tn)
             open_g(1, 0, (tn + 2) % PACK, (tn + 2) % PACK)
-        linear(1, 1, 3)
-        quant_r1(1, 1)
-        for dg in range(GROUPS):
-            for j in range(PACK):
-                make_g(1, dg, j, j)
-        final_r2(1, 1)
-        quant_out(0, 0)
-        quant_r2(1, 1)
-        h_mm(1, 0, 4)
-        h_mm(1, 1, 6)
-        quant_out(0, 1)
+        linear(1, 1, PACK - 1)
+        quantize("r1", 1, 1)
+        for j in range(PACK):
+            close_g(1, 0, j)
+            scale_g(1, 0, j)
+        for j in range(PACK):
+            make_g(1, 1, j, j)
+        stage_r2(1, 1)
+        quantize_out(0, 0)
+        quantize("r2", 1, 1)
+        for t in range(2):
+            for dg in range(GROUPS):
+                close_h(1, t, dg)
+        quantize_out(0, 1)
         store_scales(0, [nc.sync])
-        h_scale(1, 0)
-        norm_h(1, 0)
-        h_mm(1, 2, 4)
-        h_scale(1, 1)
-        norm_h(1, 1)
-        h_mm(1, 3, 6)
-        for t in range(2, PACK):
-            h_scale(1, t)
+        for t in range(PACK):
+            scale_h(1, t)
             norm_h(1, t)
+            if t + 2 < PACK:
+                h_mm(1, t + 2, 4 + 2 * t)
+
         for t in range(PACK):
             turn_g(1, t, 2 * t)
         for t in range(PACK):
@@ -656,6 +625,6 @@ def tile_adversarialdebiasingprojectedrepresentat_x1_kernel(
             project_half(1, t, 1)
         round_out(1, 1, on_vector, 0, GROUP // 2)
         round_out(1, 1, on_scalar, GROUP // 2, GROUP // 2)
-        quant_out(1, 0)
-        quant_out(1, 1)
+        for dg in range(GROUPS):
+            quantize_out(1, dg)
         store_scales(1, [nc.scalar, nc.sync])

from contextlib import ExitStack

import concourse.mybir as mybir
from concourse.masks import make_identity

N, D, C = 1024, 1024, 1024
FLOPS = 3 * 2 * N * D * C

F32 = mybir.dt.float32
BF16 = mybir.dt.bfloat16
U32 = mybir.dt.uint32
I32 = mybir.dt.int32
U8 = mybir.dt.uint8
FP8X4 = mybir.dt.float8_e4m3fn_x4
ACT = mybir.ActivationFunctionType
ALU = mybir.AluOpType

P = 128
PACK = 4
GROUP = P * PACK
GROUPS = 2
HALF_STAGE = GROUP * PACK // 2
EPS = 1e-6

ROW_TILES = 4
STAGE_TILES = 4


def tile_adversarialdebiasingprojectedrepresentat_x1_kernel(
    tc, x, gamma, w, beta, y, z, a, out_0, out_1, out_2
):
    nc = tc.nc
    with ExitStack() as ctx:
        const = ctx.enter_context(tc.tile_pool(name="const", bufs=1))
        raw = ctx.enter_context(tc.tile_pool(name="raw", bufs=1))
        mx = ctx.enter_context(tc.tile_pool(name="mx", bufs=1))
        work = ctx.enter_context(tc.tile_pool(name="work", bufs=1))
        small = ctx.enter_context(tc.tile_pool(name="small", bufs=PACK))
        psum = ctx.enter_context(tc.psum_pool(name="psum", bufs=1))

        ctx.enter_context(tc.manual_schedule())

        def bank(i):
            return psum.tile([P, GROUP], F32, tag="bank%d" % i, name="bank%d" % i)

        def load_rows(src, row_group, col_group, tag, bufs):
            rows = raw.tile([P, PACK, GROUP], BF16, tag=tag, name=tag, bufs=bufs)
            view = src[row_group * GROUP : (row_group + 1) * GROUP, col_group * GROUP : (col_group + 1) * GROUP]
            nc.sync.dma_start(out=rows[:], in_=view.rearrange("(p t) c -> p t c", t=PACK))
            return rows

        def load_slots(vec, name, queue):
            slots = const.tile([P, GROUPS, PACK], BF16, name=name)
            queue.dma_start(out=slots[:], in_=vec.rearrange("(g p t) -> p g t", g=GROUPS, t=PACK))
            return slots

        w_rows, x_rows, y_rows = {}, {}, {}

        def load_w(dg, cg):
            w_rows[dg, cg] = load_rows(w, dg, cg, "w_rows", GROUPS * GROUPS)

        def load_x(ng, dg):
            x_rows[ng, dg] = load_rows(x, ng, dg, "xy_rows", ROW_TILES)

        def load_y(ng, cg):
            y_rows[ng, cg] = load_rows(y, ng, cg, "xy_rows", ROW_TILES)

        gamma_slots = load_slots(gamma, "gamma_slots", nc.scalar)
        z_row = const.tile([P, N], BF16)
        nc.vector.memset(z_row[:], 0.0)
        nc.scalar.dma_start(out=z_row[0:1, :], in_=z.rearrange("(o n) -> o n", o=1))
        for dg in range(GROUPS):
            load_x(0, dg)
            load_w(dg, 0)
        beta_slots = load_slots(beta, "beta_slots", nc.sync)
        a_slots = load_slots(a, "a_slots", nc.sync)
        load_y(0, 0)
        for dg in range(GROUPS):
            load_w(dg, 1)
        load_x(1, 0)

        ident = const.tile([P, P], F32)
        make_identity(nc, ident[:])
        neg_ident = const.tile([P, P], BF16)
        nc.vector.tensor_scalar(out=neg_ident[:], in0=ident[:], scalar1=-1.0, scalar2=None, op0=ALU.mult)
        neg_half = const.tile([P, 1], F32)
        nc.vector.memset(neg_half[:], -0.5)

        gamma_f = const.tile([P, GROUPS, PACK], F32)
        beta_f = const.tile([P, GROUPS, PACK], F32)
        a_f = const.tile([P, GROUPS, PACK], F32)
        ab_f = const.tile([P, GROUPS, PACK], F32)
        neg_ab_f = const.tile([P, GROUPS, PACK], F32)
        nc.gpsimd.tensor_copy(out=gamma_f[:], in_=gamma_slots[:])
        nc.gpsimd.tensor_copy(out=beta_f[:], in_=beta_slots[:])
        nc.gpsimd.tensor_copy(out=a_f[:], in_=a_slots[:])
        nc.gpsimd.tensor_tensor(out=ab_f[:], in0=a_slots[:], in1=beta_slots[:], op=ALU.mult)
        nc.gpsimd.tensor_scalar(out=neg_ab_f[:], in0=ab_f[:], scalar1=-1.0, scalar2=0.0, op0=ALU.mult, op1=ALU.add)

        neg_z = const.tile([P, N], BF16)
        gamma_all = const.tile([P, D], BF16)

        def spread_z(first_bank):
            for ng in range(GROUPS):
                acc = bank(first_bank + ng)
                cols = slice(ng * GROUP, (ng + 1) * GROUP)
                nc.tensor.matmul(
                    acc[:], lhsT=neg_ident[:, 0:1].to_broadcast([P, P]), rhs=z_row[:, cols], start=True, stop=True
                )
                nc.scalar.copy(
                    out=neg_z[:, cols].rearrange("p (t m) -> p t m", t=PACK),
                    in_=acc[:].rearrange("p (m t) -> p t m", t=PACK),
                )

        staged = {}
        quantised = {}

        def new_stage(key):
            staged[key] = work.tile(
                [P, GROUP * PACK], BF16, tag="stage", name="stage", bufs=STAGE_TILES, align_bytes=64
            )
            return staged[key]

        def quantize(kind, i, j):
            name = "%s_%d%d" % (kind, i, j)
            codes = mx.tile([P, GROUP], U32, name=name + "_codes", align_bytes=64)
            scales = mx.tile([P, GROUP], U8, name=name + "_scales", align_bytes=64)
            nc.vector.quantize_mx(out=codes[:].bitcast(FP8X4), scales=scales[:], in_=staged[kind, i, j][:])
            quantised[kind, i, j] = (codes, scales)

        def mx_pass(acc, stationary, t, moving, group):
            cols = slice(t * P, (t + 1) * P)
            nc.tensor.matmul_mx(
                out=acc[:],
                lhsT=quantised[stationary][0][:, cols].bitcast(FP8X4),
                lhsT_scale=quantised[stationary][1][:, cols],
                rhs=quantised[moving][0][:].bitcast(FP8X4),
                rhs_scale=quantised[moving][1][:],
                start=(group == 0),
                stop=(group == GROUPS - 1),
            )

        def sort_w(dg, cg, copy, slots):
            stage = staged[("w", dg, cg)] if ("w", dg, cg) in staged else new_stage(("w", dg, cg))
            copy(
                out=stage[:].rearrange("p (t m j) -> p t m j", t=PACK, j=PACK)[:, slots],
                in_=w_rows[dg, cg][:].rearrange("p j (m t) -> p t m j", t=PACK)[:, slots],
            )

        turned = {}

        def turn(kind, rows, key, first_bank):
            for half in range(2):
                acc = bank(first_bank + half)
                for u in range(2):
                    for tt in range(2):
                        words = rows[key][:, 2 * half + tt, :].bitcast(F32)
                        col = (2 * u + tt) * P
                        nc.tensor.transpose(acc[:, col : col + P], words[:, u::2], ident[:])
                turned[kind, key, half] = acc

        def scale_x(ng, dg):
            stage = new_stage(("x", ng, dg))
            factors = gamma_slots[:, dg, :].rearrange("p (u e) -> p u e", e=2)
            for half in range(2):
                nc.vector.tensor_tensor(
                    out=stage[:, half * HALF_STAGE : (half + 1) * HALF_STAGE].rearrange("p (n u e) -> p n u e", u=2, e=2),
                    in0=turned["x", (ng, dg), half][:].bitcast(BF16).rearrange("p (u n e) -> p n u e", u=2, e=2),
                    in1=factors.unsqueeze(1).to_broadcast([P, 2 * P, 2, 2]),
                    op=ALU.mult,
                )

        def copy_wt(cg, dg):
            stage = new_stage(("wt", cg, dg))
            for half in range(2):
                nc.scalar.copy(
                    out=stage[:, half * HALF_STAGE : (half + 1) * HALF_STAGE].bitcast(F32).rearrange("p (n u) -> p n u", u=2),
                    in_=turned["w", (dg, cg), half][:].rearrange("p (u n) -> p n u", u=2),
                )

        scores, tanhs, sigs, slopes, lins, y_turned, r1_sums = {}, {}, {}, {}, {}, {}, {}
        squares_waiting = []

        def score_mm(ng, cg, t):
            acc = bank(t % 2)
            for dg in range(GROUPS):
                mx_pass(acc, ("w", dg, cg), t, ("x", ng, dg), dg)
            scores[ng, cg, t] = acc

        def finish_slope():
            ng, cg, t, q_squared = squares_waiting.pop()
            if t == 0:
                slopes[ng, cg] = work.tile([P, PACK, GROUP], F32, tag="slope", name="slope", bufs=2)
            nc.scalar.activation(
                out=slopes[ng, cg][:, t, :], in_=q_squared[:], func=ACT.Identity,
                scale=neg_ab_f[:, cg, t : t + 1], bias=ab_f[:, cg, t : t + 1],
            )

        def activate(ng, cg, t):
            if t == 0:
                sigs[ng, cg] = work.tile([P, PACK, GROUP], F32, tag="sig", name="sig", bufs=2)
            q = work.tile([P, GROUP], F32, tag="q", name="q", bufs=PACK)
            q_squared = work.tile([P, GROUP], F32, tag="q_squared", name="q_squared", bufs=2)
            beta_t = beta_f[:, cg, t : t + 1]
            nc.scalar.activation(out=sigs[ng, cg][:, t, :], in_=scores[ng, cg, t][:], func=ACT.Sigmoid, scale=beta_t)
            nc.scalar.activation(out=q[:], in_=scores[ng, cg, t][:], func=ACT.Tanh, scale=beta_t)
            if squares_waiting:
                finish_slope()
            nc.scalar.activation(out=q_squared[:], in_=q[:], func=ACT.Square)
            squares_waiting.append((ng, cg, t, q_squared))
            tanhs[ng, cg, t] = q

        def linear(ng, cg, t):
            if t == 0:
                lins[ng, cg] = work.tile([P, PACK, GROUP], F32, tag="lin", name="lin")
            nc.vector.scalar_tensor_tensor(
                out=lins[ng, cg][:, t, :], in0=tanhs[ng, cg, t][:], scalar=a_f[:, cg, t : t + 1],
                in1=neg_z[:, ng * GROUP : (ng + 1) * GROUP], op0=ALU.mult, op1=ALU.add,
            )

        def pairs_out(stage_part):
            return stage_part.rearrange("p (c i t) -> p c t i", i=2, t=PACK)

        def pairs_in(slot_tile):
            return slot_tile.rearrange("p t (c i) -> p c t i", i=2)

        def stage_r2(ng, cg):
            stage = new_stage(("r2", ng, cg))
            nc.vector.tensor_tensor(
                out=pairs_out(stage[:]), in0=pairs_in(lins[ng, cg][:]), in1=pairs_in(slopes[ng, cg][:]), op=ALU.mult
            )

        def turn_y(cg, u):
            acc = bank(2 + u)
            for tn in range(PACK):
                words = y_rows[0, cg][:, tn, :].bitcast(F32)
                nc.tensor.transpose(acc[:, tn * P : (tn + 1) * P], words[:, u::2], ident[:])
            y_turned[cg, u] = acc

        def residuals(cg, t):
            sig = sigs[0, cg][:, t, :]
            y_slot = y_turned[cg, t // 2][:].bitcast(BF16)[:, t % 2 :: 2]
            nc.vector.tensor_tensor(out=sig, in0=sig, in1=y_slot, op=ALU.subtract)
            linear(0, cg, t)

        def stage_r1(cg):
            stage = new_stage(("r1", 0, cg))
            nc.vector.tensor_tensor(
                out=pairs_out(stage[:]), in0=pairs_in(sigs[0, cg][:]),
                in1=beta_f[:, cg, :].unsqueeze(1).unsqueeze(3).to_broadcast([P, GROUP // 2, PACK, 2]),
                op=ALU.mult,
            )

        def open_r1(cg, tn, which_bank):
            acc = bank(which_bank)
            for t in range(PACK):
                nc.tensor.matmul(
                    acc[:, t * P : (t + 1) * P], lhsT=y_rows[1, cg][:, tn, t::PACK], rhs=neg_ident[:],
                    start=(t == 0), stop=False,
                )
            r1_sums[cg, tn] = acc

        def close_r1(cg, tn):
            nc.tensor.matmul(
                r1_sums[cg, tn][:].rearrange("p (t m) -> p t m", t=PACK), lhsT=ident[:],
                rhs=sigs[1, cg][:, :, tn * P : (tn + 1) * P], start=False, stop=True,
            )

        def sum_r1(cg, tn, which_bank):
            open_r1(cg, tn, which_bank)
            close_r1(cg, tn)

        def stage_r1_sum(cg, tn):
            stage = new_stage(("r1", 1, cg)) if tn == 0 else staged["r1", 1, cg]
            nc.vector.tensor_tensor(
                out=stage[:, tn * GROUP : (tn + 1) * GROUP].rearrange("p (m t) -> p m t", t=PACK),
                in0=r1_sums[cg, tn][:].rearrange("p (t m) -> p m t", t=PACK),
                in1=beta_f[:, cg, :].unsqueeze(1).to_broadcast([P, P, PACK]),
                op=ALU.mult,
            )

        g_sums, h_sums, g_cols, g_rows, h_rows = {}, {}, {}, {}, {}
        neg_dens, coef_parts, coefs, result, out_planes = {}, {}, {}, {}, {}

        def open_g(ng, dg, j, which_bank):
            g_sums[ng, dg, j] = bank(which_bank)
            mx_pass(g_sums[ng, dg, j], ("wt", 0, dg), j, ("r1", ng, 0), 0)

        def close_g(ng, dg, j):
            mx_pass(g_sums[ng, dg, j], ("wt", 1, dg), j, ("r1", ng, 1), 1)

        def scale_g(ng, dg, j):
            g_cols[ng, dg, j] = work.tile([P, GROUP], F32, tag="g_cols", name="g_cols", bufs=GROUPS * PACK)
            nc.scalar.activation(
                out=g_cols[ng, dg, j][:], in_=g_sums[ng, dg, j][:], func=ACT.Copy, scale=gamma_f[:, dg, j : j + 1]
            )

        def make_g(ng, dg, j, which_bank):
            open_g(ng, dg, j, which_bank)
            close_g(ng, dg, j)
            scale_g(ng, dg, j)

        def open_h(ng, t, dg, first_bank):
            h_sums[ng, t, dg] = bank(first_bank + dg)
            mx_pass(h_sums[ng, t, dg], ("r2", ng, 0), t, ("wt", 0, dg), 0)

        def close_h(ng, t, dg):
            mx_pass(h_sums[ng, t, dg], ("r2", ng, 1), t, ("wt", 1, dg), 1)

        def h_mm(ng, t, first_bank):
            for dg in range(GROUPS):
                open_h(ng, t, dg, first_bank)
                close_h(ng, t, dg)

        def in_order(acc):
            return acc[:].rearrange("p (j m) -> p m j", j=PACK)

        def split(row_part):
            return row_part.rearrange("p (m j) -> p m j", j=PACK)

        def scale_h(ng, t):
            h = work.tile([P, D], F32, tag="h", name="h", bufs=PACK)
            for dg in range(GROUPS):
                cols = slice(dg * GROUP, (dg + 1) * GROUP)
                nc.vector.tensor_tensor(
                    out=split(h[:, cols]), in0=in_order(h_sums[ng, t, dg]), in1=split(gamma_all[:, cols]), op=ALU.mult
                )
            h_rows[ng, t] = h

        def norm_h(ng, t):
            h_squared = work.tile([P, D], BF16, tag="h_squared", name="h_squared", bufs=2)
            hh = small.tile([P, 1], F32, tag="hh", name="hh")
            nc.scalar.activation(out=h_squared[:], in_=h_rows[ng, t][:], func=ACT.Square, accum_out=hh[:])
            neg_den = small.tile([P, 1], F32, tag="neg_den", name="neg_den")
            nc.gpsimd.tensor_scalar(out=neg_den[:], in0=hh[:], scalar1=-1.0, scalar2=-EPS, op0=ALU.mult, op1=ALU.add)
            neg_dens[ng, t] = neg_den

        def turn_g(ng, t, first_bank):
            for dg in range(GROUPS):
                acc = bank(first_bank + dg)
                for j in range(PACK):
                    nc.tensor.transpose(acc[:, j * P : (j + 1) * P], g_cols[ng, dg, j][:, t * P : (t + 1) * P], ident[:])
                g_rows[ng, t, dg] = acc

        def scale_add(ng, out, value, factor, term):
            if ng == 0:
                nc.gpsimd.tensor_scalar(
                    out=out[:], in0=value[:], scalar1=factor[:], scalar2=term[:], op0=ALU.mult, op1=ALU.add
                )
            else:
                nc.scalar.activation(out=out[:], in_=value[:], func=ACT.Identity, scale=factor[:], bias=term[:])

        def dot_gh(ng, t):
            neg_inv = small.tile([P, 1], F32, tag="neg_inv", name="neg_inv")
            part = small.tile([P, 1], F32, tag="part", name="part")
            sums = []
            for dg in range(GROUPS):
                products = work.tile([P, GROUP], BF16, tag="products", name="products", bufs=2)
                gh = small.tile([P, 1], F32, tag="gh%d" % dg, name="gh")
                nc.vector.scalar_tensor_tensor(
                    out=split(products[:]), in0=in_order(g_rows[ng, t, dg]), scalar=1.0,
                    in1=split(h_rows[ng, t][:, dg * GROUP : (dg + 1) * GROUP]),
                    op0=ALU.mult, op1=ALU.mult, accum_out=gh[:],
                )
                sums.append(gh)
                if dg == 0:
                    nc.vector.reciprocal(out=neg_inv[:], in_=neg_dens[ng, t][:])
            scale_add(ng, part, sums[0], neg_inv, neg_half)
            coef_parts[ng, t] = (neg_inv, part, sums[1])

        def make_coef(ng, t):
            neg_inv, part, gh = coef_parts[ng, t]
            coefs[ng, t] = small.tile([P, 1], F32, tag="coef", name="coef")
            scale_add(ng, coefs[ng, t], gh, neg_inv, part)

        def project_half(ng, t, dg):
            if ng not in result:
                result[ng] = work.tile([P, PACK, D], F32, tag="result", name="result")
            rows = out_0[ng * GROUP : (ng + 1) * GROUP, :].rearrange("(p t) d -> p t d", t=PACK)
            cols = slice(dg * GROUP, (dg + 1) * GROUP)
            nc.vector.scalar_tensor_tensor(
                out=split(result[ng][:, t, cols]), in0=split(h_rows[ng, t][:, cols]), scalar=coefs[ng, t][:],
                in1=in_order(g_rows[ng, t, dg]), op0=ALU.mult, op1=ALU.add,
            )
            nc.sync.dma_start(out=rows[:, t, cols], in_=result[ng][:, t, cols])

        def project(ng, t):
            for dg in range(GROUPS):
                project_half(ng, t, dg)

        def round_out(ng, dg, copy, first, width):
            stage = new_stage(("out", ng, dg)) if first == 0 else staged["out", ng, dg]
            col = dg * GROUP + first
            copy(
                out=pairs_out(stage[:, PACK * first : PACK * (first + width)]),
                in_=pairs_in(result[ng][:, :, col : col + width]),
            )

        def quantize_out(ng, dg):
            if dg == 0:
                new_codes = mx.tile([P, D], U32, tag="out_codes", name="out_codes", align_bytes=64)
                new_scales = mx.tile([P, D], U8, tag="out_scales", name="out_scales", align_bytes=64)
                out_planes[ng] = (new_codes, new_scales)
            codes, scales = out_planes[ng]
            words = out_1[ng].rearrange("p m t -> p (m t)").bitcast(I32)
            cols = slice(dg * GROUP, (dg + 1) * GROUP)
            nc.vector.quantize_mx(out=codes[:, cols].bitcast(FP8X4), scales=scales[:, cols], in_=staged["out", ng, dg][:])
            nc.sync.dma_start(out=words[:, cols], in_=codes[:, cols].bitcast(I32))

        def store_scales(ng, queues):
            scales = out_planes[ng][1]
            for quad in range(4):
                queues[quad % len(queues)].dma_start(
                    out=out_2[ng, 4 * quad : 4 * quad + 4, :].bitcast(I32),
                    in_=scales[32 * quad : 32 * quad + 4, :].bitcast(I32),
                )

        on_scalar, on_vector = nc.scalar.copy, nc.vector.tensor_copy
        every_slot = slice(0, PACK)


        sort_w(0, 0, on_scalar, every_slot)
        turn("x", x_rows, (0, 0), 4)
        turn("x", x_rows, (0, 1), 6)
        scale_x(0, 0)
        sort_w(1, 0, on_scalar, slice(0, PACK - 1))
        spread_z(4)
        quantize("x", 0, 0)
        scale_x(0, 1)
        quantize("w", 0, 0)
        sort_w(1, 0, on_vector, slice(PACK - 1, PACK))
        quantize("x", 0, 1)
        quantize("w", 1, 0)
        load_x(1, 1)
        load_y(0, 1)

        turn_y(0, 0)
        score_mm(0, 0, 0)
        score_mm(0, 0, 1)
        turn_y(0, 1)
        load_y(1, 0)
        for dg in range(GROUPS):
            sort_w(dg, 1, on_vector, every_slot)
        activate(0, 0, 0)
        score_mm(0, 0, 2)
        turn("x", x_rows, (1, 0), 4)
        load_y(1, 1)
        nc.sync.dma_start(out=gamma_all[:], in_=gamma.partition_broadcast(P))
        residuals(0, 0)
        activate(0, 0, 1)
        score_mm(0, 0, 3)
        turn("x", x_rows, (1, 1), 6)
        for dg in range(GROUPS):
            quantize("w", dg, 1)
        residuals(0, 1)
        activate(0, 0, 2)
        score_mm(0, 1, 0)
        turn_y(1, 0)
        scale_x(1, 0)
        residuals(0, 2)
        quantize("x", 1, 0)
        activate(0, 0, 3)
        score_mm(0, 1, 1)
        turn("w", w_rows, (0, 0), 4)
        scale_x(1, 1)
        residuals(0, 3)
        quantize("x", 1, 1)

        activate(0, 1, 0)
        score_mm(0, 1, 2)
        turn_y(1, 1)
        turn("w", w_rows, (1, 0), 6)
        stage_r1(0)
        activate(0, 1, 1)
        score_mm(0, 1, 3)
        copy_wt(0, 0)
        turn("w", w_rows, (0, 1), 4)
        stage_r2(0, 0)
        activate(0, 1, 2)
        score_mm(1, 0, 0)
        copy_wt(0, 1)
        turn("w", w_rows, (1, 1), 6)
        quantize("r1", 0, 0)
        residuals(1, 0)
        quantize("r2", 0, 0)
        residuals(1, 1)
        activate(0, 1, 3)
        score_mm(1, 0, 1)
        quantize("wt", 0, 0)
        residuals(1, 2)
        quantize("wt", 0, 1)
        copy_wt(1, 0)
        for dg in range(GROUPS):
            open_h(0, 0, dg, 4)

        activate(1, 0, 0)
        score_mm(1, 0, 2)
        residuals(1, 3)
        copy_wt(1, 1)
        for j, which_bank in enumerate((6, 7, 2, 3)):
            open_g(0, 0, j, which_bank)
        stage_r1(1)
        activate(1, 0, 1)
        score_mm(1, 0, 3)
        quantize("wt", 1, 0)
        stage_r2(0, 1)
        activate(1, 0, 2)
        quantize("r1", 0, 1)
        close_g(0, 0, 0)
        close_g(0, 0, 1)
        quantize("wt", 1, 1)
        quantize("r2", 0, 1)
        for dg in range(GROUPS):
            close_h(0, 0, dg)
        close_g(0, 0, 2)
        close_g(0, 0, 3)
        activate(1, 0, 3)
        linear(1, 0, 0)
        scale_h(0, 0)
        h_mm(0, 1, 4)
        scale_g(0, 0, 0)
        finish_slope()
        for j in range(1, PACK):
            scale_g(0, 0, j)
        linear(1, 0, 1)
        scale_h(0, 1)
        h_mm(0, 2, 4)
        make_g(0, 1, 0, 0)
        make_g(0, 1, 1, 1)
        linear(1, 0, 2)
        scale_h(0, 2)
        h_mm(0, 3, 4)
        make_g(0, 1, 2, 6)
        make_g(0, 1, 3, 7)
        norm_h(0, 0)
        linear(1, 0, 3)
        scale_h(0, 3)

        score_mm(1, 1, 0)
        turn_g(0, 0, 4)
        score_mm(1, 1, 1)
        turn_g(0, 1, 6)
        sum_r1(0, 0, 2)
        sum_r1(0, 1, 3)
        norm_h(0, 1)
        activate(1, 1, 0)
        score_mm(1, 1, 2)
        stage_r2(1, 0)
        dot_gh(0, 0)
        quantize("r2", 1, 0)
        make_coef(0, 0)
        dot_gh(0, 1)
        stage_r1_sum(0, 0)
        sum_r1(0, 2, 2)
        make_coef(0, 1)
        stage_r1_sum(0, 1)
        norm_h(0, 2)
        activate(1, 1, 1)
        score_mm(1, 1, 3)
        project(0, 0)
        turn_g(0, 2, 4)
        sum_r1(0, 3, 3)
        project(0, 1)
        turn_g(0, 3, 6)
        stage_r1_sum(0, 2)
        open_r1(1, 0, 2)
        dot_gh(0, 2)
        stage_r1_sum(0, 3)
        open_r1(1, 1, 3)
        norm_h(0, 3)
        activate(1, 1, 2)
        activate(1, 1, 3)
        close_r1(1, 0)
        close_r1(1, 1)
        sum_r1(1, 2, 0)
        sum_r1(1, 3, 1)
        finish_slope()
        make_coef(0, 2)
        dot_gh(0, 3)
        project(0, 2)
        make_coef(0, 3)
        quantize("r1", 1, 0)
        project(0, 3)
        for dg in range(GROUPS):
            round_out(0, dg, on_scalar, 0, GROUP)

        for t in range(2):
            for dg in range(GROUPS):
                open_h(1, t, dg, 4 + 2 * t)
        for tn in range(PACK):
            if tn < PACK - 1:
                linear(1, 1, tn)
            stage_r1_sum(1, tn)
            open_g(1, 0, (tn + 2) % PACK, (tn + 2) % PACK)
        linear(1, 1, PACK - 1)
        quantize("r1", 1, 1)
        for j in range(PACK):
            close_g(1, 0, j)
            scale_g(1, 0, j)
        for j in range(PACK):
            make_g(1, 1, j, j)
        stage_r2(1, 1)
        quantize_out(0, 0)
        quantize("r2", 1, 1)
        for t in range(2):
            for dg in range(GROUPS):
                close_h(1, t, dg)
        quantize_out(0, 1)
        store_scales(0, [nc.sync])
        for t in range(PACK):
            scale_h(1, t)
            norm_h(1, t)
            if t + 2 < PACK:
                h_mm(1, t + 2, 4 + 2 * t)

        for t in range(PACK):
            turn_g(1, t, 2 * t)
        for t in range(PACK):
            dot_gh(1, t)
            make_coef(1, t)
        for t in range(PACK):
            project_half(1, t, 0)
        round_out(1, 0, on_scalar, 0, GROUP)
        for t in range(PACK):
            project_half(1, t, 1)
        round_out(1, 1, on_vector, 0, GROUP // 2)
        round_out(1, 1, on_scalar, GROUP // 2, GROUP // 2)
        for dg in range(GROUPS):
            quantize_out(1, dg)
        store_scales(1, [nc.scalar, nc.sync])
